import numpy as np
import ml_dtypes


def mxq(x, axis, fmt="e4m3"):
    dtype, down = {"e4m3": (ml_dtypes.float8_e4m3fn, 7), "e5m2": (ml_dtypes.float8_e5m2, 14)}[fmt]
    v = np.moveaxis(np.asarray(x, np.float32).astype(ml_dtypes.bfloat16).astype(np.float64), axis, -1)
    blocks = v.reshape(v.shape[:-1] + (-1, 32))
    amax = np.abs(blocks).max(-1, keepdims=True)
    byte = np.maximum(np.where(amax > 0, np.frexp(amax)[1] - 1 + 127, 0) - down, 1)
    scale = np.exp2(byte - 127.0)
    codes = (blocks / scale).astype(np.float32).astype(dtype).astype(np.float64)
    return np.moveaxis((codes * scale).reshape(v.shape), -1, axis)


WIDE = False


def mx_kscale(k):
    if not WIDE:
        return np.ones(k)
    levels = np.array([10, -10, 5, -5, 0])
    if k % 512:
        return np.exp2(np.random.permutation(np.resize(levels, k // 32))).repeat(32)
    a = np.empty((k // 512, 16))
    for p in range(k // 512):
        a[p, :8] = np.random.permutation(np.resize(levels, 8))
        for g in range(8):
            far = levels[np.abs(levels - a[p, g]) >= 10]
            a[p, g + 8] = far[np.random.randint(len(far))]
    return np.exp2(a.ravel()).repeat(32)


def f64(x):
    return np.asarray(x).astype(np.float64)


def striped(idx):
    return np.tile(idx.reshape(-1, 16).T, (8, 1)).astype(np.uint16)


def unstriped(offs):
    return offs[:16].T.reshape(-1).astype(np.int64)


E2M1 = np.array([0.0, 0.5, 1.0, 1.5, 2.0, 3.0, 4.0, 6.0, -0.0, -0.5, -1.0, -1.5, -2.0, -3.0, -4.0, -6.0])


def pack_weight(w, fmt):
    k, n = w.shape
    w = f64(np.asarray(w, np.float32).astype(ml_dtypes.bfloat16)).reshape(k // 32, 32, n)
    amax = np.abs(w).max(1)
    if fmt == "e4m3":
        byte = np.frexp(amax)[1] - 1 + 127 - 7
    else:
        mant, ex = np.frexp(amax / 6.0)
        byte = np.where(mant > 0.5, ex, ex - 1) + 127
    byte = np.clip(np.where(amax > 0, byte, 1), 1, 254)
    scaled = (w * np.exp2(127.0 - byte)[:, None, :]).reshape(k, n).astype(np.float32)
    by_word = np.ascontiguousarray(scaled.reshape(k // 512, 128, 4, n).transpose(0, 1, 3, 2))
    if fmt == "e4m3":
        words = by_word.astype(ml_dtypes.float8_e4m3fn).view(np.uint8)
    else:
        c = by_word.astype(ml_dtypes.float4_e2m1fn).view(np.uint8) & 0xF
        words = (c[..., 0::2] | (c[..., 1::2] << 4)).reshape(k // 512, 128, 2 * n)
    return np.ascontiguousarray(words), np.ascontiguousarray(byte.astype(np.uint8).reshape(k // 512, 16, n))


def unpack_weight(words, scales, fmt):
    g, _, n = scales.shape
    words = np.ascontiguousarray(words).reshape(g, 128, n, -1)
    if fmt == "e4m3":
        vals = words.view(ml_dtypes.float8_e4m3fn).astype(np.float64)
    else:
        nib = np.empty((g, 128, n, 4), np.uint8)
        nib[..., 0::2] = words & 0xF
        nib[..., 1::2] = words >> 4
        vals = E2M1[nib]
    vals = vals * np.repeat(np.exp2(scales.astype(np.float64) - 127.0), 8, axis=1)[..., None]
    return vals.transpose(0, 1, 3, 2).reshape(g * 512, n)


def gelu(v):
    return 0.5 * v * (1.0 + np.tanh(np.sqrt(2.0 / np.pi) * (v + 0.044715 * v**3)))


def bf(x):
    return np.asarray(x, np.float32).astype(ml_dtypes.bfloat16)

def planes(Y):
    n, m = Y.shape
    b = f64(bf(Y)).reshape(n // 32, 32, m)
    amax = np.abs(b).max(1)
    byte = np.clip(np.where(amax > 0, np.frexp(amax)[1] - 1 + 127 - 7, 1), 1, 254)
    codes = (b * np.exp2(127.0 - byte)[:, None, :]).reshape(n, m).astype(np.float32).astype(ml_dtypes.float8_e4m3fn).view(np.uint8)
    words = codes.reshape(n // 512, 128, 4, m).transpose(0, 1, 3, 2)
    return np.ascontiguousarray(words), np.ascontiguousarray(byte.astype(np.uint8).reshape(n // 512, 16, m))


K, T, S, P, H, N = 1024, 4096, 1024, 512, 1024, 1024

def setup_inputs():
    n = np.random.standard_normal
    s = mx_kscale(K)[:, None]
    u = mx_kscale(H)[:, None]
    bits = np.where(n((K, T)) > 0, 1.0, -1.0)
    v = bits * np.exp(0.3 * n((K, 1))) * np.exp(0.3 * n((1, T))) * s
    tab_words, tab_scales = pack_weight(v, "e4m3")
    w1 = 0.8 * n((K, H)) / np.sqrt(K) / s
    w4 = 1.5 * n((H, N)) / np.sqrt(H) * np.exp(0.8 * n(N)) / u
    w4_words, w4_scales = pack_weight(w4, "e2m1")
    g = np.exp(0.3 * n(H)) * u[:, 0]
    return {"tab_words": tab_words, "tab_scales": tab_scales,
            "offs": striped(np.random.permutation(T)[:S]),
            "w1": w1.astype(np.float32),
            "pos1": striped(np.random.permutation(S)[:P]),
            "pos2": striped(np.random.permutation(S)[:P]),
            "g": g.astype(np.float32),
            "w4_words": w4_words, "w4_scales": w4_scales}

def reference(tab_words, tab_scales, offs, w1, pos1, pos2, g, w4_words, w4_scales):
    v = unpack_weight(tab_words, tab_scales, "e4m3")[:, unstriped(offs)]
    h = 1.0 / (1.0 + np.exp(-(mxq(f64(w1), 0, "e4m3").T @ v)))
    a = h[:, unstriped(pos1)]
    b = h[:, unstriped(pos2)]
    z = np.minimum(a, b) / np.maximum(a, b) * f64(g)[:, None]
    w4 = unpack_weight(w4_words, w4_scales, "e2m1")
    y = w4.T @ mxq(z, 0, "e4m3")
    words, scales = planes(y)
    return y, words, scales

@@ -1,0 +1,237 @@
+from contextlib import ExitStack
+
+import concourse.mybir as mybir
+
+K, T, S, PAIRS, H, N = 1024, 4096, 1024, 512, 1024, 1024
+FLOPS = 2 * K * H * S + 2 * H * N * PAIRS
+
+F32 = mybir.dt.float32
+BF16 = mybir.dt.bfloat16
+I32 = mybir.dt.int32
+U32 = mybir.dt.uint32
+U16 = mybir.dt.uint16
+U8 = mybir.dt.uint8
+E4M3 = mybir.dt.float8_e4m3fn_x4
+E2M1 = mybir.dt.float4_e2m1fn_x4
+ACT = mybir.ActivationFunctionType
+ALU = mybir.AluOpType
+
+P = 128
+PACK = 4
+SPAN = P * PACK
+BANK = 512
+CHUNK = 128
+
+
+def tile_list_malware_pair_family_kernel(tc, tab_words, tab_scales, offs, w1, pos1, pos2, g, w4_words, w4_scales, out_0, out_1, out_2):
+    nc = tc.nc
+    with ExitStack() as ctx:
+        keep = ctx.enter_context(tc.tile_pool(name="keep", bufs=1))
+        ring = ctx.enter_context(tc.tile_pool(name="ring", bufs=2))
+        psum = ctx.enter_context(tc.psum_pool(name="psum", bufs=1))
+
+        def kept(shape, dtype, name, tag=None):
+            return keep.tile(shape, dtype, name=name, tag=tag or name, align_bytes=64)
+
+        def bank(index, shape, name):
+            return psum.tile(shape, F32, name=name, tag="bank%d" % index)
+
+        offs_sb = keep.tile([P, S // 16], U16, name="offs_sb")
+        pos1_sb = keep.tile([P, PAIRS // 16], U16, name="pos1_sb")
+        pos2_sb = keep.tile([P, PAIRS // 16], U16, name="pos2_sb")
+
+        w4_planes = kept([P, 2 * N], U8, "w4_planes")
+        nc.vector.memset(w4_planes[:].bitcast(I32), 0)
+        tab_planes = kept([P, T], U8, "tab_planes")
+        nc.vector.memset(tab_planes[:].bitcast(I32), 0)
+        warm = kept([P, 1], F32, "warm")
+        nc.vector.memset(warm[:], 0.0)
+        nc.scalar.activation(warm[:], warm[:], ACT.Sigmoid)
+
+        nc.sync.dma_start(offs_sb[:], offs)
+        w4_raw = kept([P, 2, 2 * N], U8, "w4_raw")
+        nc.sync.dma_start(w4_raw[:].bitcast(I32), w4_words.rearrange("a p c -> p a c").bitcast(I32))
+        for q in range(4):
+            nc.sync.dma_start(
+                w4_planes[32 * q : 32 * q + 4, :].rearrange("r (a c) -> r a c", a=2).bitcast(I32),
+                w4_scales[:, 4 * q : 4 * q + 4, :].rearrange("a r c -> r a c").bitcast(I32),
+            )
+        table = [kept([P, T], I32, "table%d" % a) for a in range(2)]
+        words = [tab_words[a].rearrange("p t i -> p (t i)").bitcast(I32) for a in range(2)]
+        nc.sync.dma_start(table[0][:], words[0])
+        for q in range(4):
+            nc.sync.dma_start(tab_planes[32 * q : 32 * q + 8, :].bitcast(I32), tab_scales[:, 4 * q : 4 * q + 4, :].bitcast(I32))
+        nc.sync.dma_start(table[1][:], words[1])
+
+        def load_w1(b, a, half):
+            raw = kept([P, PACK, SPAN // 2], F32, "w1_raw%d%d%d" % (b, a, half))
+            c0 = SPAN * b + half * (SPAN // 2)
+            nc.sync.dma_start(raw[:], w1[SPAN * a : SPAN * (a + 1), c0 : c0 + SPAN // 2].rearrange("(p j) c -> p j c", j=PACK))
+            return raw
+
+        raw_a = {(a, half): load_w1(0, a, half) for a in range(2) for half in range(2)}
+        nc.sync.dma_start(pos1_sb[:], pos1)
+        nc.sync.dma_start(pos2_sb[:], pos2)
+        raw_b = {(a, half): load_w1(1, a, half) for a in range(2) for half in range(2)}
+        gain = kept([P, 2, PACK], F32, "gain")
+        nc.sync.dma_start(gain[:], g.rearrange("(b p t) -> p b t", b=2, t=PACK))
+
+        w4_codes = kept([P, 2, 2 * N], U8, "w4_codes")
+        w4_dealt = kept([P, 2 * N], U8, "w4_dealt")
+        nc.vector.tensor_copy(
+            w4_codes[:].rearrange("p a c -> p (a c)").bitcast(U16).rearrange("p (x t c i) -> p x c t i", x=4, t=PACK, i=8),
+            w4_raw[:].rearrange("p a c -> p (a c)").bitcast(U16).rearrange("p (x c i t) -> p x c t i", x=4, t=PACK, i=8),
+        )
+        nc.vector.tensor_copy(
+            w4_dealt[:].rearrange("p (x t c i) -> p x c t i", x=4, t=PACK, i=16),
+            w4_planes[:].rearrange("p (x c i t) -> p x c t i", x=4, t=PACK, i=16),
+        )
+
+        picked = [kept([P, S], U32, "picked%d" % a) for a in range(2)]
+        picked_planes = kept([P, S], U8, "picked_planes")
+        nc.vector.tensor_copy(picked[0][:], table[0][:].bitcast(U32).indirect(offs_sb[:]))
+        nc.vector.tensor_copy(picked_planes[:], tab_planes[:].indirect(offs_sb[:]))
+        nc.vector.tensor_copy(picked[1][:], table[1][:].bitcast(U32).indirect(offs_sb[:]))
+
+        def quantise_w1(b, raws, engines):
+            codes = kept([P, 2, SPAN], U32, "w1_codes%d" % b, tag="w1_codes_a" if b == 0 else "codes_then_inverse")
+            planes = kept([P, 2, SPAN], U8, "w1_planes%d" % b)
+            for a in range(2):
+                dealt = ring.tile([P, PACK, P, PACK], BF16, name="dealt", align_bytes=64)
+                for half in range(2):
+                    src = raws[(a, half)][:].rearrange("p j (m t) -> p m j t", t=PACK)
+                    dst = dealt[:, :, half * 64 : (half + 1) * 64, :].rearrange("p t m j -> p m j t")
+                    if engines[2 * a + half] == "scalar":
+                        nc.scalar.copy(dst, src)
+                    else:
+                        nc.vector.tensor_copy(dst, src)
+                nc.vector.quantize_mx(out=codes[:, a, :].bitcast(E4M3), scales=planes[:, a, :], in_=dealt[:].rearrange("p t m j -> p (t m j)"))
+            return codes, planes
+
+        def first_pass(acc, codes, planes, t, half, a):
+            cols = slice(half * BANK, (half + 1) * BANK)
+            nc.tensor.matmul_mx(
+                out=acc[:],
+                lhsT=codes[:, a, t * P : (t + 1) * P].bitcast(E4M3),
+                lhsT_scale=planes[:, a, t * P : (t + 1) * P],
+                rhs=picked[a][:, cols].bitcast(E4M3),
+                rhs_scale=picked_planes[4 * a : P, cols],
+                start=(a == 0),
+                stop=(a == 1),
+            )
+
+        h = {(b, t): kept([P, S], F32, "h%d%d" % (b, t)) for b in range(2) for t in range(PACK)}
+
+        codes, planes = quantise_w1(0, raw_a, ("scalar", "scalar", "scalar", "vector"))
+        accs = {(t, half): bank(2 * t + half, [P, BANK], "acc_a") for t in range(PACK) for half in range(2)}
+        for a in range(2):
+            for t in range(PACK):
+                for half in range(2):
+                    first_pass(accs[(t, half)], codes, planes, t, half, a)
+                    if a == 1:
+                        nc.scalar.activation(h[(0, t)][:, half * BANK : (half + 1) * BANK], accs[(t, half)][:], ACT.Sigmoid)
+
+        inv_gain = kept([P, 2, PACK], F32, "inv_gain")
+        nc.vector.reciprocal(inv_gain[:], gain[:])
+
+        codes, planes = quantise_w1(1, raw_b, ("scalar",) * 4)
+        for t in range(PACK):
+            for half in range(2):
+                acc = bank(2 * t + half, [P, BANK], "acc_b")
+                for a in range(2):
+                    first_pass(acc, codes, planes, t, half, a)
+                nc.scalar.activation(h[(1, t)][:, half * BANK : (half + 1) * BANK], acc[:], ACT.Sigmoid)
+
+        inverse = kept([P, 2 * PACK * PAIRS], F32, "inverse", tag="codes_then_inverse")
+        z_codes = kept([P, 2, PAIRS], U32, "z_codes")
+        z_planes = kept([P, 2, PAIRS], U8, "z_planes")
+
+        def pick(b, j0, width):
+            pool = keep if b == 0 else ring
+            larger = pool.tile([P, PACK, width], F32, name="larger%d" % b)
+            smaller = pool.tile([P, PACK, width], F32, name="smaller%d" % b)
+            cols = slice(j0 // 16, (j0 + width) // 16)
+            together = PAIRS // width
+            for t0 in range(0, PACK, together):
+                second = ring.tile([P, together, width], F32, name="second")
+                for u in range(together):
+                    nc.vector.tensor_copy(smaller[:, t0 + u, :], h[(b, t0 + u)][:].indirect(pos1_sb[:, cols]))
+                    nc.vector.tensor_copy(second[:, u, :], h[(b, t0 + u)][:].indirect(pos2_sb[:, cols]))
+                first = smaller[:, t0 : t0 + together, :]
+                nc.vector.tensor_tensor(larger[:, t0 : t0 + together, :], first, second[:], ALU.max)
+                nc.vector.tensor_tensor(first, first, second[:], ALU.min)
+            return larger, smaller
+
+        def invert(b, j0, width, larger):
+            base = PACK * (b * PAIRS + j0)
+            part = inverse[:, base : base + PACK * width]
+            for t in range(PACK):
+                nc.scalar.activation(part[:, t * width : (t + 1) * width], larger[:, t, :], ACT.Abs_reciprocal_sqrt, scale=inv_gain[:, b, t : t + 1])
+            nc.scalar.activation(part, part, ACT.Square)
+            return part
+
+        def agree(b, j0, width, smaller, part):
+            z = ring.tile([P, width, PACK], BF16, name="z", tag="z%d" % b, align_bytes=64)
+            nc.vector.tensor_tensor(
+                z[:].rearrange("p (c i) t -> p c t i", i=4),
+                smaller[:].rearrange("p t (c i) -> p c t i", i=4),
+                part.rearrange("p (t c i) -> p c t i", t=PACK, i=4),
+                ALU.mult,
+            )
+            nc.vector.quantize_mx(out=z_codes[:, b, j0 : j0 + width].bitcast(E4M3), scales=z_planes[:, b, j0 : j0 + width], in_=z[:].rearrange("p j t -> p (j t)"))
+
+        def second_pass(acc, a, grp, j0):
+            for t in range(PACK):
+                c0 = SPAN * grp + P * t
+                nc.tensor.matmul_mx(
+                    out=acc[:, t, :],
+                    lhsT=w4_codes[:, a, 2 * c0 : 2 * (c0 + P)].bitcast(E2M1),
+                    lhsT_scale=w4_dealt[:, a * N + c0 : a * N + c0 + P],
+                    rhs=z_codes[:, a, j0 : j0 + CHUNK].bitcast(E4M3),
+                    rhs_scale=z_planes[:, a, j0 : j0 + CHUNK],
+                    start=(a == 0 and t == 0),
+                    stop=(a == 1 and t == PACK - 1),
+                )
+
+        y_planes = kept([P, 2, PAIRS], U8, "y_planes")
+
+        def hand_out(j0, accs, shared):
+            y_codes = ring.tile([P, 2, CHUNK], I32, name="y_codes", align_bytes=64)
+            for step in range(2):
+                y = ring.tile([P, PACK, CHUNK], F32, name="y", tag="y%d" % step)
+                nc.scalar.copy(y[:], accs[step][:])
+                nc.sync.dma_start(out_0[SPAN * step : SPAN * (step + 1), j0 : j0 + CHUNK].rearrange("(p t) j -> p t j", t=PACK), y[:])
+                grp = 1 - step if shared else step
+                rounded = ring.tile([P, CHUNK, PACK], BF16, name="rounded", tag="rounded%d" % grp, align_bytes=64)
+                dst = rounded[:].rearrange("p (c i) t -> p c t i", i=4)
+                src = accs[grp][:].rearrange("p t (c i) -> p c t i", i=4)
+                if shared:
+                    nc.vector.tensor_copy(dst, src)
+                else:
+                    nc.scalar.copy(dst, src)
+                nc.vector.quantize_mx(out=y_codes[:, grp, :].bitcast(E4M3), scales=y_planes[:, grp, j0 : j0 + CHUNK], in_=rounded[:].rearrange("p j t -> p (j t)"))
+            nc.sync.dma_start(out_1[:, :, j0 : j0 + CHUNK, :].rearrange("g p m i -> p g (m i)").bitcast(I32), y_codes[:])
+
+        starts = list(range(0, PAIRS, CHUNK))
+        larger_a, smaller_a = pick(0, 0, PAIRS)
+        part_a = invert(0, 0, PAIRS, larger_a)
+        picks = {starts[0]: pick(1, starts[0], CHUNK)}
+        parts = {starts[0]: invert(1, starts[0], CHUNK, picks[starts[0]][0])}
+        picks[starts[1]] = pick(1, starts[1], CHUNK)
+        parts[starts[1]] = invert(1, starts[1], CHUNK, picks[starts[1]][0])
+        agree(0, 0, PAIRS, smaller_a, part_a)
+        sums = {j0: [bank(2 * n + grp, [P, PACK, CHUNK], "sums") for grp in range(2)] for n, j0 in enumerate(starts)}
+        for j0 in starts:
+            for grp in range(2):
+                second_pass(sums[j0][grp], 0, grp, j0)
+        for n, j0 in enumerate(starts):
+            agree(1, j0, CHUNK, picks[j0][1], parts[j0])
+            for grp in range(2):
+                second_pass(sums[j0][grp], 1, grp, j0)
+            hand_out(j0, sums[j0], n >= 2)
+            if n + 2 < len(starts):
+                ahead = starts[n + 2]
+                picks[ahead] = pick(1, ahead, CHUNK)
+                parts[ahead] = invert(1, ahead, CHUNK, picks[ahead][0])
+        for q in range(4):
+            nc.sync.dma_start(out_2[:, 4 * q : 4 * q + 4, :].rearrange("g r m -> r g m").bitcast(I32), y_planes[32 * q : 32 * q + 4, :, :].bitcast(I32))

@@ -61,18 +61,20 @@ def tile_list_malware_pair_family_kernel(tc, tab_words, tab_scales, offs, w1, po
         nc.sync.dma_start(table[0][:], words[0])
         for q in range(4):
             nc.sync.dma_start(tab_planes[32 * q : 32 * q + 8, :].bitcast(I32), tab_scales[:, 4 * q : 4 * q + 4, :].bitcast(I32))
+
+        def load_w1(b, a, c0, width):
+            raw = kept([P, PACK, width], F32, "w1_raw%d%d_%d" % (b, a, c0))
+            cols = slice(SPAN * b + c0, SPAN * b + c0 + width)
+            nc.sync.dma_start(raw[:], w1[SPAN * a : SPAN * (a + 1), cols].rearrange("(p j) c -> p j c", j=PACK))
+            return raw, c0, width
+
+        raw = {(0, 0): [load_w1(0, 0, 0, SPAN)]}
         nc.sync.dma_start(table[1][:], words[1])
-
-        def load_w1(b, a, half):
-            raw = kept([P, PACK, SPAN // 2], F32, "w1_raw%d%d%d" % (b, a, half))
-            c0 = SPAN * b + half * (SPAN // 2)
-            nc.sync.dma_start(raw[:], w1[SPAN * a : SPAN * (a + 1), c0 : c0 + SPAN // 2].rearrange("(p j) c -> p j c", j=PACK))
-            return raw
-
-        raw_a = {(a, half): load_w1(0, a, half) for a in range(2) for half in range(2)}
+        raw[(0, 1)] = [load_w1(0, 1, c0, SPAN // 2) for c0 in (0, SPAN // 2)]
         nc.sync.dma_start(pos1_sb[:], pos1)
         nc.sync.dma_start(pos2_sb[:], pos2)
-        raw_b = {(a, half): load_w1(1, a, half) for a in range(2) for half in range(2)}
+        for a in range(2):
+            raw[(1, a)] = [load_w1(1, a, 0, SPAN)]
         gain = kept([P, 2, PACK], F32, "gain")
         nc.sync.dma_start(gain[:], g.rearrange("(b p t) -> p b t", b=2, t=PACK))
 
@@ -91,29 +93,39 @@ def tile_list_malware_pair_family_kernel(tc, tab_words, tab_scales, offs, w1, po
         picked_planes = kept([P, S], U8, "picked_planes")
         nc.vector.tensor_copy(picked[0][:], table[0][:].bitcast(U32).indirect(offs_sb[:]))
         nc.vector.tensor_copy(picked_planes[:], tab_planes[:].indirect(offs_sb[:]))
-        nc.vector.tensor_copy(picked[1][:], table[1][:].bitcast(U32).indirect(offs_sb[:]))
 
-        def quantise_w1(b, raws, engines):
-            codes = kept([P, 2, SPAN], U32, "w1_codes%d" % b, tag="w1_codes_a" if b == 0 else "codes_then_inverse")
-            planes = kept([P, 2, SPAN], U8, "w1_planes%d" % b)
-            for a in range(2):
-                dealt = ring.tile([P, PACK, P, PACK], BF16, name="dealt", align_bytes=64)
-                for half in range(2):
-                    src = raws[(a, half)][:].rearrange("p j (m t) -> p m j t", t=PACK)
-                    dst = dealt[:, :, half * 64 : (half + 1) * 64, :].rearrange("p t m j -> p m j t")
-                    if engines[2 * a + half] == "scalar":
-                        nc.scalar.copy(dst, src)
-                    else:
-                        nc.vector.tensor_copy(dst, src)
-                nc.vector.quantize_mx(out=codes[:, a, :].bitcast(E4M3), scales=planes[:, a, :], in_=dealt[:].rearrange("p t m j -> p (t m j)"))
-            return codes, planes
+        w1_codes = {(0, t): kept([P, 2, P], U32, "w1_codes0%d" % t, tag="stage%d" % t) for t in range(PACK)}
+        second_codes = kept([P, 2, PACK, P], U32, "w1_codes1", tag="codes_then_inverse")
+        w1_planes = kept([P, 2, 2, PACK, P], U8, "w1_planes")
 
-        def first_pass(acc, codes, planes, t, half, a):
+        def codes_of(b, t, a):
+            return w1_codes[(0, t)][:, a, :] if b == 0 else second_codes[:, a, t, :]
+
+        def quantise_w1(b, a):
+            dealt = kept([P, PACK, P, PACK], BF16, "dealt", tag=("dealt%d" if b == 0 else "stage%d") % a)
+            for piece, c0, width in raw[(b, a)]:
+                src = piece[:].rearrange("p j (m t) -> p m j t", t=PACK)
+                dst = dealt[:, :, c0 // PACK : (c0 + width) // PACK, :].rearrange("p t m j -> p m j t")
+                if c0 == 0:
+                    nc.scalar.copy(dst, src)
+                else:
+                    nc.vector.tensor_copy(dst, src)
+            if b == 0:
+                for t in range(PACK):
+                    nc.vector.quantize_mx(out=codes_of(b, t, a).bitcast(E4M3), scales=w1_planes[:, b, a, t, :], in_=dealt[:, t, :, :].rearrange("p m j -> p (m j)"))
+            else:
+                nc.vector.quantize_mx(
+                    out=second_codes[:, a, :, :].rearrange("p t m -> p (t m)").bitcast(E4M3),
+                    scales=w1_planes[:, b, a, :, :].rearrange("p t m -> p (t m)"),
+                    in_=dealt[:].rearrange("p t m j -> p (t m j)"),
+                )
+
+        def first_pass(acc, b, t, half, a):
             cols = slice(half * BANK, (half + 1) * BANK)
             nc.tensor.matmul_mx(
                 out=acc[:],
-                lhsT=codes[:, a, t * P : (t + 1) * P].bitcast(E4M3),
-                lhsT_scale=planes[:, a, t * P : (t + 1) * P],
+                lhsT=codes_of(b, t, a).bitcast(E4M3),
+                lhsT_scale=w1_planes[:, b, a, t, :],
                 rhs=picked[a][:, cols].bitcast(E4M3),
                 rhs_scale=picked_planes[4 * a : P, cols],
                 start=(a == 0),
@@ -122,63 +134,67 @@ def tile_list_malware_pair_family_kernel(tc, tab_words, tab_scales, offs, w1, po
 
         h = {(b, t): kept([P, S], F32, "h%d%d" % (b, t)) for b in range(2) for t in range(PACK)}
 
-        codes, planes = quantise_w1(0, raw_a, ("scalar", "scalar", "scalar", "vector"))
         accs = {(t, half): bank(2 * t + half, [P, BANK], "acc_a") for t in range(PACK) for half in range(2)}
-        for a in range(2):
-            for t in range(PACK):
-                for half in range(2):
-                    first_pass(accs[(t, half)], codes, planes, t, half, a)
-                    if a == 1:
-                        nc.scalar.activation(h[(0, t)][:, half * BANK : (half + 1) * BANK], accs[(t, half)][:], ACT.Sigmoid)
+        quantise_w1(0, 0)
+        nc.vector.tensor_copy(picked[1][:], table[1][:].bitcast(U32).indirect(offs_sb[:]))
+        quantise_w1(0, 1)
+        for t in range(PACK):
+            for half in range(2):
+                for a in range(2):
+                    first_pass(accs[(t, half)], 0, t, half, a)
+        for t in range(PACK):
+            for half in range(2):
+                nc.scalar.activation(h[(0, t)][:, half * BANK : (half + 1) * BANK], accs[(t, half)][:], ACT.Sigmoid)
+            if t < 2:
+                quantise_w1(1, t)
 
         inv_gain = kept([P, 2, PACK], F32, "inv_gain")
         nc.vector.reciprocal(inv_gain[:], gain[:])
 
-        codes, planes = quantise_w1(1, raw_b, ("scalar",) * 4)
         for t in range(PACK):
             for half in range(2):
                 acc = bank(2 * t + half, [P, BANK], "acc_b")
                 for a in range(2):
-                    first_pass(acc, codes, planes, t, half, a)
+                    first_pass(acc, 1, t, half, a)
                 nc.scalar.activation(h[(1, t)][:, half * BANK : (half + 1) * BANK], acc[:], ACT.Sigmoid)
 
-        inverse = kept([P, 2 * PACK * PAIRS], F32, "inverse", tag="codes_then_inverse")
-        z_codes = kept([P, 2, PAIRS], U32, "z_codes")
+        z_codes = {(b, j0): kept([P, CHUNK], U32, "z_codes", tag="z_codes%d_%d" % (b, j0)) for b in range(2) for j0 in range(0, PAIRS, CHUNK)}
         z_planes = kept([P, 2, PAIRS], U8, "z_planes")
 
-        def pick(b, j0, width):
-            pool = keep if b == 0 else ring
-            larger = pool.tile([P, PACK, width], F32, name="larger%d" % b)
-            smaller = pool.tile([P, PACK, width], F32, name="smaller%d" % b)
+        def pick(b, j0, width, tags):
+            larger = kept([P, PACK, width], F32, "larger%d_%d" % (b, j0))
+            smaller = kept([P, PACK, width], F32, "smaller%d_%d" % (b, j0))
             cols = slice(j0 // 16, (j0 + width) // 16)
-            together = PAIRS // width
-            for t0 in range(0, PACK, together):
-                second = ring.tile([P, together, width], F32, name="second")
+            together = PACK // len(tags)
+            for n, tag in enumerate(tags):
+                pair = kept([P, 2, together, width], F32, "pair", tag=tag)
                 for u in range(together):
-                    nc.vector.tensor_copy(smaller[:, t0 + u, :], h[(b, t0 + u)][:].indirect(pos1_sb[:, cols]))
-                    nc.vector.tensor_copy(second[:, u, :], h[(b, t0 + u)][:].indirect(pos2_sb[:, cols]))
-                first = smaller[:, t0 : t0 + together, :]
-                nc.vector.tensor_tensor(larger[:, t0 : t0 + together, :], first, second[:], ALU.max)
-                nc.vector.tensor_tensor(first, first, second[:], ALU.min)
+                    window = h[(b, n * together + u)]
+                    nc.vector.tensor_copy(pair[:, 0, u, :], window[:].indirect(pos1_sb[:, cols]))
+                    nc.vector.tensor_copy(pair[:, 1, u, :], window[:].indirect(pos2_sb[:, cols]))
+                rows = slice(n * together, (n + 1) * together)
+                nc.vector.tensor_tensor(larger[:, rows, :], pair[:, 0, :, :], pair[:, 1, :, :], ALU.max)
+                nc.vector.tensor_tensor(smaller[:, rows, :], pair[:, 0, :, :], pair[:, 1, :, :], ALU.min)
             return larger, smaller
 
-        def invert(b, j0, width, larger):
-            base = PACK * (b * PAIRS + j0)
-            part = inverse[:, base : base + PACK * width]
-            for t in range(PACK):
-                nc.scalar.activation(part[:, t * width : (t + 1) * width], larger[:, t, :], ACT.Abs_reciprocal_sqrt, scale=inv_gain[:, b, t : t + 1])
-            nc.scalar.activation(part, part, ACT.Square)
+        def invert(b, width, larger, tag):
+            part = kept([P, PACK, width], F32, "inverse", tag=tag)
+            together = PAIRS // width
+            for t0 in range(0, PACK, together):
+                for t in range(t0, t0 + together):
+                    nc.scalar.activation(part[:, t, :], larger[:, t, :], ACT.Abs_reciprocal_sqrt, scale=inv_gain[:, b, t : t + 1])
+                nc.scalar.activation(part[:, t0 : t0 + together, :], part[:, t0 : t0 + together, :], ACT.Square)
             return part
 
-        def agree(b, j0, width, smaller, part):
-            z = ring.tile([P, width, PACK], BF16, name="z", tag="z%d" % b, align_bytes=64)
+        def agree(b, j0, smaller, part, tag):
+            z = kept([P, CHUNK, PACK], BF16, "z", tag=tag)
             nc.vector.tensor_tensor(
                 z[:].rearrange("p (c i) t -> p c t i", i=4),
-                smaller[:].rearrange("p t (c i) -> p c t i", i=4),
-                part.rearrange("p (t c i) -> p c t i", t=PACK, i=4),
+                smaller.rearrange("p t (c i) -> p c t i", i=4),
+                part.rearrange("p t (c i) -> p c t i", i=4),
                 ALU.mult,
             )
-            nc.vector.quantize_mx(out=z_codes[:, b, j0 : j0 + width].bitcast(E4M3), scales=z_planes[:, b, j0 : j0 + width], in_=z[:].rearrange("p j t -> p (j t)"))
+            nc.vector.quantize_mx(out=z_codes[(b, j0)][:].bitcast(E4M3), scales=z_planes[:, b, j0 : j0 + CHUNK], in_=z[:].rearrange("p j t -> p (j t)"))
 
         def second_pass(acc, a, grp, j0):
             for t in range(PACK):
@@ -187,7 +203,7 @@ def tile_list_malware_pair_family_kernel(tc, tab_words, tab_scales, offs, w1, po
                     out=acc[:, t, :],
                     lhsT=w4_codes[:, a, 2 * c0 : 2 * (c0 + P)].bitcast(E2M1),
                     lhsT_scale=w4_dealt[:, a * N + c0 : a * N + c0 + P],
-                    rhs=z_codes[:, a, j0 : j0 + CHUNK].bitcast(E4M3),
+                    rhs=z_codes[(a, j0)][:].bitcast(E4M3),
                     rhs_scale=z_planes[:, a, j0 : j0 + CHUNK],
                     start=(a == 0 and t == 0),
                     stop=(a == 1 and t == PACK - 1),
@@ -213,25 +229,23 @@ def tile_list_malware_pair_family_kernel(tc, tab_words, tab_scales, offs, w1, po
             nc.sync.dma_start(out_1[:, :, j0 : j0 + CHUNK, :].rearrange("g p m i -> p g (m i)").bitcast(I32), y_codes[:])
 
         starts = list(range(0, PAIRS, CHUNK))
-        larger_a, smaller_a = pick(0, 0, PAIRS)
-        part_a = invert(0, 0, PAIRS, larger_a)
-        picks = {starts[0]: pick(1, starts[0], CHUNK)}
-        parts = {starts[0]: invert(1, starts[0], CHUNK, picks[starts[0]][0])}
-        picks[starts[1]] = pick(1, starts[1], CHUNK)
-        parts[starts[1]] = invert(1, starts[1], CHUNK, picks[starts[1]][0])
-        agree(0, 0, PAIRS, smaller_a, part_a)
+        larger_a, smaller_a = pick(0, 0, PAIRS, ("pair", "stage1"))
+        part_a = invert(0, PAIRS, larger_a, "codes_then_inverse")
+        larger_b, smaller_b = pick(1, 0, 2 * CHUNK, ("pair",))
+        part_b = invert(1, 2 * CHUNK, larger_b, "larger0_0")
+        ready = {j0: (smaller_b[:, :, j0 : j0 + CHUNK], part_b[:, :, j0 : j0 + CHUNK]) for j0 in starts[:2]}
         sums = {j0: [bank(2 * n + grp, [P, PACK, CHUNK], "sums") for grp in range(2)] for n, j0 in enumerate(starts)}
-        for j0 in starts:
+        for n, j0 in enumerate(starts):
+            agree(0, j0, smaller_a[:, :, j0 : j0 + CHUNK], part_a[:, :, j0 : j0 + CHUNK], "chain%d" % n)
             for grp in range(2):
                 second_pass(sums[j0][grp], 0, grp, j0)
-        for n, j0 in enumerate(starts):
-            agree(1, j0, CHUNK, picks[j0][1], parts[j0])
+            agree(1, j0, ready[j0][0], ready[j0][1], "chain%d" % (n + 1))
             for grp in range(2):
                 second_pass(sums[j0][grp], 1, grp, j0)
             hand_out(j0, sums[j0], n >= 2)
             if n + 2 < len(starts):
                 ahead = starts[n + 2]
-                picks[ahead] = pick(1, ahead, CHUNK)
-                parts[ahead] = invert(1, ahead, CHUNK, picks[ahead][0])
+                larger, smaller = pick(1, ahead, CHUNK, ("chain%d" % (n + 1),))
+                ready[ahead] = (smaller[:], invert(1, CHUNK, larger, "z_codes1_%d" % j0)[:])
         for q in range(4):
             nc.sync.dma_start(out_2[:, 4 * q : 4 * q + 4, :].rearrange("g r m -> r g m").bitcast(I32), y_planes[32 * q : 32 * q + 4, :, :].bitcast(I32))

@@ -1,4 +1,5 @@
 from contextlib import ExitStack
+from itertools import product
 
 import concourse.mybir as mybir
 
@@ -40,27 +41,25 @@ def tile_list_malware_pair_family_kernel(tc, tab_words, tab_scales, offs, w1, po
         pos1_sb = keep.tile([P, PAIRS // 16], U16, name="pos1_sb")
         pos2_sb = keep.tile([P, PAIRS // 16], U16, name="pos2_sb")
 
-        w4_planes = kept([P, 2 * N], U8, "w4_planes")
-        nc.vector.memset(w4_planes[:].bitcast(I32), 0)
         tab_planes = kept([P, T], U8, "tab_planes")
         nc.vector.memset(tab_planes[:].bitcast(I32), 0)
+        w4_planes = kept([P, 2 * N], U8, "w4_planes")
+        nc.vector.memset(w4_planes[:].bitcast(I32), 0)
         warm = kept([P, 1], F32, "warm")
         nc.vector.memset(warm[:], 0.0)
         nc.scalar.activation(warm[:], warm[:], ACT.Sigmoid)
 
         nc.sync.dma_start(offs_sb[:], offs)
-        w4_raw = kept([P, 2, 2 * N], U8, "w4_raw")
-        nc.sync.dma_start(w4_raw[:].bitcast(I32), w4_words.rearrange("a p c -> p a c").bitcast(I32))
+        table = [kept([P, T], I32, "table%d" % a) for a in range(2)]
+        words = [tab_words[a].rearrange("p t i -> p (t i)").bitcast(I32) for a in range(2)]
+        nc.sync.dma_start(table[0][:], words[0])
+        for q in range(4):
+            nc.gpsimd.dma_start(tab_planes[32 * q : 32 * q + 8, :].bitcast(I32), tab_scales[:, 4 * q : 4 * q + 4, :].bitcast(I32))
         for q in range(4):
             nc.sync.dma_start(
                 w4_planes[32 * q : 32 * q + 4, :].rearrange("r (a c) -> r a c", a=2).bitcast(I32),
                 w4_scales[:, 4 * q : 4 * q + 4, :].rearrange("a r c -> r a c").bitcast(I32),
             )
-        table = [kept([P, T], I32, "table%d" % a) for a in range(2)]
-        words = [tab_words[a].rearrange("p t i -> p (t i)").bitcast(I32) for a in range(2)]
-        nc.sync.dma_start(table[0][:], words[0])
-        for q in range(4):
-            nc.sync.dma_start(tab_planes[32 * q : 32 * q + 8, :].bitcast(I32), tab_scales[:, 4 * q : 4 * q + 4, :].bitcast(I32))
 
         def load_w1(b, a, c0, width):
             raw = kept([P, PACK, width], F32, "w1_raw%d%d_%d" % (b, a, c0))
@@ -71,6 +70,8 @@ def tile_list_malware_pair_family_kernel(tc, tab_words, tab_scales, offs, w1, po
         raw = {(0, 0): [load_w1(0, 0, 0, SPAN)]}
         nc.sync.dma_start(table[1][:], words[1])
         raw[(0, 1)] = [load_w1(0, 1, c0, SPAN // 2) for c0 in (0, SPAN // 2)]
+        w4_raw = kept([P, 2, 2 * N], U8, "w4_raw")
+        nc.sync.dma_start(w4_raw[:].bitcast(I32), w4_words.rearrange("a p c -> p a c").bitcast(I32))
         nc.sync.dma_start(pos1_sb[:], pos1)
         nc.sync.dma_start(pos2_sb[:], pos2)
         for a in range(2):
@@ -78,18 +79,7 @@ def tile_list_malware_pair_family_kernel(tc, tab_words, tab_scales, offs, w1, po
         gain = kept([P, 2, PACK], F32, "gain")
         nc.sync.dma_start(gain[:], g.rearrange("(b p t) -> p b t", b=2, t=PACK))
 
-        w4_codes = kept([P, 2, 2 * N], U8, "w4_codes")
-        w4_dealt = kept([P, 2 * N], U8, "w4_dealt")
-        nc.vector.tensor_copy(
-            w4_codes[:].rearrange("p a c -> p (a c)").bitcast(U16).rearrange("p (x t c i) -> p x c t i", x=4, t=PACK, i=8),
-            w4_raw[:].rearrange("p a c -> p (a c)").bitcast(U16).rearrange("p (x c i t) -> p x c t i", x=4, t=PACK, i=8),
-        )
-        nc.vector.tensor_copy(
-            w4_dealt[:].rearrange("p (x t c i) -> p x c t i", x=4, t=PACK, i=16),
-            w4_planes[:].rearrange("p (x c i t) -> p x c t i", x=4, t=PACK, i=16),
-        )
-
-        picked = [kept([P, S], U32, "picked%d" % a) for a in range(2)]
+        picked = [kept([P, S], U32, "picked0")]
         picked_planes = kept([P, S], U8, "picked_planes")
         nc.vector.tensor_copy(picked[0][:], table[0][:].bitcast(U32).indirect(offs_sb[:]))
         nc.vector.tensor_copy(picked_planes[:], tab_planes[:].indirect(offs_sb[:]))
@@ -106,10 +96,7 @@ def tile_list_malware_pair_family_kernel(tc, tab_words, tab_scales, offs, w1, po
             for piece, c0, width in raw[(b, a)]:
                 src = piece[:].rearrange("p j (m t) -> p m j t", t=PACK)
                 dst = dealt[:, :, c0 // PACK : (c0 + width) // PACK, :].rearrange("p t m j -> p m j t")
-                if c0 == 0:
-                    nc.scalar.copy(dst, src)
-                else:
-                    nc.vector.tensor_copy(dst, src)
+                nc.scalar.copy(dst, src)
             if b == 0:
                 for t in range(PACK):
                     nc.vector.quantize_mx(out=codes_of(b, t, a).bitcast(E4M3), scales=w1_planes[:, b, a, t, :], in_=dealt[:, t, :, :].rearrange("p m j -> p (m j)"))
@@ -132,49 +119,64 @@ def tile_list_malware_pair_family_kernel(tc, tab_words, tab_scales, offs, w1, po
                 stop=(a == 1),
             )
 
-        h = {(b, t): kept([P, S], F32, "h%d%d" % (b, t)) for b in range(2) for t in range(PACK)}
+        h = {}
 
         accs = {(t, half): bank(2 * t + half, [P, BANK], "acc_a") for t in range(PACK) for half in range(2)}
         quantise_w1(0, 0)
+        w4_dealt = kept([P, 2 * N], U8, "w4_dealt")
+        nc.vector.tensor_copy(
+            w4_dealt[:].rearrange("p (x t c i) -> p x c t i", x=4, t=PACK, i=16),
+            w4_planes[:].rearrange("p (x c i t) -> p x c t i", x=4, t=PACK, i=16),
+        )
+        picked.append(kept([P, S], U32, "picked1", tag="w4_planes"))
         nc.vector.tensor_copy(picked[1][:], table[1][:].bitcast(U32).indirect(offs_sb[:]))
         quantise_w1(0, 1)
+        w4_codes = kept([P, 2, 2 * N], U8, "w4_codes")
+        nc.vector.tensor_copy(
+            w4_codes[:].rearrange("p a c -> p (a c)").bitcast(U16).rearrange("p (x t c i) -> p x c t i", x=4, t=PACK, i=8),
+            w4_raw[:].rearrange("p a c -> p (a c)").bitcast(U16).rearrange("p (x c i t) -> p x c t i", x=4, t=PACK, i=8),
+        )
         for t in range(PACK):
             for half in range(2):
                 for a in range(2):
                     first_pass(accs[(t, half)], 0, t, half, a)
         for t in range(PACK):
+            h[(0, t)] = kept([P, S], F32, "h0%d" % t, tag="h0%d" % t if t < 2 else "w1_raw1%d_0" % (3 - t))
             for half in range(2):
                 nc.scalar.activation(h[(0, t)][:, half * BANK : (half + 1) * BANK], accs[(t, half)][:], ACT.Sigmoid)
-            if t < 2:
-                quantise_w1(1, t)
+            if t == 1:
+                for a in range(2):
+                    quantise_w1(1, a)
 
         inv_gain = kept([P, 2, PACK], F32, "inv_gain")
         nc.vector.reciprocal(inv_gain[:], gain[:])
 
         for t in range(PACK):
+            h[(1, t)] = kept([P, S], F32, "h1%d" % t)
             for half in range(2):
                 acc = bank(2 * t + half, [P, BANK], "acc_b")
                 for a in range(2):
                     first_pass(acc, 1, t, half, a)
                 nc.scalar.activation(h[(1, t)][:, half * BANK : (half + 1) * BANK], acc[:], ACT.Sigmoid)
 
-        z_codes = {(b, j0): kept([P, CHUNK], U32, "z_codes", tag="z_codes%d_%d" % (b, j0)) for b in range(2) for j0 in range(0, PAIRS, CHUNK)}
+        z_codes = {}
         z_planes = kept([P, 2, PAIRS], U8, "z_planes")
 
         def pick(b, j0, width, tags):
-            larger = kept([P, PACK, width], F32, "larger%d_%d" % (b, j0))
             smaller = kept([P, PACK, width], F32, "smaller%d_%d" % (b, j0))
             cols = slice(j0 // 16, (j0 + width) // 16)
             together = PACK // len(tags)
-            for n, tag in enumerate(tags):
-                pair = kept([P, 2, together, width], F32, "pair", tag=tag)
+            larger = []
+            for n, (pair_tag, larger_tag) in enumerate(tags):
+                pair = kept([P, 2, together, width], F32, "pair", tag=pair_tag)
                 for u in range(together):
                     window = h[(b, n * together + u)]
                     nc.vector.tensor_copy(pair[:, 0, u, :], window[:].indirect(pos1_sb[:, cols]))
                     nc.vector.tensor_copy(pair[:, 1, u, :], window[:].indirect(pos2_sb[:, cols]))
-                rows = slice(n * together, (n + 1) * together)
-                nc.vector.tensor_tensor(larger[:, rows, :], pair[:, 0, :, :], pair[:, 1, :, :], ALU.max)
-                nc.vector.tensor_tensor(smaller[:, rows, :], pair[:, 0, :, :], pair[:, 1, :, :], ALU.min)
+                most = kept([P, together, width], F32, "larger", tag=larger_tag)
+                nc.vector.tensor_tensor(most[:], pair[:, 0, :, :], pair[:, 1, :, :], ALU.max)
+                nc.vector.tensor_tensor(smaller[:, n * together : (n + 1) * together, :], pair[:, 0, :, :], pair[:, 1, :, :], ALU.min)
+                larger.extend(most[:, u, :] for u in range(together))
             return larger, smaller
 
         def invert(b, width, larger, tag):
@@ -182,28 +184,31 @@ def tile_list_malware_pair_family_kernel(tc, tab_words, tab_scales, offs, w1, po
             together = PAIRS // width
             for t0 in range(0, PACK, together):
                 for t in range(t0, t0 + together):
-                    nc.scalar.activation(part[:, t, :], larger[:, t, :], ACT.Abs_reciprocal_sqrt, scale=inv_gain[:, b, t : t + 1])
+                    nc.scalar.activation(part[:, t, :], larger[t], ACT.Abs_reciprocal_sqrt, scale=inv_gain[:, b, t : t + 1])
                 nc.scalar.activation(part[:, t0 : t0 + together, :], part[:, t0 : t0 + together, :], ACT.Square)
             return part
 
-        def agree(b, j0, smaller, part, tag):
-            z = kept([P, CHUNK, PACK], BF16, "z", tag=tag)
+        def agree(b, j0, width, smaller, part, tag):
+            z = kept([P, width, PACK], BF16, "z", tag=tag)
+            codes = kept([P, width], U32, "z_codes%d_%d" % (b, j0))
             nc.vector.tensor_tensor(
                 z[:].rearrange("p (c i) t -> p c t i", i=4),
                 smaller.rearrange("p t (c i) -> p c t i", i=4),
                 part.rearrange("p t (c i) -> p c t i", i=4),
                 ALU.mult,
             )
-            nc.vector.quantize_mx(out=z_codes[(b, j0)][:].bitcast(E4M3), scales=z_planes[:, b, j0 : j0 + CHUNK], in_=z[:].rearrange("p j t -> p (j t)"))
+            nc.vector.quantize_mx(out=codes[:].bitcast(E4M3), scales=z_planes[:, b, j0 : j0 + width], in_=z[:].rearrange("p j t -> p (j t)"))
+            for c0 in range(0, width, CHUNK):
+                z_codes[(b, j0 + c0)] = codes[:, c0 : c0 + CHUNK]
 
-        def second_pass(acc, a, grp, j0):
-            for t in range(PACK):
+        def second_pass(a, j0):
+            for grp, t in product(range(2), range(PACK)):
                 c0 = SPAN * grp + P * t
                 nc.tensor.matmul_mx(
-                    out=acc[:, t, :],
+                    out=sums[j0][grp][:, t, :],
                     lhsT=w4_codes[:, a, 2 * c0 : 2 * (c0 + P)].bitcast(E2M1),
                     lhsT_scale=w4_dealt[:, a * N + c0 : a * N + c0 + P],
-                    rhs=z_codes[(a, j0)][:].bitcast(E4M3),
+                    rhs=z_codes[(a, j0)].bitcast(E4M3),
                     rhs_scale=z_planes[:, a, j0 : j0 + CHUNK],
                     start=(a == 0 and t == 0),
                     stop=(a == 1 and t == PACK - 1),
@@ -226,26 +231,36 @@ def tile_list_malware_pair_family_kernel(tc, tab_words, tab_scales, offs, w1, po
                 else:
                     nc.scalar.copy(dst, src)
                 nc.vector.quantize_mx(out=y_codes[:, grp, :].bitcast(E4M3), scales=y_planes[:, grp, j0 : j0 + CHUNK], in_=rounded[:].rearrange("p j t -> p (j t)"))
-            nc.sync.dma_start(out_1[:, :, j0 : j0 + CHUNK, :].rearrange("g p m i -> p g (m i)").bitcast(I32), y_codes[:])
+            queue = nc.scalar if shared else nc.sync
+            queue.dma_start(out_1[:, :, j0 : j0 + CHUNK, :].rearrange("g p m i -> p g (m i)").bitcast(I32), y_codes[:])
 
         starts = list(range(0, PAIRS, CHUNK))
-        larger_a, smaller_a = pick(0, 0, PAIRS, ("pair", "stage1"))
+        larger_a, smaller_a = pick(0, 0, PAIRS, (("w4_raw", "stage1"), ("stage0", "larger_a")))
         part_a = invert(0, PAIRS, larger_a, "codes_then_inverse")
-        larger_b, smaller_b = pick(1, 0, 2 * CHUNK, ("pair",))
-        part_b = invert(1, 2 * CHUNK, larger_b, "larger0_0")
-        ready = {j0: (smaller_b[:, :, j0 : j0 + CHUNK], part_b[:, :, j0 : j0 + CHUNK]) for j0 in starts[:2]}
+        larger_b, smaller_b = pick(1, 0, 2 * CHUNK, (("w4_raw", "larger_b"),))
+        part_b = invert(1, 2 * CHUNK, larger_b, "larger_a")
         sums = {j0: [bank(2 * n + grp, [P, PACK, CHUNK], "sums") for grp in range(2)] for n, j0 in enumerate(starts)}
-        for n, j0 in enumerate(starts):
-            agree(0, j0, smaller_a[:, :, j0 : j0 + CHUNK], part_a[:, :, j0 : j0 + CHUNK], "chain%d" % n)
-            for grp in range(2):
-                second_pass(sums[j0][grp], 0, grp, j0)
-            agree(1, j0, ready[j0][0], ready[j0][1], "chain%d" % (n + 1))
-            for grp in range(2):
-                second_pass(sums[j0][grp], 1, grp, j0)
-            hand_out(j0, sums[j0], n >= 2)
-            if n + 2 < len(starts):
-                ahead = starts[n + 2]
-                larger, smaller = pick(1, ahead, CHUNK, ("chain%d" % (n + 1),))
-                ready[ahead] = (smaller[:], invert(1, CHUNK, larger, "z_codes1_%d" % j0)[:])
+        half = 2 * CHUNK
+        agree(0, 0, half, smaller_a[:, :, 0:half], part_a[:, :, 0:half], "z_a")
+        agree(1, 0, half, smaller_b[:], part_b[:], "z_b")
+        for j0 in starts[:2]:
+            for a in range(2):
+                second_pass(a, j0)
+        late = {}
+        hand_out(starts[0], sums[starts[0]], False)
+        larger, smaller = pick(1, starts[2], CHUNK, (("smaller1_0", "larger_c"),))
+        late[starts[2]] = (smaller, invert(1, CHUNK, larger, "z_codes1_0"))
+        agree(0, half, half, smaller_a[:, :, half:PAIRS], part_a[:, :, half:PAIRS], "smaller1_0")
+        for j0 in starts[2:]:
+            second_pass(0, j0)
+        hand_out(starts[1], sums[starts[1]], False)
+        larger, smaller = pick(1, starts[3], CHUNK, (("z_b", "larger_d"),))
+        late[starts[3]] = (smaller, invert(1, CHUNK, larger, "inverse_last"))
+        for j0 in starts[2:]:
+            agree(1, j0, CHUNK, late[j0][0][:], late[j0][1][:], "z_late%d" % j0)
+            second_pass(1, j0)
+        for j0 in starts[2:]:
+            hand_out(j0, sums[j0], j0 == starts[-1])
         for q in range(4):
-            nc.sync.dma_start(out_2[:, 4 * q : 4 * q + 4, :].rearrange("g r m -> r g m").bitcast(I32), y_planes[32 * q : 32 * q + 4, :, :].bitcast(I32))
+            queue = nc.scalar if q % 2 else nc.sync
+            queue.dma_start(out_2[:, 4 * q : 4 * q + 4, :].rearrange("g r m -> r g m").bitcast(I32), y_planes[32 * q : 32 * q + 4, :, :].bitcast(I32))

@@ -20,11 +20,17 @@ ALU = mybir.AluOpType
 P = 128
 PACK = 4
 SPAN = P * PACK
+SPANS = 2
+QUADS = 4
 BANK = 512
-CHUNK = 128
+CHUNK = BANK // PACK
+LINE = 16
+PER_COLUMN = 16
 
 
-def tile_list_malware_pair_family_kernel(tc, tab_words, tab_scales, offs, w1, pos1, pos2, g, w4_words, w4_scales, out_0, out_1, out_2):
+def tile_list_malware_pair_family_kernel(
+    tc, tab_words, tab_scales, offs, w1, pos1, pos2, g, w4_words, w4_scales, out_0, out_1, out_2
+):
     nc = tc.nc
     with ExitStack() as ctx:
         keep = ctx.enter_context(tc.tile_pool(name="keep", bufs=1))
@@ -37,134 +43,142 @@ def tile_list_malware_pair_family_kernel(tc, tab_words, tab_scales, offs, w1, po
         def bank(index, shape, name):
             return psum.tile(shape, F32, name=name, tag="bank%d" % index)
 
-        offs_sb = keep.tile([P, S // 16], U16, name="offs_sb")
-        pos1_sb = keep.tile([P, PAIRS // 16], U16, name="pos1_sb")
-        pos2_sb = keep.tile([P, PAIRS // 16], U16, name="pos2_sb")
+        offs_sb = keep.tile([P, S // PER_COLUMN], U16, name="offs_sb")
+        pos1_sb = keep.tile([P, PAIRS // PER_COLUMN], U16, name="pos1_sb")
+        pos2_sb = keep.tile([P, PAIRS // PER_COLUMN], U16, name="pos2_sb")
 
         tab_planes = kept([P, T], U8, "tab_planes")
         nc.vector.memset(tab_planes[:].bitcast(I32), 0)
-        w4_planes = kept([P, 2 * N], U8, "w4_planes")
+        w4_planes = kept([P, SPANS * N], U8, "w4_planes")
         nc.vector.memset(w4_planes[:].bitcast(I32), 0)
-        warm = kept([P, 1], F32, "warm")
-        nc.vector.memset(warm[:], 0.0)
-        nc.scalar.activation(warm[:], warm[:], ACT.Sigmoid)
 
         nc.sync.dma_start(offs_sb[:], offs)
-        table = [kept([P, T], I32, "table%d" % a) for a in range(2)]
-        words = [tab_words[a].rearrange("p t i -> p (t i)").bitcast(I32) for a in range(2)]
-        nc.sync.dma_start(table[0][:], words[0])
-        for q in range(4):
-            nc.gpsimd.dma_start(tab_planes[32 * q : 32 * q + 8, :].bitcast(I32), tab_scales[:, 4 * q : 4 * q + 4, :].bitcast(I32))
-        for q in range(4):
+        table = [kept([P, T], I32, "table%d" % a) for a in range(SPANS)]
+        table_hbm = [tab_words[a].rearrange("p t i -> p (t i)").bitcast(I32) for a in range(SPANS)]
+        nc.sync.dma_start(table[0][:], table_hbm[0])
+        for q in range(QUADS):
+            nc.gpsimd.dma_start(
+                tab_planes[32 * q : 32 * q + 4 * SPANS, :].bitcast(I32), tab_scales[:, 4 * q : 4 * q + 4, :].bitcast(I32)
+            )
+        for q in range(QUADS):
             nc.sync.dma_start(
-                w4_planes[32 * q : 32 * q + 4, :].rearrange("r (a c) -> r a c", a=2).bitcast(I32),
+                w4_planes[32 * q : 32 * q + 4, :].rearrange("r (a c) -> r a c", a=SPANS).bitcast(I32),
                 w4_scales[:, 4 * q : 4 * q + 4, :].rearrange("a r c -> r a c").bitcast(I32),
             )
 
         def load_w1(b, a, c0, width):
-            raw = kept([P, PACK, width], F32, "w1_raw%d%d_%d" % (b, a, c0))
+            piece = kept([P, PACK, width], F32, "w1_raw%d%d_%d" % (b, a, c0))
             cols = slice(SPAN * b + c0, SPAN * b + c0 + width)
-            nc.sync.dma_start(raw[:], w1[SPAN * a : SPAN * (a + 1), cols].rearrange("(p j) c -> p j c", j=PACK))
-            return raw, c0, width
+            nc.sync.dma_start(piece[:], w1[SPAN * a : SPAN * (a + 1), cols].rearrange("(p j) c -> p j c", j=PACK))
+            return piece, c0, width
 
         raw = {(0, 0): [load_w1(0, 0, 0, SPAN)]}
-        nc.sync.dma_start(table[1][:], words[1])
+        nc.sync.dma_start(table[1][:], table_hbm[1])
         raw[(0, 1)] = [load_w1(0, 1, c0, SPAN // 2) for c0 in (0, SPAN // 2)]
-        w4_raw = kept([P, 2, 2 * N], U8, "w4_raw")
+        w4_raw = kept([P, SPANS, 2 * N], U8, "w4_raw")
         nc.sync.dma_start(w4_raw[:].bitcast(I32), w4_words.rearrange("a p c -> p a c").bitcast(I32))
         nc.sync.dma_start(pos1_sb[:], pos1)
         nc.sync.dma_start(pos2_sb[:], pos2)
-        for a in range(2):
+        for a in range(SPANS):
             raw[(1, a)] = [load_w1(1, a, 0, SPAN)]
-        gain = kept([P, 2, PACK], F32, "gain")
-        nc.sync.dma_start(gain[:], g.rearrange("(b p t) -> p b t", b=2, t=PACK))
+        gain = kept([P, SPANS, PACK], F32, "gain")
+        nc.sync.dma_start(gain[:], g.rearrange("(b p t) -> p b t", b=SPANS, t=PACK))
 
         picked = [kept([P, S], U32, "picked0")]
         picked_planes = kept([P, S], U8, "picked_planes")
         nc.vector.tensor_copy(picked[0][:], table[0][:].bitcast(U32).indirect(offs_sb[:]))
         nc.vector.tensor_copy(picked_planes[:], tab_planes[:].indirect(offs_sb[:]))
 
-        w1_codes = {(0, t): kept([P, 2, P], U32, "w1_codes0%d" % t, tag="stage%d" % t) for t in range(PACK)}
-        second_codes = kept([P, 2, PACK, P], U32, "w1_codes1", tag="codes_then_inverse")
-        w1_planes = kept([P, 2, 2, PACK, P], U8, "w1_planes")
-
-        def codes_of(b, t, a):
-            return w1_codes[(0, t)][:, a, :] if b == 0 else second_codes[:, a, t, :]
+        first_codes = [kept([P, SPANS, P], U32, "w1_codes0%d" % t, tag="stage%d" % t) for t in range(PACK)]
+        second_codes = kept([P, SPANS, PACK, P], U32, "w1_codes1", tag="codes_then_inverse")
+        w1_planes = kept([P, SPANS, SPANS, PACK, P], U8, "w1_planes")
 
         def quantise_w1(b, a):
             dealt = kept([P, PACK, P, PACK], BF16, "dealt", tag=("dealt%d" if b == 0 else "stage%d") % a)
             for piece, c0, width in raw[(b, a)]:
                 src = piece[:].rearrange("p j (m t) -> p m j t", t=PACK)
                 dst = dealt[:, :, c0 // PACK : (c0 + width) // PACK, :].rearrange("p t m j -> p m j t")
-                nc.scalar.copy(dst, src)
+                if c0 == 0:
+                    nc.scalar.copy(dst, src)
+                else:
+                    share = width // PACK // 2
+                    nc.scalar.copy(dst[:, :share], src[:, :share])
+                    nc.vector.tensor_copy(dst[:, share:], src[:, share:])
             if b == 0:
                 for t in range(PACK):
-                    nc.vector.quantize_mx(out=codes_of(b, t, a).bitcast(E4M3), scales=w1_planes[:, b, a, t, :], in_=dealt[:, t, :, :].rearrange("p m j -> p (m j)"))
+                    nc.vector.quantize_mx(
+                        out=first_codes[t][:, a, :].bitcast(E4M3),
+                        scales=w1_planes[:, b, a, t, :],
+                        in_=dealt[:, t, :, :].rearrange("p m j -> p (m j)"),
+                    )
             else:
-                nc.vector.quantize_mx(
-                    out=second_codes[:, a, :, :].rearrange("p t m -> p (t m)").bitcast(E4M3),
-                    scales=w1_planes[:, b, a, :, :].rearrange("p t m -> p (t m)"),
-                    in_=dealt[:].rearrange("p t m j -> p (t m j)"),
+                together = PACK // (a + 1)
+                for t0 in range(0, PACK, together):
+                    rows = slice(t0, t0 + together)
+                    nc.vector.quantize_mx(
+                        out=second_codes[:, a, rows, :].rearrange("p t m -> p (t m)").bitcast(E4M3),
+                        scales=w1_planes[:, b, a, rows, :].rearrange("p t m -> p (t m)"),
+                        in_=dealt[:, rows, :, :].rearrange("p t m j -> p (t m j)"),
+                    )
+
+        def first_product(acc, b, t, half):
+            cols = slice(half * BANK, (half + 1) * BANK)
+            for a in range(SPANS):
+                codes = first_codes[t][:, a, :] if b == 0 else second_codes[:, a, t, :]
+                nc.tensor.matmul_mx(
+                    out=acc[:],
+                    lhsT=codes.bitcast(E4M3),
+                    lhsT_scale=w1_planes[:, b, a, t, :],
+                    rhs=picked[a][:, cols].bitcast(E4M3),
+                    rhs_scale=picked_planes[4 * a : P, cols],
+                    start=(a == 0),
+                    stop=(a == SPANS - 1),
                 )
 
-        def first_pass(acc, b, t, half, a):
-            cols = slice(half * BANK, (half + 1) * BANK)
-            nc.tensor.matmul_mx(
-                out=acc[:],
-                lhsT=codes_of(b, t, a).bitcast(E4M3),
-                lhsT_scale=w1_planes[:, b, a, t, :],
-                rhs=picked[a][:, cols].bitcast(E4M3),
-                rhs_scale=picked_planes[4 * a : P, cols],
-                start=(a == 0),
-                stop=(a == 1),
-            )
-
-        h = {}
-
-        accs = {(t, half): bank(2 * t + half, [P, BANK], "acc_a") for t in range(PACK) for half in range(2)}
+        halves = range(S // BANK)
+        accs = {(t, half): bank(2 * t + half, [P, BANK], "acc_a") for t in range(PACK) for half in halves}
         quantise_w1(0, 0)
-        w4_dealt = kept([P, 2 * N], U8, "w4_dealt")
+        w4_dealt_planes = kept([P, SPANS * N], U8, "w4_dealt_planes")
         nc.vector.tensor_copy(
-            w4_dealt[:].rearrange("p (x t c i) -> p x c t i", x=4, t=PACK, i=16),
-            w4_planes[:].rearrange("p (x c i t) -> p x c t i", x=4, t=PACK, i=16),
+            w4_dealt_planes[:].rearrange("p (x t c i) -> p x c t i", x=SPANS * SPANS, t=PACK, i=LINE),
+            w4_planes[:].rearrange("p (x c i t) -> p x c t i", x=SPANS * SPANS, t=PACK, i=LINE),
         )
         picked.append(kept([P, S], U32, "picked1", tag="w4_planes"))
         nc.vector.tensor_copy(picked[1][:], table[1][:].bitcast(U32).indirect(offs_sb[:]))
         quantise_w1(0, 1)
-        w4_codes = kept([P, 2, 2 * N], U8, "w4_codes")
+        w4_codes = kept([P, SPANS, 2 * N], U8, "w4_codes")
         nc.vector.tensor_copy(
-            w4_codes[:].rearrange("p a c -> p (a c)").bitcast(U16).rearrange("p (x t c i) -> p x c t i", x=4, t=PACK, i=8),
-            w4_raw[:].rearrange("p a c -> p (a c)").bitcast(U16).rearrange("p (x c i t) -> p x c t i", x=4, t=PACK, i=8),
+            w4_codes[:].rearrange("p a c -> p (a c)").bitcast(U16).rearrange("p (x t c i) -> p x c t i", x=SPANS * SPANS, t=PACK, i=LINE // 2),
+            w4_raw[:].rearrange("p a c -> p (a c)").bitcast(U16).rearrange("p (x c i t) -> p x c t i", x=SPANS * SPANS, t=PACK, i=LINE // 2),
         )
+        for t, half in product(range(PACK), halves):
+            first_product(accs[(t, half)], 0, t, half)
+
+        h = {}
         for t in range(PACK):
-            for half in range(2):
-                for a in range(2):
-                    first_pass(accs[(t, half)], 0, t, half, a)
-        for t in range(PACK):
-            h[(0, t)] = kept([P, S], F32, "h0%d" % t, tag="h0%d" % t if t < 2 else "w1_raw1%d_0" % (3 - t))
-            for half in range(2):
+            h[(0, t)] = kept([P, S], F32, "h0%d" % t, tag="h0%d" % t if t < SPANS else "w1_raw1%d_0" % (PACK - 1 - t))
+            for half in halves:
                 nc.scalar.activation(h[(0, t)][:, half * BANK : (half + 1) * BANK], accs[(t, half)][:], ACT.Sigmoid)
-            if t == 1:
-                for a in range(2):
+            if t == SPANS - 1:
+                for a in range(SPANS):
                     quantise_w1(1, a)
 
-        inv_gain = kept([P, 2, PACK], F32, "inv_gain")
+        inv_gain = kept([P, SPANS, PACK], F32, "inv_gain")
         nc.vector.reciprocal(inv_gain[:], gain[:])
 
         for t in range(PACK):
             h[(1, t)] = kept([P, S], F32, "h1%d" % t)
-            for half in range(2):
+            for half in halves:
                 acc = bank(2 * t + half, [P, BANK], "acc_b")
-                for a in range(2):
-                    first_pass(acc, 1, t, half, a)
+                first_product(acc, 1, t, half)
                 nc.scalar.activation(h[(1, t)][:, half * BANK : (half + 1) * BANK], acc[:], ACT.Sigmoid)
 
         z_codes = {}
-        z_planes = kept([P, 2, PAIRS], U8, "z_planes")
+        z_planes = kept([P, SPANS, PAIRS], U8, "z_planes")
 
         def pick(b, j0, width, tags):
             smaller = kept([P, PACK, width], F32, "smaller%d_%d" % (b, j0))
-            cols = slice(j0 // 16, (j0 + width) // 16)
+            cols = slice(j0 // PER_COLUMN, (j0 + width) // PER_COLUMN)
             together = PACK // len(tags)
             larger = []
             for n, (pair_tag, larger_tag) in enumerate(tags):
@@ -175,92 +189,105 @@ def tile_list_malware_pair_family_kernel(tc, tab_words, tab_scales, offs, w1, po
                     nc.vector.tensor_copy(pair[:, 1, u, :], window[:].indirect(pos2_sb[:, cols]))
                 most = kept([P, together, width], F32, "larger", tag=larger_tag)
                 nc.vector.tensor_tensor(most[:], pair[:, 0, :, :], pair[:, 1, :, :], ALU.max)
-                nc.vector.tensor_tensor(smaller[:, n * together : (n + 1) * together, :], pair[:, 0, :, :], pair[:, 1, :, :], ALU.min)
+                nc.vector.tensor_tensor(
+                    smaller[:, n * together : (n + 1) * together, :], pair[:, 0, :, :], pair[:, 1, :, :], ALU.min
+                )
                 larger.extend(most[:, u, :] for u in range(together))
             return larger, smaller
 
         def invert(b, width, larger, tag):
-            part = kept([P, PACK, width], F32, "inverse", tag=tag)
+            inverse = kept([P, PACK, width], F32, "inverse", tag=tag)
             together = PAIRS // width
             for t0 in range(0, PACK, together):
                 for t in range(t0, t0 + together):
-                    nc.scalar.activation(part[:, t, :], larger[t], ACT.Abs_reciprocal_sqrt, scale=inv_gain[:, b, t : t + 1])
-                nc.scalar.activation(part[:, t0 : t0 + together, :], part[:, t0 : t0 + together, :], ACT.Square)
-            return part
+                    nc.scalar.activation(inverse[:, t, :], larger[t], ACT.Abs_reciprocal_sqrt, scale=inv_gain[:, b, t : t + 1])
+                nc.scalar.activation(inverse[:, t0 : t0 + together, :], inverse[:, t0 : t0 + together, :], ACT.Square)
+            return inverse
 
-        def agree(b, j0, width, smaller, part, tag):
+        def agree(b, j0, width, smaller, inverse, tag):
             z = kept([P, width, PACK], BF16, "z", tag=tag)
             codes = kept([P, width], U32, "z_codes%d_%d" % (b, j0))
             nc.vector.tensor_tensor(
-                z[:].rearrange("p (c i) t -> p c t i", i=4),
-                smaller.rearrange("p t (c i) -> p c t i", i=4),
-                part.rearrange("p t (c i) -> p c t i", i=4),
+                z[:].rearrange("p (c i) t -> p c t i", i=LINE // 4),
+                smaller.rearrange("p t (c i) -> p c t i", i=LINE // 4),
+                inverse.rearrange("p t (c i) -> p c t i", i=LINE // 4),
                 ALU.mult,
             )
-            nc.vector.quantize_mx(out=codes[:].bitcast(E4M3), scales=z_planes[:, b, j0 : j0 + width], in_=z[:].rearrange("p j t -> p (j t)"))
+            nc.vector.quantize_mx(
+                out=codes[:].bitcast(E4M3), scales=z_planes[:, b, j0 : j0 + width], in_=z[:].rearrange("p j t -> p (j t)")
+            )
             for c0 in range(0, width, CHUNK):
                 z_codes[(b, j0 + c0)] = codes[:, c0 : c0 + CHUNK]
 
         def second_pass(a, j0):
-            for grp, t in product(range(2), range(PACK)):
+            for grp, t in product(range(SPANS), range(PACK)):
                 c0 = SPAN * grp + P * t
                 nc.tensor.matmul_mx(
                     out=sums[j0][grp][:, t, :],
                     lhsT=w4_codes[:, a, 2 * c0 : 2 * (c0 + P)].bitcast(E2M1),
-                    lhsT_scale=w4_dealt[:, a * N + c0 : a * N + c0 + P],
+                    lhsT_scale=w4_dealt_planes[:, a * N + c0 : a * N + c0 + P],
                     rhs=z_codes[(a, j0)].bitcast(E4M3),
                     rhs_scale=z_planes[:, a, j0 : j0 + CHUNK],
                     start=(a == 0 and t == 0),
-                    stop=(a == 1 and t == PACK - 1),
+                    stop=(a == SPANS - 1 and t == PACK - 1),
                 )
 
-        y_planes = kept([P, 2, PAIRS], U8, "y_planes")
+        y_planes = kept([P, SPANS, PAIRS], U8, "y_planes")
 
-        def hand_out(j0, accs, shared):
-            y_codes = ring.tile([P, 2, CHUNK], I32, name="y_codes", align_bytes=64)
-            for step in range(2):
+        def hand_out(j0, last):
+            y_codes = ring.tile([P, SPANS, CHUNK], I32, name="y_codes", align_bytes=64)
+            for step in range(SPANS):
                 y = ring.tile([P, PACK, CHUNK], F32, name="y", tag="y%d" % step)
-                nc.scalar.copy(y[:], accs[step][:])
-                nc.sync.dma_start(out_0[SPAN * step : SPAN * (step + 1), j0 : j0 + CHUNK].rearrange("(p t) j -> p t j", t=PACK), y[:])
-                grp = 1 - step if shared else step
+                nc.scalar.copy(y[:], sums[j0][step][:])
+                nc.sync.dma_start(
+                    out_0[SPAN * step : SPAN * (step + 1), j0 : j0 + CHUNK].rearrange("(p t) j -> p t j", t=PACK), y[:]
+                )
+                grp = SPANS - 1 - step if last else step
                 rounded = ring.tile([P, CHUNK, PACK], BF16, name="rounded", tag="rounded%d" % grp, align_bytes=64)
-                dst = rounded[:].rearrange("p (c i) t -> p c t i", i=4)
-                src = accs[grp][:].rearrange("p t (c i) -> p c t i", i=4)
-                if shared:
+                dst = rounded[:].rearrange("p (c i) t -> p c t i", i=LINE // 4)
+                src = sums[j0][grp][:].rearrange("p t (c i) -> p c t i", i=LINE // 4)
+                if last:
                     nc.vector.tensor_copy(dst, src)
                 else:
                     nc.scalar.copy(dst, src)
-                nc.vector.quantize_mx(out=y_codes[:, grp, :].bitcast(E4M3), scales=y_planes[:, grp, j0 : j0 + CHUNK], in_=rounded[:].rearrange("p j t -> p (j t)"))
-            queue = nc.scalar if shared else nc.sync
+                nc.vector.quantize_mx(
+                    out=y_codes[:, grp, :].bitcast(E4M3),
+                    scales=y_planes[:, grp, j0 : j0 + CHUNK],
+                    in_=rounded[:].rearrange("p j t -> p (j t)"),
+                )
+            queue = nc.scalar if last else nc.sync
             queue.dma_start(out_1[:, :, j0 : j0 + CHUNK, :].rearrange("g p m i -> p g (m i)").bitcast(I32), y_codes[:])
 
-        starts = list(range(0, PAIRS, CHUNK))
-        larger_a, smaller_a = pick(0, 0, PAIRS, (("w4_raw", "stage1"), ("stage0", "larger_a")))
-        part_a = invert(0, PAIRS, larger_a, "codes_then_inverse")
-        larger_b, smaller_b = pick(1, 0, 2 * CHUNK, (("w4_raw", "larger_b"),))
-        part_b = invert(1, 2 * CHUNK, larger_b, "larger_a")
-        sums = {j0: [bank(2 * n + grp, [P, PACK, CHUNK], "sums") for grp in range(2)] for n, j0 in enumerate(starts)}
-        half = 2 * CHUNK
-        agree(0, 0, half, smaller_a[:, :, 0:half], part_a[:, :, 0:half], "z_a")
-        agree(1, 0, half, smaller_b[:], part_b[:], "z_b")
-        for j0 in starts[:2]:
-            for a in range(2):
-                second_pass(a, j0)
-        late = {}
-        hand_out(starts[0], sums[starts[0]], False)
-        larger, smaller = pick(1, starts[2], CHUNK, (("smaller1_0", "larger_c"),))
-        late[starts[2]] = (smaller, invert(1, CHUNK, larger, "z_codes1_0"))
-        agree(0, half, half, smaller_a[:, :, half:PAIRS], part_a[:, :, half:PAIRS], "smaller1_0")
-        for j0 in starts[2:]:
+        first, second, third, fourth = range(0, PAIRS, CHUNK)
+        larger_a, smaller_a = pick(0, first, PAIRS, (("w4_raw", "stage1"), ("stage0", "larger_a")))
+        inverse_a = invert(0, PAIRS, larger_a, "codes_then_inverse")
+        larger_b, smaller_b = pick(1, first, third, (("w4_raw", "larger_b"),))
+        inverse_b = invert(1, third, larger_b, "larger_a")
+        sums = {
+            j0: [bank(SPANS * (j0 // CHUNK) + grp, [P, PACK, CHUNK], "sums") for grp in range(SPANS)]
+            for j0 in (first, second, third, fourth)
+        }
+        agree(0, first, third, smaller_a[:, :, first:third], inverse_a[:, :, first:third], "z_a")
+        agree(1, first, third, smaller_b[:], inverse_b[:], "z_b")
+        for j0, a in product((first, second), range(SPANS)):
+            second_pass(a, j0)
+        hand_out(first, False)
+        larger_c, smaller_c = pick(1, third, CHUNK, (("smaller1_0", "larger_c"),))
+        inverse_c = invert(1, CHUNK, larger_c, "z_codes1_0")
+        agree(0, third, PAIRS - third, smaller_a[:, :, third:PAIRS], inverse_a[:, :, third:PAIRS], "smaller1_0")
+        for j0 in (third, fourth):
             second_pass(0, j0)
-        hand_out(starts[1], sums[starts[1]], False)
-        larger, smaller = pick(1, starts[3], CHUNK, (("z_b", "larger_d"),))
-        late[starts[3]] = (smaller, invert(1, CHUNK, larger, "inverse_last"))
-        for j0 in starts[2:]:
-            agree(1, j0, CHUNK, late[j0][0][:], late[j0][1][:], "z_late%d" % j0)
+        hand_out(second, False)
+        larger_d, smaller_d = pick(1, fourth, CHUNK, (("z_b", "larger_d"),))
+        inverse_d = invert(1, CHUNK, larger_d, "inverse_d")
+        for j0, smaller, inverse in ((third, smaller_c, inverse_c), (fourth, smaller_d, inverse_d)):
+            agree(1, j0, CHUNK, smaller[:], inverse[:], "z_late%d" % j0)
             second_pass(1, j0)
-        for j0 in starts[2:]:
-            hand_out(j0, sums[j0], j0 == starts[-1])
-        for q in range(4):
+        for j0 in (third, fourth):
+            hand_out(j0, j0 == fourth)
+        for q in range(QUADS):
             queue = nc.scalar if q % 2 else nc.sync
-            queue.dma_start(out_2[:, 4 * q : 4 * q + 4, :].rearrange("g r m -> r g m").bitcast(I32), y_planes[32 * q : 32 * q + 4, :, :].bitcast(I32))
+            queue.dma_start(
+                out_2[:, 4 * q : 4 * q + 4, :].rearrange("g r m -> r g m").bitcast(I32),
+                y_planes[32 * q : 32 * q + 4, :, :].bitcast(I32),
+            )

@@ -34,7 +34,6 @@ def tile_list_malware_pair_family_kernel(
     nc = tc.nc
     with ExitStack() as ctx:
         keep = ctx.enter_context(tc.tile_pool(name="keep", bufs=1))
-        ring = ctx.enter_context(tc.tile_pool(name="ring", bufs=2))
         psum = ctx.enter_context(tc.psum_pool(name="psum", bufs=1))
 
         def kept(shape, dtype, name, tag=None):
@@ -75,59 +74,48 @@ def tile_list_malware_pair_family_kernel(
         raw = {(0, 0): [load_w1(0, 0, 0, SPAN)]}
         nc.sync.dma_start(table[1][:], table_hbm[1])
         raw[(0, 1)] = [load_w1(0, 1, c0, SPAN // 2) for c0 in (0, SPAN // 2)]
-        w4_raw = kept([P, SPANS, 2 * N], U8, "w4_raw")
-        nc.sync.dma_start(w4_raw[:].bitcast(I32), w4_words.rearrange("a p c -> p a c").bitcast(I32))
         nc.sync.dma_start(pos1_sb[:], pos1)
+        raw[(1, 0)] = [load_w1(1, 0, 0, SPAN)]
+        raw[(1, 1)] = [load_w1(1, 1, c0, SPAN // 2) for c0 in (0, SPAN // 2)]
         nc.sync.dma_start(pos2_sb[:], pos2)
-        for a in range(SPANS):
-            raw[(1, a)] = [load_w1(1, a, 0, SPAN)]
         gain = kept([P, SPANS, PACK], F32, "gain")
         nc.sync.dma_start(gain[:], g.rearrange("(b p t) -> p b t", b=SPANS, t=PACK))
+        w4_raw = kept([P, SPANS, 2 * N], U8, "w4_raw")
+        nc.sync.dma_start(w4_raw[:].bitcast(I32), w4_words.rearrange("a p c -> p a c").bitcast(I32))
 
-        picked = [kept([P, S], U32, "picked0")]
+        picked = [kept([P, S], U32, "picked%d" % a) for a in range(SPANS)]
         picked_planes = kept([P, S], U8, "picked_planes")
         nc.vector.tensor_copy(picked[0][:], table[0][:].bitcast(U32).indirect(offs_sb[:]))
         nc.vector.tensor_copy(picked_planes[:], tab_planes[:].indirect(offs_sb[:]))
 
-        first_codes = [kept([P, SPANS, P], U32, "w1_codes0%d" % t, tag="stage%d" % t) for t in range(PACK)]
-        second_codes = kept([P, SPANS, PACK, P], U32, "w1_codes1", tag="codes_then_inverse")
+        w1_codes = {}
         w1_planes = kept([P, SPANS, SPANS, PACK, P], U8, "w1_planes")
 
-        def quantise_w1(b, a):
-            dealt = kept([P, PACK, P, PACK], BF16, "dealt", tag=("dealt%d" if b == 0 else "stage%d") % a)
-            for piece, c0, width in raw[(b, a)]:
+        def quantise_w1(b, a, engines, together):
+            dealt = kept([P, PACK, P, PACK], BF16, "dealt%d%d" % (b, a))
+            for (piece, c0, width), copy in zip(raw[(b, a)], engines):
                 src = piece[:].rearrange("p j (m t) -> p m j t", t=PACK)
                 dst = dealt[:, :, c0 // PACK : (c0 + width) // PACK, :].rearrange("p t m j -> p m j t")
-                if c0 == 0:
-                    nc.scalar.copy(dst, src)
-                else:
-                    share = width // PACK // 2
-                    nc.scalar.copy(dst[:, :share], src[:, :share])
-                    nc.vector.tensor_copy(dst[:, share:], src[:, share:])
-            if b == 0:
-                for t in range(PACK):
-                    nc.vector.quantize_mx(
-                        out=first_codes[t][:, a, :].bitcast(E4M3),
-                        scales=w1_planes[:, b, a, t, :],
-                        in_=dealt[:, t, :, :].rearrange("p m j -> p (m j)"),
-                    )
-            else:
-                together = PACK // (a + 1)
-                for t0 in range(0, PACK, together):
-                    rows = slice(t0, t0 + together)
-                    nc.vector.quantize_mx(
-                        out=second_codes[:, a, rows, :].rearrange("p t m -> p (t m)").bitcast(E4M3),
-                        scales=w1_planes[:, b, a, rows, :].rearrange("p t m -> p (t m)"),
-                        in_=dealt[:, rows, :, :].rearrange("p t m j -> p (t m j)"),
-                    )
+                copy(dst, src)
+            for t0 in range(0, PACK, together):
+                codes = kept([P, together, P], U32, "w1_codes%d%d%d" % (b, a, t0))
+                rows = slice(t0, t0 + together)
+                nc.vector.quantize_mx(
+                    out=codes[:].rearrange("p t m -> p (t m)").bitcast(E4M3),
+                    scales=w1_planes[:, b, a, rows, :].rearrange("p t m -> p (t m)"),
+                    in_=dealt[:, rows, :, :].rearrange("p t m j -> p (t m j)"),
+                )
+                for u in range(together):
+                    w1_codes[(b, a, t0 + u)] = codes[:, u, :]
 
-        def first_product(acc, b, t, half):
-            cols = slice(half * BANK, (half + 1) * BANK)
-            for a in range(SPANS):
-                codes = first_codes[t][:, a, :] if b == 0 else second_codes[:, a, t, :]
+        halves = range(S // BANK)
+
+        def first_pass(accs, b, a):
+            for t, half in product(range(PACK), halves):
+                cols = slice(half * BANK, (half + 1) * BANK)
                 nc.tensor.matmul_mx(
-                    out=acc[:],
-                    lhsT=codes.bitcast(E4M3),
+                    out=accs[(t, half)][:],
+                    lhsT=w1_codes[(b, a, t)].bitcast(E4M3),
                     lhsT_scale=w1_planes[:, b, a, t, :],
                     rhs=picked[a][:, cols].bitcast(E4M3),
                     rhs_scale=picked_planes[4 * a : P, cols],
@@ -135,89 +123,69 @@ def tile_list_malware_pair_family_kernel(
                     stop=(a == SPANS - 1),
                 )
 
-        halves = range(S // BANK)
-        accs = {(t, half): bank(2 * t + half, [P, BANK], "acc_a") for t in range(PACK) for half in halves}
-        quantise_w1(0, 0)
+        accs = [
+            {(t, half): bank(2 * t + half, [P, BANK], "acc%d" % b) for t in range(PACK) for half in halves} for b in range(SPANS)
+        ]
+        quantise_w1(0, 0, [nc.scalar.copy], PACK)
+        first_pass(accs[0], 0, 0)
         w4_dealt_planes = kept([P, SPANS * N], U8, "w4_dealt_planes")
         nc.vector.tensor_copy(
             w4_dealt_planes[:].rearrange("p (x t c i) -> p x c t i", x=SPANS * SPANS, t=PACK, i=LINE),
             w4_planes[:].rearrange("p (x c i t) -> p x c t i", x=SPANS * SPANS, t=PACK, i=LINE),
         )
-        picked.append(kept([P, S], U32, "picked1", tag="w4_planes"))
         nc.vector.tensor_copy(picked[1][:], table[1][:].bitcast(U32).indirect(offs_sb[:]))
-        quantise_w1(0, 1)
-        w4_codes = kept([P, SPANS, 2 * N], U8, "w4_codes")
-        nc.vector.tensor_copy(
-            w4_codes[:].rearrange("p a c -> p (a c)").bitcast(U16).rearrange("p (x t c i) -> p x c t i", x=SPANS * SPANS, t=PACK, i=LINE // 2),
-            w4_raw[:].rearrange("p a c -> p (a c)").bitcast(U16).rearrange("p (x c i t) -> p x c t i", x=SPANS * SPANS, t=PACK, i=LINE // 2),
-        )
-        for t, half in product(range(PACK), halves):
-            first_product(accs[(t, half)], 0, t, half)
+        quantise_w1(0, 1, [nc.scalar.copy, nc.vector.tensor_copy], 1)
+        first_pass(accs[0], 0, 1)
 
         h = {}
-        for t in range(PACK):
-            h[(0, t)] = kept([P, S], F32, "h0%d" % t, tag="h0%d" % t if t < SPANS else "w1_raw1%d_0" % (PACK - 1 - t))
-            for half in halves:
-                nc.scalar.activation(h[(0, t)][:, half * BANK : (half + 1) * BANK], accs[(t, half)][:], ACT.Sigmoid)
-            if t == SPANS - 1:
-                for a in range(SPANS):
-                    quantise_w1(1, a)
+        first_sample = [kept([P, PACK, PAIRS], F32, "first_sample%d" % b, tag="table1" if b else "dealt11") for b in range(SPANS)]
 
+        def sigmoids(b):
+            for t in range(PACK):
+                h[(b, t)] = kept([P, S], F32, "h%d%d" % (b, t))
+                for half in halves:
+                    nc.scalar.activation(h[(b, t)][:, half * BANK : (half + 1) * BANK], accs[b][(t, half)][:], ACT.Sigmoid)
+
+        def pick_first(b):
+            for t in range(PACK):
+                nc.vector.tensor_copy(first_sample[b][:, t, :], h[(b, t)][:].indirect(pos1_sb[:]))
+
+        sigmoids(0)
+        quantise_w1(1, 0, [nc.vector.tensor_copy], PACK)
+        first_pass(accs[1], 1, 0)
+        quantise_w1(1, 1, [nc.vector.tensor_copy, nc.vector.tensor_copy], 2)
+        first_pass(accs[1], 1, 1)
+        pick_first(0)
         inv_gain = kept([P, SPANS, PACK], F32, "inv_gain")
         nc.vector.reciprocal(inv_gain[:], gain[:])
+        sigmoids(1)
+        pick_first(1)
 
-        for t in range(PACK):
-            h[(1, t)] = kept([P, S], F32, "h1%d" % t)
-            for half in halves:
-                acc = bank(2 * t + half, [P, BANK], "acc_b")
-                first_product(acc, 1, t, half)
-                nc.scalar.activation(h[(1, t)][:, half * BANK : (half + 1) * BANK], acc[:], ACT.Sigmoid)
-
+        units = [(0, 0, 256), (1, 0, 256), (0, 256, 256), (1, 256, 128), (1, 384, 128)]
+        slots = ["picked1", "w1_raw10_0", "picked_planes", "w1_raw01_256", "w1_raw11_0"]
+        inverse, ratio, root, rounded_z = {}, {}, {}, {}
         z_codes = {}
         z_planes = kept([P, SPANS, PAIRS], U8, "z_planes")
 
-        def pick(b, j0, width, tags):
-            smaller = kept([P, PACK, width], F32, "smaller%d_%d" % (b, j0))
+        def root_first(n):
+            b, j0, width = units[n]
+            inverse[n] = kept([P, PACK, width], F32, "inverse%d" % n, tag=slots[n])
+            nc.scalar.activation(inverse[n][:], first_sample[b][:, :, j0 : j0 + width], ACT.Abs_reciprocal_sqrt)
+
+        def invert_and_pick(n):
+            b, j0, width = units[n]
+            nc.scalar.activation(inverse[n][:], inverse[n][:], ACT.Square)
+            ratio[n] = kept([P, PACK, width], F32, "ratio%d" % n)
             cols = slice(j0 // PER_COLUMN, (j0 + width) // PER_COLUMN)
-            together = PACK // len(tags)
-            larger = []
-            for n, (pair_tag, larger_tag) in enumerate(tags):
-                pair = kept([P, 2, together, width], F32, "pair", tag=pair_tag)
-                for u in range(together):
-                    window = h[(b, n * together + u)]
-                    nc.vector.tensor_copy(pair[:, 0, u, :], window[:].indirect(pos1_sb[:, cols]))
-                    nc.vector.tensor_copy(pair[:, 1, u, :], window[:].indirect(pos2_sb[:, cols]))
-                most = kept([P, together, width], F32, "larger", tag=larger_tag)
-                nc.vector.tensor_tensor(most[:], pair[:, 0, :, :], pair[:, 1, :, :], ALU.max)
-                nc.vector.tensor_tensor(
-                    smaller[:, n * together : (n + 1) * together, :], pair[:, 0, :, :], pair[:, 1, :, :], ALU.min
-                )
-                larger.extend(most[:, u, :] for u in range(together))
-            return larger, smaller
+            for t in range(PACK):
+                nc.vector.tensor_tensor(ratio[n][:, t, :], h[(b, t)][:].indirect(pos2_sb[:, cols]), inverse[n][:, t, :], ALU.mult)
 
-        def invert(b, width, larger, tag):
-            inverse = kept([P, PACK, width], F32, "inverse", tag=tag)
-            together = PAIRS // width
-            for t0 in range(0, PACK, together):
-                for t in range(t0, t0 + together):
-                    nc.scalar.activation(inverse[:, t, :], larger[t], ACT.Abs_reciprocal_sqrt, scale=inv_gain[:, b, t : t + 1])
-                nc.scalar.activation(inverse[:, t0 : t0 + together, :], inverse[:, t0 : t0 + together, :], ACT.Square)
-            return inverse
-
-        def agree(b, j0, width, smaller, inverse, tag):
-            z = kept([P, width, PACK], BF16, "z", tag=tag)
-            codes = kept([P, width], U32, "z_codes%d_%d" % (b, j0))
-            nc.vector.tensor_tensor(
-                z[:].rearrange("p (c i) t -> p c t i", i=LINE // 4),
-                smaller.rearrange("p t (c i) -> p c t i", i=LINE // 4),
-                inverse.rearrange("p t (c i) -> p c t i", i=LINE // 4),
-                ALU.mult,
-            )
-            nc.vector.quantize_mx(
-                out=codes[:].bitcast(E4M3), scales=z_planes[:, b, j0 : j0 + width], in_=z[:].rearrange("p j t -> p (j t)")
-            )
-            for c0 in range(0, width, CHUNK):
-                z_codes[(b, j0 + c0)] = codes[:, c0 : c0 + CHUNK]
+        def fold(n):
+            b, j0, width = units[n]
+            root[n] = kept([P, PACK, width], F32, "root%d" % n)
+            for t in range(PACK):
+                nc.scalar.activation(root[n][:, t, :], ratio[n][:, t, :], ACT.Abs_reciprocal_sqrt, scale=inv_gain[:, b, t : t + 1])
+            nc.vector.scalar_tensor_tensor(root[n][:], ratio[n][:], 1.0, root[n][:], ALU.min, ALU.mult)
 
         def second_pass(a, j0):
             for grp, t in product(range(SPANS), range(PACK)):
@@ -232,59 +200,84 @@ def tile_list_malware_pair_family_kernel(
                     stop=(a == SPANS - 1 and t == PACK - 1),
                 )
 
+        def agree(n):
+            b, j0, width = units[n]
+            z = kept([P, width, PACK], BF16, "z%d" % n)
+            nc.scalar.activation(
+                z[:].rearrange("p (c i) t -> p c t i", i=LINE // 4),
+                root[n][:].rearrange("p t (c i) -> p c t i", i=LINE // 4),
+                ACT.Square,
+            )
+            codes = kept([P, width], U32, "z_codes%d" % n)
+            nc.vector.quantize_mx(
+                out=codes[:].bitcast(E4M3), scales=z_planes[:, b, j0 : j0 + width], in_=z[:].rearrange("p j t -> p (j t)")
+            )
+            for c0 in range(0, width, CHUNK):
+                z_codes[(b, j0 + c0)] = codes[:, c0 : c0 + CHUNK]
+                second_pass(b, j0 + c0)
+
         y_planes = kept([P, SPANS, PAIRS], U8, "y_planes")
 
-        def hand_out(j0, last):
-            y_codes = ring.tile([P, SPANS, CHUNK], I32, name="y_codes", align_bytes=64)
-            for step in range(SPANS):
-                y = ring.tile([P, PACK, CHUNK], F32, name="y", tag="y%d" % step)
-                nc.scalar.copy(y[:], sums[j0][step][:])
-                nc.sync.dma_start(
-                    out_0[SPAN * step : SPAN * (step + 1), j0 : j0 + CHUNK].rearrange("(p t) j -> p t j", t=PACK), y[:]
-                )
-                grp = SPANS - 1 - step if last else step
-                rounded = ring.tile([P, CHUNK, PACK], BF16, name="rounded", tag="rounded%d" % grp, align_bytes=64)
-                dst = rounded[:].rearrange("p (c i) t -> p c t i", i=LINE // 4)
-                src = sums[j0][grp][:].rearrange("p t (c i) -> p c t i", i=LINE // 4)
-                if last:
-                    nc.vector.tensor_copy(dst, src)
-                else:
-                    nc.scalar.copy(dst, src)
-                nc.vector.quantize_mx(
-                    out=y_codes[:, grp, :].bitcast(E4M3),
-                    scales=y_planes[:, grp, j0 : j0 + CHUNK],
-                    in_=rounded[:].rearrange("p j t -> p (j t)"),
-                )
-            queue = nc.scalar if last else nc.sync
-            queue.dma_start(out_1[:, :, j0 : j0 + CHUNK, :].rearrange("g p m i -> p g (m i)").bitcast(I32), y_codes[:])
+        def hand_out(j0, width, grp, y_codes, src=None):
+            y = kept([P, PACK, width], F32, "y%d_%d" % (j0, grp))
+            for c0 in range(0, width, CHUNK):
+                nc.scalar.copy(y[:, :, c0 : c0 + CHUNK], sums[j0 + c0][grp][:])
+            nc.sync.dma_start(
+                out_0[SPAN * grp : SPAN * (grp + 1), j0 : j0 + width].rearrange("(p t) j -> p t j", t=PACK), y[:]
+            )
+            if src is None:
+                requantise(j0, width, grp, y_codes, y)
+            return y
 
-        first, second, third, fourth = range(0, PAIRS, CHUNK)
-        larger_a, smaller_a = pick(0, first, PAIRS, (("w4_raw", "stage1"), ("stage0", "larger_a")))
-        inverse_a = invert(0, PAIRS, larger_a, "codes_then_inverse")
-        larger_b, smaller_b = pick(1, first, third, (("w4_raw", "larger_b"),))
-        inverse_b = invert(1, third, larger_b, "larger_a")
+        def requantise(j0, width, grp, y_codes, src):
+            rounded = kept([P, width, PACK], BF16, "rounded%d_%d" % (j0, grp))
+            nc.vector.tensor_copy(
+                rounded[:].rearrange("p (c i) t -> p c t i", i=LINE // 4),
+                src[:].rearrange("p t (c i) -> p c t i", i=LINE // 4),
+            )
+            nc.vector.quantize_mx(
+                out=y_codes[:, grp, :].bitcast(E4M3),
+                scales=y_planes[:, grp, j0 : j0 + width],
+                in_=rounded[:].rearrange("p j t -> p (j t)"),
+            )
+
+        def store_codes(j0, width, y_codes, queue):
+            queue.dma_start(out_1[:, :, j0 : j0 + width, :].rearrange("g p m i -> p g (m i)").bitcast(I32), y_codes[:])
+
         sums = {
             j0: [bank(SPANS * (j0 // CHUNK) + grp, [P, PACK, CHUNK], "sums") for grp in range(SPANS)]
-            for j0 in (first, second, third, fourth)
+            for j0 in range(0, PAIRS, CHUNK)
         }
-        agree(0, first, third, smaller_a[:, :, first:third], inverse_a[:, :, first:third], "z_a")
-        agree(1, first, third, smaller_b[:], inverse_b[:], "z_b")
-        for j0, a in product((first, second), range(SPANS)):
-            second_pass(a, j0)
-        hand_out(first, False)
-        larger_c, smaller_c = pick(1, third, CHUNK, (("smaller1_0", "larger_c"),))
-        inverse_c = invert(1, CHUNK, larger_c, "z_codes1_0")
-        agree(0, third, PAIRS - third, smaller_a[:, :, third:PAIRS], inverse_a[:, :, third:PAIRS], "smaller1_0")
-        for j0 in (third, fourth):
-            second_pass(0, j0)
-        hand_out(second, False)
-        larger_d, smaller_d = pick(1, fourth, CHUNK, (("z_b", "larger_d"),))
-        inverse_d = invert(1, CHUNK, larger_d, "inverse_d")
-        for j0, smaller, inverse in ((third, smaller_c, inverse_c), (fourth, smaller_d, inverse_d)):
-            agree(1, j0, CHUNK, smaller[:], inverse[:], "z_late%d" % j0)
-            second_pass(1, j0)
-        for j0 in (third, fourth):
-            hand_out(j0, j0 == fourth)
+        for n in range(2):
+            root_first(n)
+            invert_and_pick(n)
+        w4_codes = kept([P, SPANS, 2 * N], U8, "w4_codes", tag=slots[0])
+        nc.vector.tensor_copy(
+            w4_codes[:].rearrange("p a c -> p (a c)").bitcast(U16).rearrange("p (x t c i) -> p x c t i", x=SPANS * SPANS, t=PACK, i=LINE // 2),
+            w4_raw[:].rearrange("p a c -> p (a c)").bitcast(U16).rearrange("p (x c i t) -> p x c t i", x=SPANS * SPANS, t=PACK, i=LINE // 2),
+        )
+        y_codes = {j0: kept([P, SPANS, width], I32, "y_codes%d" % j0) for b, j0, width in units if b}
+        for n in range(len(units)):
+            if n + 2 < len(units):
+                root_first(n + 2)
+            fold(n)
+            if n + 2 < len(units):
+                invert_and_pick(n + 2)
+            if n > 0:
+                agree(n - 1)
+            if n >= 3:
+                hand_out(0, 2 * CHUNK, n - 3, y_codes[0])
+        store_codes(0, 2 * CHUNK, y_codes[0], nc.sync)
+        agree(len(units) - 1)
+        for grp in range(SPANS):
+            hand_out(2 * CHUNK, CHUNK, grp, y_codes[2 * CHUNK])
+        store_codes(2 * CHUNK, CHUNK, y_codes[2 * CHUNK], nc.sync)
+        last = 3 * CHUNK
+        y_first = hand_out(last, CHUNK, 0, y_codes[last], True)
+        requantise(last, CHUNK, 1, y_codes[last], sums[last][1])
+        hand_out(last, CHUNK, 1, y_codes[last], True)
+        requantise(last, CHUNK, 0, y_codes[last], y_first)
+        store_codes(last, CHUNK, y_codes[last], nc.scalar)
         for q in range(QUADS):
             queue = nc.scalar if q % 2 else nc.sync
             queue.dma_start(

@@ -34,6 +34,7 @@ def tile_list_malware_pair_family_kernel(
     nc = tc.nc
     with ExitStack() as ctx:
         keep = ctx.enter_context(tc.tile_pool(name="keep", bufs=1))
+        stage = ctx.enter_context(tc.tile_pool(name="stage", bufs=1))
         psum = ctx.enter_context(tc.psum_pool(name="psum", bufs=1))
 
         def kept(shape, dtype, name, tag=None):
@@ -46,47 +47,44 @@ def tile_list_malware_pair_family_kernel(
         pos1_sb = keep.tile([P, PAIRS // PER_COLUMN], U16, name="pos1_sb")
         pos2_sb = keep.tile([P, PAIRS // PER_COLUMN], U16, name="pos2_sb")
 
-        tab_planes = kept([P, T], U8, "tab_planes")
-        nc.vector.memset(tab_planes[:].bitcast(I32), 0)
-        w4_planes = kept([P, SPANS * N], U8, "w4_planes")
-        nc.vector.memset(w4_planes[:].bitcast(I32), 0)
+        tab_rows = kept([P, SPANS, T], U8, "tab_rows")
+        nc.vector.memset(tab_rows[:].rearrange("p a t -> p (a t)").bitcast(I32), 0)
+        picked_planes = kept([P, SPANS, S], U8, "picked_planes")
+        nc.vector.memset(picked_planes[:].rearrange("p a s -> p (a s)").bitcast(I32), 0)
 
-        nc.sync.dma_start(offs_sb[:], offs)
-        table = [kept([P, T], I32, "table%d" % a) for a in range(SPANS)]
-        table_hbm = [tab_words[a].rearrange("p t i -> p (t i)").bitcast(I32) for a in range(SPANS)]
-        nc.sync.dma_start(table[0][:], table_hbm[0])
-        for q in range(QUADS):
-            nc.gpsimd.dma_start(
-                tab_planes[32 * q : 32 * q + 4 * SPANS, :].bitcast(I32), tab_scales[:, 4 * q : 4 * q + 4, :].bitcast(I32)
-            )
-        for q in range(QUADS):
-            nc.sync.dma_start(
-                w4_planes[32 * q : 32 * q + 4, :].rearrange("r (a c) -> r a c", a=SPANS).bitcast(I32),
-                w4_scales[:, 4 * q : 4 * q + 4, :].rearrange("a r c -> r a c").bitcast(I32),
-            )
-
-        def load_w1(b, a, c0, width):
-            piece = kept([P, PACK, width], F32, "w1_raw%d%d_%d" % (b, a, c0))
+        def load_w1(pool_tile, b, a, c0, width):
+            piece = pool_tile([P, PACK, width], F32, "w1_raw%d%d_%d" % (b, a, c0))
             cols = slice(SPAN * b + c0, SPAN * b + c0 + width)
             nc.sync.dma_start(piece[:], w1[SPAN * a : SPAN * (a + 1), cols].rearrange("(p j) c -> p j c", j=PACK))
             return piece, c0, width
 
-        raw = {(0, 0): [load_w1(0, 0, 0, SPAN)]}
-        nc.sync.dma_start(table[1][:], table_hbm[1])
-        raw[(0, 1)] = [load_w1(0, 1, c0, SPAN // 2) for c0 in (0, SPAN // 2)]
-        nc.sync.dma_start(pos1_sb[:], pos1)
-        raw[(1, 0)] = [load_w1(1, 0, 0, SPAN)]
-        raw[(1, 1)] = [load_w1(1, 1, c0, SPAN // 2) for c0 in (0, SPAN // 2)]
-        nc.sync.dma_start(pos2_sb[:], pos2)
-        gain = kept([P, SPANS, PACK], F32, "gain")
-        nc.sync.dma_start(gain[:], g.rearrange("(b p t) -> p b t", b=SPANS, t=PACK))
-        w4_raw = kept([P, SPANS, 2 * N], U8, "w4_raw")
-        nc.sync.dma_start(w4_raw[:].bitcast(I32), w4_words.rearrange("a p c -> p a c").bitcast(I32))
+        def over_table(offset):
+            return lambda shape, dtype, name: stage.tile(shape, dtype, name=name, tag=name, offset=offset)
 
+        nc.sync.dma_start(offs_sb[:], offs)
+        table = [over_table(0)([P, T], I32, "table0"), kept([P, T], I32, "table1")]
+        table_hbm = [tab_words[a].rearrange("p t i -> p (t i)").bitcast(I32) for a in range(SPANS)]
+        nc.sync.dma_start(table[0][:], table_hbm[0])
+        nc.scalar.dma_start(tab_rows[0:P:8, :, :].bitcast(I32), tab_scales.rearrange("a q t -> q a t").bitcast(I32))
+        raw = {(0, 0): [load_w1(kept, 0, 0, 0, SPAN)]}
+        nc.sync.dma_start(pos1_sb[:], pos1)
+        nc.sync.dma_start(pos2_sb[:], pos2)
+        nc.sync.dma_start(table[1][:], table_hbm[1])
+        raw[(0, 1)] = [load_w1(kept, 0, 1, c0, SPAN // 2) for c0 in (0, SPAN // 2)]
+
+        picked_rows = kept([P, SPANS, S], U8, "picked_rows")
+        for a in range(SPANS):
+            nc.vector.tensor_copy(picked_rows[:, a, :], tab_rows[:, a, :].indirect(offs_sb[:]))
+        for q in range(QUADS):
+            nc.scalar.dma_start(
+                picked_planes[32 * q : 32 * q + 4, :, :].rearrange("p a s -> p (a s)").bitcast(I32),
+                picked_rows[32 * q : 32 * q + 32 : 8, :, :].rearrange("p a s -> p (a s)").bitcast(I32),
+            )
         picked = [kept([P, S], U32, "picked%d" % a) for a in range(SPANS)]
-        picked_planes = kept([P, S], U8, "picked_planes")
         nc.vector.tensor_copy(picked[0][:], table[0][:].bitcast(U32).indirect(offs_sb[:]))
-        nc.vector.tensor_copy(picked_planes[:], tab_planes[:].indirect(offs_sb[:]))
+
+        raw[(1, 0)] = [load_w1(over_table(0), 1, 0, 0, SPAN)]
+        raw[(1, 1)] = [load_w1(over_table(8192 + 16 * c0), 1, 1, c0, SPAN // 2) for c0 in (0, SPAN // 2)]
 
         w1_codes = {}
         w1_planes = kept([P, SPANS, SPANS, PACK, P], U8, "w1_planes")
@@ -118,7 +116,7 @@ def tile_list_malware_pair_family_kernel(
                     lhsT=w1_codes[(b, a, t)].bitcast(E4M3),
                     lhsT_scale=w1_planes[:, b, a, t, :],
                     rhs=picked[a][:, cols].bitcast(E4M3),
-                    rhs_scale=picked_planes[4 * a : P, cols],
+                    rhs_scale=picked_planes[:, a, cols],
                     start=(a == 0),
                     stop=(a == SPANS - 1),
                 )
@@ -128,11 +126,10 @@ def tile_list_malware_pair_family_kernel(
         ]
         quantise_w1(0, 0, [nc.scalar.copy], PACK)
         first_pass(accs[0], 0, 0)
-        w4_dealt_planes = kept([P, SPANS * N], U8, "w4_dealt_planes")
-        nc.vector.tensor_copy(
-            w4_dealt_planes[:].rearrange("p (x t c i) -> p x c t i", x=SPANS * SPANS, t=PACK, i=LINE),
-            w4_planes[:].rearrange("p (x c i t) -> p x c t i", x=SPANS * SPANS, t=PACK, i=LINE),
-        )
+        w4_raw = kept([P, SPANS, 2 * N], U8, "w4_raw", tag="w1_raw00_0")
+        nc.sync.dma_start(w4_raw[:].bitcast(I32), w4_words.rearrange("a p c -> p a c").bitcast(I32))
+        gain = kept([P, SPANS, PACK], F32, "gain", tag="dealt00")
+        nc.sync.dma_start(gain[:], g.rearrange("(b p t) -> p b t", b=SPANS, t=PACK))
         nc.vector.tensor_copy(picked[1][:], table[1][:].bitcast(U32).indirect(offs_sb[:]))
         quantise_w1(0, 1, [nc.scalar.copy, nc.vector.tensor_copy], 1)
         first_pass(accs[0], 0, 1)
@@ -155,6 +152,13 @@ def tile_list_malware_pair_family_kernel(
         first_pass(accs[1], 1, 0)
         quantise_w1(1, 1, [nc.vector.tensor_copy, nc.vector.tensor_copy], 2)
         first_pass(accs[1], 1, 1)
+        w4_planes = kept([P, SPANS * N], U8, "w4_planes", tag="dealt10")
+        nc.vector.memset(w4_planes[:].bitcast(I32), 0)
+        for q in range(QUADS):
+            nc.sync.dma_start(
+                w4_planes[32 * q : 32 * q + 4, :].rearrange("r (a c) -> r a c", a=SPANS).bitcast(I32),
+                w4_scales[:, 4 * q : 4 * q + 4, :].rearrange("a r c -> r a c").bitcast(I32),
+            )
         pick_first(0)
         inv_gain = kept([P, SPANS, PACK], F32, "inv_gain")
         nc.vector.reciprocal(inv_gain[:], gain[:])
@@ -162,7 +166,7 @@ def tile_list_malware_pair_family_kernel(
         pick_first(1)
 
         units = [(0, 0, 256), (1, 0, 256), (0, 256, 256), (1, 256, 128), (1, 384, 128)]
-        slots = ["picked1", "w1_raw10_0", "picked_planes", "w1_raw01_256", "w1_raw11_0"]
+        slots = ["picked1", "tab_rows", "picked_planes", "w1_raw01_256", "w1_raw01_0"]
         inverse, ratio, root, rounded_z = {}, {}, {}, {}
         z_codes = {}
         z_planes = kept([P, SPANS, PAIRS], U8, "z_planes")
@@ -255,6 +259,11 @@ def tile_list_malware_pair_family_kernel(
         nc.vector.tensor_copy(
             w4_codes[:].rearrange("p a c -> p (a c)").bitcast(U16).rearrange("p (x t c i) -> p x c t i", x=SPANS * SPANS, t=PACK, i=LINE // 2),
             w4_raw[:].rearrange("p a c -> p (a c)").bitcast(U16).rearrange("p (x c i t) -> p x c t i", x=SPANS * SPANS, t=PACK, i=LINE // 2),
+        )
+        w4_dealt_planes = kept([P, SPANS * N], U8, "w4_dealt_planes", tag=slots[1])
+        nc.vector.tensor_copy(
+            w4_dealt_planes[:].rearrange("p (x t c i) -> p x c t i", x=SPANS * SPANS, t=PACK, i=LINE),
+            w4_planes[:].rearrange("p (x c i t) -> p x c t i", x=SPANS * SPANS, t=PACK, i=LINE),
         )
         y_codes = {j0: kept([P, SPANS, width], I32, "y_codes%d" % j0) for b, j0, width in units if b}
         for n in range(len(units)):

@@ -47,10 +47,17 @@ def tile_list_malware_pair_family_kernel(
         pos1_sb = keep.tile([P, PAIRS // PER_COLUMN], U16, name="pos1_sb")
         pos2_sb = keep.tile([P, PAIRS // PER_COLUMN], U16, name="pos2_sb")
 
-        tab_rows = kept([P, SPANS, T], U8, "tab_rows")
+        def over_table(offset):
+            return lambda shape, dtype, name: stage.tile(shape, dtype, name=name, tag=name, offset=offset)
+
+        tab_rows = over_table(16384)([P, SPANS, T], U8, "tab_rows")
         nc.vector.memset(tab_rows[:].rearrange("p a t -> p (a t)").bitcast(I32), 0)
         picked_planes = kept([P, SPANS, S], U8, "picked_planes")
         nc.vector.memset(picked_planes[:].rearrange("p a s -> p (a s)").bitcast(I32), 0)
+        w4_rows = kept([P, SPANS, N], U8, "w4_rows")
+        nc.vector.memset(w4_rows[:].rearrange("p a c -> p (a c)").bitcast(I32), 0)
+        w4_planes = kept([P, SPANS * N], U8, "w4_planes")
+        nc.vector.memset(w4_planes[:].bitcast(I32), 0)
 
         def load_w1(pool_tile, b, a, c0, width):
             piece = pool_tile([P, PACK, width], F32, "w1_raw%d%d_%d" % (b, a, c0))
@@ -58,28 +65,30 @@ def tile_list_malware_pair_family_kernel(
             nc.sync.dma_start(piece[:], w1[SPAN * a : SPAN * (a + 1), cols].rearrange("(p j) c -> p j c", j=PACK))
             return piece, c0, width
 
-        def over_table(offset):
-            return lambda shape, dtype, name: stage.tile(shape, dtype, name=name, tag=name, offset=offset)
-
         nc.sync.dma_start(offs_sb[:], offs)
-        table = [over_table(0)([P, T], I32, "table0"), kept([P, T], I32, "table1")]
+        table = [over_table(0)([P, T], I32, "table0"), None]
         table_hbm = [tab_words[a].rearrange("p t i -> p (t i)").bitcast(I32) for a in range(SPANS)]
-        nc.sync.dma_start(table[0][:], table_hbm[0])
-        nc.scalar.dma_start(tab_rows[0:P:8, :, :].bitcast(I32), tab_scales.rearrange("a q t -> q a t").bitcast(I32))
-        raw = {(0, 0): [load_w1(kept, 0, 0, 0, SPAN)]}
+        nc.sync.dma_start(table[0][:, : T // 2], table_hbm[0][:, : T // 2])
         nc.sync.dma_start(pos1_sb[:], pos1)
         nc.sync.dma_start(pos2_sb[:], pos2)
-        nc.sync.dma_start(table[1][:], table_hbm[1])
-        raw[(0, 1)] = [load_w1(kept, 0, 1, c0, SPAN // 2) for c0 in (0, SPAN // 2)]
+        nc.sync.dma_start(tab_rows[0:P:8, :, :].bitcast(I32), tab_scales.rearrange("a q t -> q a t").bitcast(I32))
+        nc.sync.dma_start(table[0][:, T // 2 :], table_hbm[0][:, T // 2 :])
+        raw = {(0, 0): [load_w1(kept, 0, 0, 0, SPAN)]}
+        raw[(0, 1)] = [load_w1(kept, 0, 1, 0, SPAN)]
+        w4_raw = kept([P, SPANS, 2 * N], U8, "w4_raw")
+        nc.sync.dma_start(w4_raw[:].bitcast(I32), w4_words.rearrange("a p c -> p a c").bitcast(I32))
+        nc.sync.dma_start(w4_rows[0:P:8, :, :].bitcast(I32), w4_scales.rearrange("a q c -> q a c").bitcast(I32))
 
         picked_rows = kept([P, SPANS, S], U8, "picked_rows")
         for a in range(SPANS):
             nc.vector.tensor_copy(picked_rows[:, a, :], tab_rows[:, a, :].indirect(offs_sb[:]))
         for q in range(QUADS):
-            nc.scalar.dma_start(
+            nc.sync.dma_start(
                 picked_planes[32 * q : 32 * q + 4, :, :].rearrange("p a s -> p (a s)").bitcast(I32),
                 picked_rows[32 * q : 32 * q + 32 : 8, :, :].rearrange("p a s -> p (a s)").bitcast(I32),
             )
+        table[1] = over_table(16384)([P, T], I32, "table1")
+        nc.sync.dma_start(table[1][:], table_hbm[1])
         picked = [kept([P, S], U32, "picked%d" % a) for a in range(SPANS)]
         nc.vector.tensor_copy(picked[0][:], table[0][:].bitcast(U32).indirect(offs_sb[:]))
 
@@ -108,8 +117,8 @@ def tile_list_malware_pair_family_kernel(
 
         halves = range(S // BANK)
 
-        def first_pass(accs, b, a):
-            for t, half in product(range(PACK), halves):
+        def first_pass(accs, b, a, order):
+            for t, half in order:
                 cols = slice(half * BANK, (half + 1) * BANK)
                 nc.tensor.matmul_mx(
                     out=accs[(t, half)][:],
@@ -121,52 +130,61 @@ def tile_list_malware_pair_family_kernel(
                     stop=(a == SPANS - 1),
                 )
 
+        by_slice = list(product(range(PACK), halves))
+        by_half = [(t, half) for half, t in product(halves, range(PACK))]
         accs = [
             {(t, half): bank(2 * t + half, [P, BANK], "acc%d" % b) for t in range(PACK) for half in halves} for b in range(SPANS)
         ]
         quantise_w1(0, 0, [nc.scalar.copy], PACK)
-        first_pass(accs[0], 0, 0)
-        w4_raw = kept([P, SPANS, 2 * N], U8, "w4_raw", tag="w1_raw00_0")
-        nc.sync.dma_start(w4_raw[:].bitcast(I32), w4_words.rearrange("a p c -> p a c").bitcast(I32))
+        first_pass(accs[0], 0, 0, by_half)
         gain = kept([P, SPANS, PACK], F32, "gain", tag="dealt00")
         nc.sync.dma_start(gain[:], g.rearrange("(b p t) -> p b t", b=SPANS, t=PACK))
-        nc.vector.tensor_copy(picked[1][:], table[1][:].bitcast(U32).indirect(offs_sb[:]))
-        quantise_w1(0, 1, [nc.scalar.copy, nc.vector.tensor_copy], 1)
-        first_pass(accs[0], 0, 1)
+        w4_codes = kept([P, SPANS, 2 * N], U8, "w4_codes")
+        nc.vector.tensor_copy(
+            w4_codes[:].rearrange("p a c -> p (a c)").bitcast(U16).rearrange("p (x t c i) -> p x c t i", x=SPANS * SPANS, t=PACK, i=LINE // 2),
+            w4_raw[:].rearrange("p a c -> p (a c)").bitcast(U16).rearrange("p (x c i t) -> p x c t i", x=SPANS * SPANS, t=PACK, i=LINE // 2),
+        )
+        w4_dealt_rows = kept([P, SPANS * N], U8, "w4_dealt_rows")
+        nc.vector.tensor_copy(
+            w4_dealt_rows[:].rearrange("p (x t c i) -> p x c t i", x=SPANS * SPANS, t=PACK, i=LINE),
+            w4_rows[:].rearrange("p a c -> p (a c)").rearrange("p (x c i t) -> p x c t i", x=SPANS * SPANS, t=PACK, i=LINE),
+        )
+        quantise_w1(0, 1, [nc.scalar.copy], PACK)
+        for half in halves:
+            nc.vector.tensor_copy(
+                picked[1][:, half * BANK : (half + 1) * BANK],
+                table[1][:].bitcast(U32).indirect(offs_sb[:, half * BANK // PER_COLUMN : (half + 1) * BANK // PER_COLUMN]),
+            )
+        first_pass(accs[0], 0, 1, by_half)
 
         h = {}
-        first_sample = [kept([P, PACK, PAIRS], F32, "first_sample%d" % b, tag="table1" if b else "dealt11") for b in range(SPANS)]
+        first_sample = [kept([P, PACK, PAIRS], F32, "first_sample%d" % b, tag="w1_raw01_0" if b else "dealt11") for b in range(SPANS)]
 
-        def sigmoids(b):
+        def sigmoids(b, order):
             for t in range(PACK):
                 h[(b, t)] = kept([P, S], F32, "h%d%d" % (b, t))
-                for half in halves:
-                    nc.scalar.activation(h[(b, t)][:, half * BANK : (half + 1) * BANK], accs[b][(t, half)][:], ACT.Sigmoid)
+            for t, half in order:
+                nc.scalar.activation(h[(b, t)][:, half * BANK : (half + 1) * BANK], accs[b][(t, half)][:], ACT.Sigmoid)
 
         def pick_first(b):
             for t in range(PACK):
                 nc.vector.tensor_copy(first_sample[b][:, t, :], h[(b, t)][:].indirect(pos1_sb[:]))
 
-        sigmoids(0)
+        sigmoids(0, by_half)
         quantise_w1(1, 0, [nc.vector.tensor_copy], PACK)
-        first_pass(accs[1], 1, 0)
+        first_pass(accs[1], 1, 0, by_half)
         quantise_w1(1, 1, [nc.vector.tensor_copy, nc.vector.tensor_copy], 2)
-        first_pass(accs[1], 1, 1)
-        w4_planes = kept([P, SPANS * N], U8, "w4_planes", tag="dealt10")
-        nc.vector.memset(w4_planes[:].bitcast(I32), 0)
+        first_pass(accs[1], 1, 1, by_slice)
         for q in range(QUADS):
-            nc.sync.dma_start(
-                w4_planes[32 * q : 32 * q + 4, :].rearrange("r (a c) -> r a c", a=SPANS).bitcast(I32),
-                w4_scales[:, 4 * q : 4 * q + 4, :].rearrange("a r c -> r a c").bitcast(I32),
-            )
+            nc.sync.dma_start(w4_planes[32 * q : 32 * q + 4, :].bitcast(I32), w4_dealt_rows[32 * q : 32 * q + 32 : 8, :].bitcast(I32))
         pick_first(0)
         inv_gain = kept([P, SPANS, PACK], F32, "inv_gain")
         nc.vector.reciprocal(inv_gain[:], gain[:])
-        sigmoids(1)
+        sigmoids(1, by_slice)
         pick_first(1)
 
         units = [(0, 0, 256), (1, 0, 256), (0, 256, 256), (1, 256, 128), (1, 384, 128)]
-        slots = ["picked1", "tab_rows", "picked_planes", "w1_raw01_256", "w1_raw01_0"]
+        slots = ["picked1", "picked0", "picked_planes", "inverse3", "inverse4"]
         inverse, ratio, root, rounded_z = {}, {}, {}, {}
         z_codes = {}
         z_planes = kept([P, SPANS, PAIRS], U8, "z_planes")
@@ -197,7 +215,7 @@ def tile_list_malware_pair_family_kernel(
                 nc.tensor.matmul_mx(
                     out=sums[j0][grp][:, t, :],
                     lhsT=w4_codes[:, a, 2 * c0 : 2 * (c0 + P)].bitcast(E2M1),
-                    lhsT_scale=w4_dealt_planes[:, a * N + c0 : a * N + c0 + P],
+                    lhsT_scale=w4_planes[:, a * N + c0 : a * N + c0 + P],
                     rhs=z_codes[(a, j0)].bitcast(E4M3),
                     rhs_scale=z_planes[:, a, j0 : j0 + CHUNK],
                     start=(a == 0 and t == 0),
@@ -255,16 +273,6 @@ def tile_list_malware_pair_family_kernel(
         for n in range(2):
             root_first(n)
             invert_and_pick(n)
-        w4_codes = kept([P, SPANS, 2 * N], U8, "w4_codes", tag=slots[0])
-        nc.vector.tensor_copy(
-            w4_codes[:].rearrange("p a c -> p (a c)").bitcast(U16).rearrange("p (x t c i) -> p x c t i", x=SPANS * SPANS, t=PACK, i=LINE // 2),
-            w4_raw[:].rearrange("p a c -> p (a c)").bitcast(U16).rearrange("p (x c i t) -> p x c t i", x=SPANS * SPANS, t=PACK, i=LINE // 2),
-        )
-        w4_dealt_planes = kept([P, SPANS * N], U8, "w4_dealt_planes", tag=slots[1])
-        nc.vector.tensor_copy(
-            w4_dealt_planes[:].rearrange("p (x t c i) -> p x c t i", x=SPANS * SPANS, t=PACK, i=LINE),
-            w4_planes[:].rearrange("p (x c i t) -> p x c t i", x=SPANS * SPANS, t=PACK, i=LINE),
-        )
         y_codes = {j0: kept([P, SPANS, width], I32, "y_codes%d" % j0) for b, j0, width in units if b}
         for n in range(len(units)):
             if n + 2 < len(units):

@@ -63,7 +63,7 @@ def tile_list_malware_pair_family_kernel(
             piece = pool_tile([P, PACK, width], F32, "w1_raw%d%d_%d" % (b, a, c0))
             cols = slice(SPAN * b + c0, SPAN * b + c0 + width)
             nc.sync.dma_start(piece[:], w1[SPAN * a : SPAN * (a + 1), cols].rearrange("(p j) c -> p j c", j=PACK))
-            return piece, c0, width
+            return piece[:], c0, width
 
         nc.sync.dma_start(offs_sb[:], offs)
         table = [over_table(0)([P, T], I32, "table0"), None]
@@ -73,10 +73,10 @@ def tile_list_malware_pair_family_kernel(
         nc.sync.dma_start(pos2_sb[:], pos2)
         nc.sync.dma_start(tab_rows[0:P:8, :, :].bitcast(I32), tab_scales.rearrange("a q t -> q a t").bitcast(I32))
         nc.sync.dma_start(table[0][:, T // 2 :], table_hbm[0][:, T // 2 :])
-        raw = {(0, 0): [load_w1(kept, 0, 0, 0, SPAN)]}
+        whole_rows = kept([P, PACK, H], F32, "w1_whole_rows")
+        nc.sync.dma_start(whole_rows[:], w1[0:SPAN, :].rearrange("(p j) c -> p j c", j=PACK))
+        raw = {(b, 0): [(whole_rows[:, :, SPAN * b : SPAN * (b + 1)], 0, SPAN)] for b in range(SPANS)}
         raw[(0, 1)] = [load_w1(kept, 0, 1, 0, SPAN)]
-        w4_raw = kept([P, SPANS, 2 * N], U8, "w4_raw")
-        nc.sync.dma_start(w4_raw[:].bitcast(I32), w4_words.rearrange("a p c -> p a c").bitcast(I32))
         nc.sync.dma_start(w4_rows[0:P:8, :, :].bitcast(I32), w4_scales.rearrange("a q c -> q a c").bitcast(I32))
 
         picked_rows = kept([P, SPANS, S], U8, "picked_rows")
@@ -92,8 +92,9 @@ def tile_list_malware_pair_family_kernel(
         picked = [kept([P, S], U32, "picked%d" % a) for a in range(SPANS)]
         nc.vector.tensor_copy(picked[0][:], table[0][:].bitcast(U32).indirect(offs_sb[:]))
 
-        raw[(1, 0)] = [load_w1(over_table(0), 1, 0, 0, SPAN)]
         raw[(1, 1)] = [load_w1(over_table(8192 + 16 * c0), 1, 1, c0, SPAN // 2) for c0 in (0, SPAN // 2)]
+        w4_raw = over_table(0)([P, SPANS, 2 * N], U8, "w4_raw")
+        nc.sync.dma_start(w4_raw[:].bitcast(I32), w4_words.rearrange("a p c -> p a c").bitcast(I32))
 
         w1_codes = {}
         w1_planes = kept([P, SPANS, SPANS, PACK, P], U8, "w1_planes")
@@ -101,7 +102,7 @@ def tile_list_malware_pair_family_kernel(
         def quantise_w1(b, a, engines, together):
             dealt = kept([P, PACK, P, PACK], BF16, "dealt%d%d" % (b, a))
             for (piece, c0, width), copy in zip(raw[(b, a)], engines):
-                src = piece[:].rearrange("p j (m t) -> p m j t", t=PACK)
+                src = piece.rearrange("p j (m t) -> p m j t", t=PACK)
                 dst = dealt[:, :, c0 // PACK : (c0 + width) // PACK, :].rearrange("p t m j -> p m j t")
                 copy(dst, src)
             for t0 in range(0, PACK, together):
@@ -131,7 +132,7 @@ def tile_list_malware_pair_family_kernel(
                 )
 
         by_slice = list(product(range(PACK), halves))
-        by_half = [(t, half) for half, t in product(halves, range(PACK))]
+        by_half = [(t0 + t, half) for t0, half, t in product((0, 2), halves, range(2))]
         accs = [
             {(t, half): bank(2 * t + half, [P, BANK], "acc%d" % b) for t in range(PACK) for half in halves} for b in range(SPANS)
         ]
@@ -139,17 +140,13 @@ def tile_list_malware_pair_family_kernel(
         first_pass(accs[0], 0, 0, by_half)
         gain = kept([P, SPANS, PACK], F32, "gain", tag="dealt00")
         nc.sync.dma_start(gain[:], g.rearrange("(b p t) -> p b t", b=SPANS, t=PACK))
-        w4_codes = kept([P, SPANS, 2 * N], U8, "w4_codes")
-        nc.vector.tensor_copy(
-            w4_codes[:].rearrange("p a c -> p (a c)").bitcast(U16).rearrange("p (x t c i) -> p x c t i", x=SPANS * SPANS, t=PACK, i=LINE // 2),
-            w4_raw[:].rearrange("p a c -> p (a c)").bitcast(U16).rearrange("p (x c i t) -> p x c t i", x=SPANS * SPANS, t=PACK, i=LINE // 2),
-        )
         w4_dealt_rows = kept([P, SPANS * N], U8, "w4_dealt_rows")
         nc.vector.tensor_copy(
             w4_dealt_rows[:].rearrange("p (x t c i) -> p x c t i", x=SPANS * SPANS, t=PACK, i=LINE),
             w4_rows[:].rearrange("p a c -> p (a c)").rearrange("p (x c i t) -> p x c t i", x=SPANS * SPANS, t=PACK, i=LINE),
         )
         quantise_w1(0, 1, [nc.scalar.copy], PACK)
+        quantise_w1(1, 0, [nc.vector.tensor_copy], PACK)
         for half in halves:
             nc.vector.tensor_copy(
                 picked[1][:, half * BANK : (half + 1) * BANK],
@@ -171,12 +168,16 @@ def tile_list_malware_pair_family_kernel(
                 nc.vector.tensor_copy(first_sample[b][:, t, :], h[(b, t)][:].indirect(pos1_sb[:]))
 
         sigmoids(0, by_half)
-        quantise_w1(1, 0, [nc.vector.tensor_copy], PACK)
         first_pass(accs[1], 1, 0, by_half)
-        quantise_w1(1, 1, [nc.vector.tensor_copy, nc.vector.tensor_copy], 2)
+        quantise_w1(1, 1, [nc.vector.tensor_copy, nc.vector.tensor_copy], 1)
         first_pass(accs[1], 1, 1, by_slice)
         for q in range(QUADS):
             nc.sync.dma_start(w4_planes[32 * q : 32 * q + 4, :].bitcast(I32), w4_dealt_rows[32 * q : 32 * q + 32 : 8, :].bitcast(I32))
+        w4_codes = kept([P, SPANS, 2 * N], U8, "w4_codes")
+        nc.vector.tensor_copy(
+            w4_codes[:].rearrange("p a c -> p (a c)").bitcast(U16).rearrange("p (x t c i) -> p x c t i", x=SPANS * SPANS, t=PACK, i=LINE // 2),
+            w4_raw[:].rearrange("p a c -> p (a c)").bitcast(U16).rearrange("p (x c i t) -> p x c t i", x=SPANS * SPANS, t=PACK, i=LINE // 2),
+        )
         pick_first(0)
         inv_gain = kept([P, SPANS, PACK], F32, "inv_gain")
         nc.vector.reciprocal(inv_gain[:], gain[:])
@@ -240,19 +241,17 @@ def tile_list_malware_pair_family_kernel(
 
         y_planes = kept([P, SPANS, PAIRS], U8, "y_planes")
 
-        def hand_out(j0, width, grp, y_codes, src=None):
+        def hand_out(j0, width, grp):
             y = kept([P, PACK, width], F32, "y%d_%d" % (j0, grp))
             for c0 in range(0, width, CHUNK):
                 nc.scalar.copy(y[:, :, c0 : c0 + CHUNK], sums[j0 + c0][grp][:])
             nc.sync.dma_start(
                 out_0[SPAN * grp : SPAN * (grp + 1), j0 : j0 + width].rearrange("(p t) j -> p t j", t=PACK), y[:]
             )
-            if src is None:
-                requantise(j0, width, grp, y_codes, y)
             return y
 
-        def requantise(j0, width, grp, y_codes, src):
-            rounded = kept([P, width, PACK], BF16, "rounded%d_%d" % (j0, grp))
+        def requantise(j0, width, grp, y_codes, src, slot=None):
+            rounded = kept([P, width, PACK], BF16, "rounded%d_%d" % (j0, grp), tag=slot)
             nc.vector.tensor_copy(
                 rounded[:].rearrange("p (c i) t -> p c t i", i=LINE // 4),
                 src[:].rearrange("p t (c i) -> p c t i", i=LINE // 4),
@@ -283,16 +282,17 @@ def tile_list_malware_pair_family_kernel(
             if n > 0:
                 agree(n - 1)
             if n >= 3:
-                hand_out(0, 2 * CHUNK, n - 3, y_codes[0])
+                requantise(0, 2 * CHUNK, n - 3, y_codes[0], hand_out(0, 2 * CHUNK, n - 3))
         store_codes(0, 2 * CHUNK, y_codes[0], nc.sync)
         agree(len(units) - 1)
+        third = 2 * CHUNK
         for grp in range(SPANS):
-            hand_out(2 * CHUNK, CHUNK, grp, y_codes[2 * CHUNK])
-        store_codes(2 * CHUNK, CHUNK, y_codes[2 * CHUNK], nc.sync)
+            requantise(third, CHUNK, grp, y_codes[third], hand_out(third, CHUNK, grp))
+        store_codes(third, CHUNK, y_codes[third], nc.sync)
         last = 3 * CHUNK
-        y_first = hand_out(last, CHUNK, 0, y_codes[last], True)
+        y_first = hand_out(last, CHUNK, 0)
         requantise(last, CHUNK, 1, y_codes[last], sums[last][1])
-        hand_out(last, CHUNK, 1, y_codes[last], True)
+        hand_out(last, CHUNK, 1)
         requantise(last, CHUNK, 0, y_codes[last], y_first)
         store_codes(last, CHUNK, y_codes[last], nc.scalar)
         for q in range(QUADS):

@@ -26,6 +26,9 @@ BANK = 512
 CHUNK = BANK // PACK
 LINE = 16
 PER_COLUMN = 16
+SPREAD = P // (4 * QUADS)
+TABLE_BYTES = 4 * T
+AHEAD = 2
 
 
 def tile_list_malware_pair_family_kernel(
@@ -47,10 +50,10 @@ def tile_list_malware_pair_family_kernel(
         pos1_sb = keep.tile([P, PAIRS // PER_COLUMN], U16, name="pos1_sb")
         pos2_sb = keep.tile([P, PAIRS // PER_COLUMN], U16, name="pos2_sb")
 
-        def over_table(offset):
+        def staged(offset):
             return lambda shape, dtype, name: stage.tile(shape, dtype, name=name, tag=name, offset=offset)
 
-        tab_rows = over_table(16384)([P, SPANS, T], U8, "tab_rows")
+        tab_rows = staged(TABLE_BYTES)([P, SPANS, T], U8, "tab_rows")
         nc.vector.memset(tab_rows[:].rearrange("p a t -> p (a t)").bitcast(I32), 0)
         picked_planes = kept([P, SPANS, S], U8, "picked_planes")
         nc.vector.memset(picked_planes[:].rearrange("p a s -> p (a s)").bitcast(I32), 0)
@@ -59,25 +62,25 @@ def tile_list_malware_pair_family_kernel(
         w4_planes = kept([P, SPANS * N], U8, "w4_planes")
         nc.vector.memset(w4_planes[:].bitcast(I32), 0)
 
-        def load_w1(pool_tile, b, a, c0, width):
-            piece = pool_tile([P, PACK, width], F32, "w1_raw%d%d_%d" % (b, a, c0))
+        def load_w1(make_tile, b, a, c0, width):
+            piece = make_tile([P, PACK, width], F32, "w1_raw%d%d_%d" % (b, a, c0))
             cols = slice(SPAN * b + c0, SPAN * b + c0 + width)
             nc.sync.dma_start(piece[:], w1[SPAN * a : SPAN * (a + 1), cols].rearrange("(p j) c -> p j c", j=PACK))
             return piece[:], c0, width
 
         nc.sync.dma_start(offs_sb[:], offs)
-        table = [over_table(0)([P, T], I32, "table0"), None]
+        table = [staged(0)([P, T], I32, "table0")]
         table_hbm = [tab_words[a].rearrange("p t i -> p (t i)").bitcast(I32) for a in range(SPANS)]
         nc.sync.dma_start(table[0][:, : T // 2], table_hbm[0][:, : T // 2])
         nc.sync.dma_start(pos1_sb[:], pos1)
         nc.sync.dma_start(pos2_sb[:], pos2)
-        nc.sync.dma_start(tab_rows[0:P:8, :, :].bitcast(I32), tab_scales.rearrange("a q t -> q a t").bitcast(I32))
+        nc.sync.dma_start(tab_rows[0:P:SPREAD, :, :].bitcast(I32), tab_scales.rearrange("a q t -> q a t").bitcast(I32))
         nc.sync.dma_start(table[0][:, T // 2 :], table_hbm[0][:, T // 2 :])
         whole_rows = kept([P, PACK, H], F32, "w1_whole_rows")
         nc.sync.dma_start(whole_rows[:], w1[0:SPAN, :].rearrange("(p j) c -> p j c", j=PACK))
         raw = {(b, 0): [(whole_rows[:, :, SPAN * b : SPAN * (b + 1)], 0, SPAN)] for b in range(SPANS)}
         raw[(0, 1)] = [load_w1(kept, 0, 1, 0, SPAN)]
-        nc.sync.dma_start(w4_rows[0:P:8, :, :].bitcast(I32), w4_scales.rearrange("a q c -> q a c").bitcast(I32))
+        nc.sync.dma_start(w4_rows[0:P:SPREAD, :, :].bitcast(I32), w4_scales.rearrange("a q c -> q a c").bitcast(I32))
 
         picked_rows = kept([P, SPANS, S], U8, "picked_rows")
         for a in range(SPANS):
@@ -85,23 +88,23 @@ def tile_list_malware_pair_family_kernel(
         for q in range(QUADS):
             nc.sync.dma_start(
                 picked_planes[32 * q : 32 * q + 4, :, :].rearrange("p a s -> p (a s)").bitcast(I32),
-                picked_rows[32 * q : 32 * q + 32 : 8, :, :].rearrange("p a s -> p (a s)").bitcast(I32),
+                picked_rows[32 * q : 32 * q + 32 : SPREAD, :, :].rearrange("p a s -> p (a s)").bitcast(I32),
             )
-        table[1] = over_table(16384)([P, T], I32, "table1")
+        table.append(staged(TABLE_BYTES)([P, T], I32, "table1"))
         nc.sync.dma_start(table[1][:], table_hbm[1])
         picked = [kept([P, S], U32, "picked%d" % a) for a in range(SPANS)]
         nc.vector.tensor_copy(picked[0][:], table[0][:].bitcast(U32).indirect(offs_sb[:]))
 
-        raw[(1, 1)] = [load_w1(over_table(8192 + 16 * c0), 1, 1, c0, SPAN // 2) for c0 in (0, SPAN // 2)]
-        w4_raw = over_table(0)([P, SPANS, 2 * N], U8, "w4_raw")
+        raw[(1, 1)] = [load_w1(staged(TABLE_BYTES // 2 + 4 * PACK * c0), 1, 1, c0, SPAN // 2) for c0 in (0, SPAN // 2)]
+        w4_raw = staged(0)([P, SPANS, 2 * N], U8, "w4_raw")
         nc.sync.dma_start(w4_raw[:].bitcast(I32), w4_words.rearrange("a p c -> p a c").bitcast(I32))
 
         w1_codes = {}
         w1_planes = kept([P, SPANS, SPANS, PACK, P], U8, "w1_planes")
 
-        def quantise_w1(b, a, engines, together):
+        def quantise_w1(b, a, copies, together):
             dealt = kept([P, PACK, P, PACK], BF16, "dealt%d%d" % (b, a))
-            for (piece, c0, width), copy in zip(raw[(b, a)], engines):
+            for (piece, c0, width), copy in zip(raw[(b, a)], copies):
                 src = piece.rearrange("p j (m t) -> p m j t", t=PACK)
                 dst = dealt[:, :, c0 // PACK : (c0 + width) // PACK, :].rearrange("p t m j -> p m j t")
                 copy(dst, src)
@@ -118,11 +121,11 @@ def tile_list_malware_pair_family_kernel(
 
         halves = range(S // BANK)
 
-        def first_pass(accs, b, a, order):
+        def first_pass(b, a, order):
             for t, half in order:
                 cols = slice(half * BANK, (half + 1) * BANK)
                 nc.tensor.matmul_mx(
-                    out=accs[(t, half)][:],
+                    out=accs[b][(t, half)][:],
                     lhsT=w1_codes[(b, a, t)].bitcast(E4M3),
                     lhsT_scale=w1_planes[:, b, a, t, :],
                     rhs=picked[a][:, cols].bitcast(E4M3),
@@ -132,12 +135,12 @@ def tile_list_malware_pair_family_kernel(
                 )
 
         by_slice = list(product(range(PACK), halves))
-        by_half = [(t0 + t, half) for t0, half, t in product((0, 2), halves, range(2))]
+        by_pair = [(t0 + t, half) for t0, half, t in product(range(0, PACK, 2), halves, range(2))]
         accs = [
             {(t, half): bank(2 * t + half, [P, BANK], "acc%d" % b) for t in range(PACK) for half in halves} for b in range(SPANS)
         ]
         quantise_w1(0, 0, [nc.scalar.copy], PACK)
-        first_pass(accs[0], 0, 0, by_half)
+        first_pass(0, 0, by_pair)
         gain = kept([P, SPANS, PACK], F32, "gain", tag="dealt00")
         nc.sync.dma_start(gain[:], g.rearrange("(b p t) -> p b t", b=SPANS, t=PACK))
         w4_dealt_rows = kept([P, SPANS * N], U8, "w4_dealt_rows")
@@ -152,10 +155,12 @@ def tile_list_malware_pair_family_kernel(
                 picked[1][:, half * BANK : (half + 1) * BANK],
                 table[1][:].bitcast(U32).indirect(offs_sb[:, half * BANK // PER_COLUMN : (half + 1) * BANK // PER_COLUMN]),
             )
-        first_pass(accs[0], 0, 1, by_half)
+        first_pass(0, 1, by_pair)
 
         h = {}
-        first_sample = [kept([P, PACK, PAIRS], F32, "first_sample%d" % b, tag="w1_raw01_0" if b else "dealt11") for b in range(SPANS)]
+        first_sample = [
+            kept([P, PACK, PAIRS], F32, "first_sample%d" % b, tag=tag) for b, tag in enumerate(("dealt11", "w1_raw01_0"))
+        ]
 
         def sigmoids(b, order):
             for t in range(PACK):
@@ -167,12 +172,12 @@ def tile_list_malware_pair_family_kernel(
             for t in range(PACK):
                 nc.vector.tensor_copy(first_sample[b][:, t, :], h[(b, t)][:].indirect(pos1_sb[:]))
 
-        sigmoids(0, by_half)
-        first_pass(accs[1], 1, 0, by_half)
+        sigmoids(0, by_pair)
+        first_pass(1, 0, by_pair)
         quantise_w1(1, 1, [nc.vector.tensor_copy, nc.vector.tensor_copy], 1)
-        first_pass(accs[1], 1, 1, by_slice)
+        first_pass(1, 1, by_slice)
         for q in range(QUADS):
-            nc.sync.dma_start(w4_planes[32 * q : 32 * q + 4, :].bitcast(I32), w4_dealt_rows[32 * q : 32 * q + 32 : 8, :].bitcast(I32))
+            nc.sync.dma_start(w4_planes[32 * q : 32 * q + 4, :].bitcast(I32), w4_dealt_rows[32 * q : 32 * q + 32 : SPREAD, :].bitcast(I32))
         w4_codes = kept([P, SPANS, 2 * N], U8, "w4_codes")
         nc.vector.tensor_copy(
             w4_codes[:].rearrange("p a c -> p (a c)").bitcast(U16).rearrange("p (x t c i) -> p x c t i", x=SPANS * SPANS, t=PACK, i=LINE // 2),
@@ -184,9 +189,10 @@ def tile_list_malware_pair_family_kernel(
         sigmoids(1, by_slice)
         pick_first(1)
 
-        units = [(0, 0, 256), (1, 0, 256), (0, 256, 256), (1, 256, 128), (1, 384, 128)]
-        slots = ["picked1", "picked0", "picked_planes", "inverse3", "inverse4"]
-        inverse, ratio, root, rounded_z = {}, {}, {}, {}
+        double, third, last = 2 * CHUNK, 2 * CHUNK, 3 * CHUNK
+        units = [(0, 0, double), (1, 0, double), (0, third, double), (1, third, CHUNK), (1, last, CHUNK)]
+        slots = ["picked1", "picked0", "picked_planes", None, None]
+        inverse, ratio, root = {}, {}, {}
         z_codes = {}
         z_planes = kept([P, SPANS, PAIRS], U8, "z_planes")
 
@@ -241,60 +247,60 @@ def tile_list_malware_pair_family_kernel(
 
         y_planes = kept([P, SPANS, PAIRS], U8, "y_planes")
 
-        def hand_out(j0, width, grp):
+        def hand_out(j0, width, grp, copy=nc.scalar.copy):
             y = kept([P, PACK, width], F32, "y%d_%d" % (j0, grp))
             for c0 in range(0, width, CHUNK):
-                nc.scalar.copy(y[:, :, c0 : c0 + CHUNK], sums[j0 + c0][grp][:])
+                copy(y[:, :, c0 : c0 + CHUNK], sums[j0 + c0][grp][:])
             nc.sync.dma_start(
                 out_0[SPAN * grp : SPAN * (grp + 1), j0 : j0 + width].rearrange("(p t) j -> p t j", t=PACK), y[:]
             )
             return y
 
-        def requantise(j0, width, grp, y_codes, src, slot=None):
-            rounded = kept([P, width, PACK], BF16, "rounded%d_%d" % (j0, grp), tag=slot)
-            nc.vector.tensor_copy(
+        def requantise(j0, width, grp, src, copy=nc.vector.tensor_copy):
+            rounded = kept([P, width, PACK], BF16, "rounded%d_%d" % (j0, grp))
+            copy(
                 rounded[:].rearrange("p (c i) t -> p c t i", i=LINE // 4),
                 src[:].rearrange("p t (c i) -> p c t i", i=LINE // 4),
             )
             nc.vector.quantize_mx(
-                out=y_codes[:, grp, :].bitcast(E4M3),
+                out=y_codes[j0][:, grp, :].bitcast(E4M3),
                 scales=y_planes[:, grp, j0 : j0 + width],
                 in_=rounded[:].rearrange("p j t -> p (j t)"),
             )
 
-        def store_codes(j0, width, y_codes, queue):
-            queue.dma_start(out_1[:, :, j0 : j0 + width, :].rearrange("g p m i -> p g (m i)").bitcast(I32), y_codes[:])
+        def store_codes(j0, width, queue):
+            queue.dma_start(out_1[:, :, j0 : j0 + width, :].rearrange("g p m i -> p g (m i)").bitcast(I32), y_codes[j0][:])
 
         sums = {
             j0: [bank(SPANS * (j0 // CHUNK) + grp, [P, PACK, CHUNK], "sums") for grp in range(SPANS)]
             for j0 in range(0, PAIRS, CHUNK)
         }
-        for n in range(2):
+        for n in range(AHEAD):
             root_first(n)
             invert_and_pick(n)
         y_codes = {j0: kept([P, SPANS, width], I32, "y_codes%d" % j0) for b, j0, width in units if b}
         for n in range(len(units)):
-            if n + 2 < len(units):
-                root_first(n + 2)
+            ahead = n + AHEAD < len(units)
+            if ahead:
+                root_first(n + AHEAD)
             fold(n)
-            if n + 2 < len(units):
-                invert_and_pick(n + 2)
+            if ahead:
+                invert_and_pick(n + AHEAD)
             if n > 0:
                 agree(n - 1)
-            if n >= 3:
-                requantise(0, 2 * CHUNK, n - 3, y_codes[0], hand_out(0, 2 * CHUNK, n - 3))
-        store_codes(0, 2 * CHUNK, y_codes[0], nc.sync)
+            if not ahead:
+                grp = n + AHEAD - len(units)
+                requantise(0, double, grp, hand_out(0, double, grp))
+        store_codes(0, double, nc.sync)
         agree(len(units) - 1)
-        third = 2 * CHUNK
         for grp in range(SPANS):
-            requantise(third, CHUNK, grp, y_codes[third], hand_out(third, CHUNK, grp))
-        store_codes(third, CHUNK, y_codes[third], nc.sync)
-        last = 3 * CHUNK
-        y_first = hand_out(last, CHUNK, 0)
-        requantise(last, CHUNK, 1, y_codes[last], sums[last][1])
-        hand_out(last, CHUNK, 1)
-        requantise(last, CHUNK, 0, y_codes[last], y_first)
-        store_codes(last, CHUNK, y_codes[last], nc.scalar)
+            requantise(third, CHUNK, grp, hand_out(third, CHUNK, grp))
+        store_codes(third, CHUNK, nc.sync)
+        hand_out(last, CHUNK, 0)
+        y_second = hand_out(last, CHUNK, 1, nc.vector.tensor_copy)
+        requantise(last, CHUNK, 0, sums[last][0], nc.scalar.copy)
+        requantise(last, CHUNK, 1, y_second)
+        store_codes(last, CHUNK, nc.scalar)
         for q in range(QUADS):
             queue = nc.scalar if q % 2 else nc.sync
             queue.dma_start(

@@ -53,14 +53,14 @@ def tile_list_malware_pair_family_kernel(
         def staged(offset):
             return lambda shape, dtype, name: stage.tile(shape, dtype, name=name, tag=name, offset=offset)
 
-        tab_rows = staged(TABLE_BYTES)([P, SPANS, T], U8, "tab_rows")
-        nc.vector.memset(tab_rows[:].rearrange("p a t -> p (a t)").bitcast(I32), 0)
+        tab_rows = staged(TABLE_BYTES)([P, T], U8, "tab_rows")
+        nc.vector.memset(tab_rows[:].bitcast(I32), 0)
         picked_planes = kept([P, SPANS, S], U8, "picked_planes")
         nc.vector.memset(picked_planes[:].rearrange("p a s -> p (a s)").bitcast(I32), 0)
-        w4_rows = kept([P, SPANS, N], U8, "w4_rows")
-        nc.vector.memset(w4_rows[:].rearrange("p a c -> p (a c)").bitcast(I32), 0)
         w4_planes = kept([P, SPANS * N], U8, "w4_planes")
         nc.vector.memset(w4_planes[:].bitcast(I32), 0)
+        w4_rows = kept([P, N], U8, "w4_rows")
+        nc.vector.memset(w4_rows[:].bitcast(I32), 0)
 
         def load_w1(make_tile, b, a, c0, width):
             piece = make_tile([P, PACK, width], F32, "w1_raw%d%d_%d" % (b, a, c0))
@@ -74,30 +74,24 @@ def tile_list_malware_pair_family_kernel(
         nc.sync.dma_start(table[0][:, : T // 2], table_hbm[0][:, : T // 2])
         nc.sync.dma_start(pos1_sb[:], pos1)
         nc.sync.dma_start(pos2_sb[:], pos2)
-        nc.sync.dma_start(tab_rows[0:P:SPREAD, :, :].bitcast(I32), tab_scales.rearrange("a q t -> q a t").bitcast(I32))
+        nc.sync.dma_start(tab_rows[0:P:4, :].bitcast(I32), tab_scales.rearrange("a q t -> q a t").bitcast(I32))
         nc.sync.dma_start(table[0][:, T // 2 :], table_hbm[0][:, T // 2 :])
-        whole_rows = kept([P, PACK, H], F32, "w1_whole_rows")
-        nc.sync.dma_start(whole_rows[:], w1[0:SPAN, :].rearrange("(p j) c -> p j c", j=PACK))
-        raw = {(b, 0): [(whole_rows[:, :, SPAN * b : SPAN * (b + 1)], 0, SPAN)] for b in range(SPANS)}
-        raw[(0, 1)] = [load_w1(kept, 0, 1, 0, SPAN)]
-        nc.sync.dma_start(w4_rows[0:P:SPREAD, :, :].bitcast(I32), w4_scales.rearrange("a q c -> q a c").bitcast(I32))
+        raw = {(0, a): [load_w1(kept, 0, a, 0, SPAN)] for a in range(SPANS)}
 
-        picked_rows = kept([P, SPANS, S], U8, "picked_rows")
-        for a in range(SPANS):
-            nc.vector.tensor_copy(picked_rows[:, a, :], tab_rows[:, a, :].indirect(offs_sb[:]))
+        picked_rows = kept([P, S], U8, "picked_rows")
+        nc.vector.tensor_copy(picked_rows[:], tab_rows[:].indirect(offs_sb[:]))
         for q in range(QUADS):
             nc.sync.dma_start(
-                picked_planes[32 * q : 32 * q + 4, :, :].rearrange("p a s -> p (a s)").bitcast(I32),
-                picked_rows[32 * q : 32 * q + 32 : SPREAD, :, :].rearrange("p a s -> p (a s)").bitcast(I32),
+                picked_planes[32 * q : 32 * q + 4, :, :].bitcast(I32),
+                picked_rows[32 * q : 32 * q + 32 : 4, :].bitcast(I32),
             )
         table.append(staged(TABLE_BYTES)([P, T], I32, "table1"))
         nc.sync.dma_start(table[1][:], table_hbm[1])
         picked = [kept([P, S], U32, "picked%d" % a) for a in range(SPANS)]
         nc.vector.tensor_copy(picked[0][:], table[0][:].bitcast(U32).indirect(offs_sb[:]))
 
+        raw[(1, 0)] = [load_w1(staged(0), 1, 0, 0, SPAN)]
         raw[(1, 1)] = [load_w1(staged(TABLE_BYTES // 2 + 4 * PACK * c0), 1, 1, c0, SPAN // 2) for c0 in (0, SPAN // 2)]
-        w4_raw = staged(0)([P, SPANS, 2 * N], U8, "w4_raw")
-        nc.sync.dma_start(w4_raw[:].bitcast(I32), w4_words.rearrange("a p c -> p a c").bitcast(I32))
 
         w1_codes = {}
         w1_planes = kept([P, SPANS, SPANS, PACK, P], U8, "w1_planes")
@@ -141,15 +135,12 @@ def tile_list_malware_pair_family_kernel(
         ]
         quantise_w1(0, 0, [nc.scalar.copy], PACK)
         first_pass(0, 0, by_pair)
+        w4_raw = kept([P, SPANS, 2 * N], U8, "w4_raw", tag="w1_raw00_0")
+        nc.sync.dma_start(w4_raw[:].bitcast(I32), w4_words.rearrange("a p c -> p a c").bitcast(I32))
         gain = kept([P, SPANS, PACK], F32, "gain", tag="dealt00")
         nc.sync.dma_start(gain[:], g.rearrange("(b p t) -> p b t", b=SPANS, t=PACK))
-        w4_dealt_rows = kept([P, SPANS * N], U8, "w4_dealt_rows")
-        nc.vector.tensor_copy(
-            w4_dealt_rows[:].rearrange("p (x t c i) -> p x c t i", x=SPANS * SPANS, t=PACK, i=LINE),
-            w4_rows[:].rearrange("p a c -> p (a c)").rearrange("p (x c i t) -> p x c t i", x=SPANS * SPANS, t=PACK, i=LINE),
-        )
         quantise_w1(0, 1, [nc.scalar.copy], PACK)
-        quantise_w1(1, 0, [nc.vector.tensor_copy], PACK)
+        nc.sync.dma_start(w4_rows[0:P:4, :].bitcast(I32), w4_scales.rearrange("a q c -> q a c").bitcast(I32))
         for half in halves:
             nc.vector.tensor_copy(
                 picked[1][:, half * BANK : (half + 1) * BANK],
@@ -173,48 +164,63 @@ def tile_list_malware_pair_family_kernel(
                 nc.vector.tensor_copy(first_sample[b][:, t, :], h[(b, t)][:].indirect(pos1_sb[:]))
 
         sigmoids(0, by_pair)
+        quantise_w1(1, 0, [nc.vector.tensor_copy], PACK)
         first_pass(1, 0, by_pair)
         quantise_w1(1, 1, [nc.vector.tensor_copy, nc.vector.tensor_copy], 1)
         first_pass(1, 1, by_slice)
+        pick_first(0)
+        w4_dealt_rows = kept([P, N], U8, "w4_dealt_rows")
+        nc.vector.tensor_copy(
+            w4_dealt_rows[:].rearrange("p (x t c i) -> p x c t i", x=SPANS, t=PACK, i=LINE),
+            w4_rows[:].rearrange("p (x c i t) -> p x c t i", x=SPANS, t=PACK, i=LINE),
+        )
         for q in range(QUADS):
-            nc.sync.dma_start(w4_planes[32 * q : 32 * q + 4, :].bitcast(I32), w4_dealt_rows[32 * q : 32 * q + 32 : SPREAD, :].bitcast(I32))
+            nc.sync.dma_start(
+                w4_planes[32 * q : 32 * q + 4, :].rearrange("p (x c) -> p x c", c=N).bitcast(I32),
+                w4_dealt_rows[32 * q : 32 * q + 32 : 4, :].bitcast(I32),
+            )
         w4_codes = kept([P, SPANS, 2 * N], U8, "w4_codes")
         nc.vector.tensor_copy(
             w4_codes[:].rearrange("p a c -> p (a c)").bitcast(U16).rearrange("p (x t c i) -> p x c t i", x=SPANS * SPANS, t=PACK, i=LINE // 2),
             w4_raw[:].rearrange("p a c -> p (a c)").bitcast(U16).rearrange("p (x c i t) -> p x c t i", x=SPANS * SPANS, t=PACK, i=LINE // 2),
         )
-        pick_first(0)
         inv_gain = kept([P, SPANS, PACK], F32, "inv_gain")
         nc.vector.reciprocal(inv_gain[:], gain[:])
+        inv_gain2 = kept([P, SPANS, PACK], F32, "inv_gain2")
+        nc.vector.tensor_tensor(inv_gain2[:], inv_gain[:], inv_gain[:], ALU.mult)
         sigmoids(1, by_slice)
         pick_first(1)
 
         double, third, last = 2 * CHUNK, 2 * CHUNK, 3 * CHUNK
         units = [(0, 0, double), (1, 0, double), (0, third, double), (1, third, CHUNK), (1, last, CHUNK)]
-        slots = ["picked1", "picked0", "picked_planes", None, None]
-        inverse, ratio, root = {}, {}, {}
+        slots = ["picked1", None, "picked0", None, None]
+        inverse, forward, backward = {}, {}, {}
         z_codes = {}
         z_planes = kept([P, SPANS, PAIRS], U8, "z_planes")
 
         def root_first(n):
             b, j0, width = units[n]
             inverse[n] = kept([P, PACK, width], F32, "inverse%d" % n, tag=slots[n])
-            nc.scalar.activation(inverse[n][:], first_sample[b][:, :, j0 : j0 + width], ACT.Abs_reciprocal_sqrt)
+            for t in range(PACK):
+                nc.scalar.activation(
+                    inverse[n][:, t, :], first_sample[b][:, t, j0 : j0 + width], ACT.Abs_reciprocal_sqrt, scale=inv_gain[:, b, t : t + 1]
+                )
 
         def invert_and_pick(n):
             b, j0, width = units[n]
             nc.scalar.activation(inverse[n][:], inverse[n][:], ACT.Square)
-            ratio[n] = kept([P, PACK, width], F32, "ratio%d" % n)
+            forward[n] = kept([P, PACK, width], F32, "forward%d" % n)
             cols = slice(j0 // PER_COLUMN, (j0 + width) // PER_COLUMN)
             for t in range(PACK):
-                nc.vector.tensor_tensor(ratio[n][:, t, :], h[(b, t)][:].indirect(pos2_sb[:, cols]), inverse[n][:, t, :], ALU.mult)
+                nc.vector.tensor_tensor(forward[n][:, t, :], h[(b, t)][:].indirect(pos2_sb[:, cols]), inverse[n][:, t, :], ALU.mult)
 
-        def fold(n):
+        def root_second(n):
             b, j0, width = units[n]
-            root[n] = kept([P, PACK, width], F32, "root%d" % n)
+            backward[n] = kept([P, PACK, width], F32, "backward%d" % n)
             for t in range(PACK):
-                nc.scalar.activation(root[n][:, t, :], ratio[n][:, t, :], ACT.Abs_reciprocal_sqrt, scale=inv_gain[:, b, t : t + 1])
-            nc.vector.scalar_tensor_tensor(root[n][:], ratio[n][:], 1.0, root[n][:], ALU.min, ALU.mult)
+                nc.scalar.activation(
+                    backward[n][:, t, :], forward[n][:, t, :], ACT.Abs_reciprocal_sqrt, scale=inv_gain2[:, b, t : t + 1]
+                )
 
         def second_pass(a, j0):
             for grp, t in product(range(SPANS), range(PACK)):
@@ -231,11 +237,13 @@ def tile_list_malware_pair_family_kernel(
 
         def agree(n):
             b, j0, width = units[n]
+            nc.scalar.activation(backward[n][:], backward[n][:], ACT.Square)
             z = kept([P, width, PACK], BF16, "z%d" % n)
-            nc.scalar.activation(
+            nc.vector.tensor_tensor(
                 z[:].rearrange("p (c i) t -> p c t i", i=LINE // 4),
-                root[n][:].rearrange("p t (c i) -> p c t i", i=LINE // 4),
-                ACT.Square,
+                forward[n][:].rearrange("p t (c i) -> p c t i", i=LINE // 4),
+                backward[n][:].rearrange("p t (c i) -> p c t i", i=LINE // 4),
+                ALU.min,
             )
             codes = kept([P, width], U32, "z_codes%d" % n)
             nc.vector.quantize_mx(
@@ -275,24 +283,32 @@ def tile_list_malware_pair_family_kernel(
             j0: [bank(SPANS * (j0 // CHUNK) + grp, [P, PACK, CHUNK], "sums") for grp in range(SPANS)]
             for j0 in range(0, PAIRS, CHUNK)
         }
-        for n in range(AHEAD):
-            root_first(n)
-            invert_and_pick(n)
         y_codes = {j0: kept([P, SPANS, width], I32, "y_codes%d" % j0) for b, j0, width in units if b}
-        for n in range(len(units)):
-            ahead = n + AHEAD < len(units)
-            if ahead:
-                root_first(n + AHEAD)
-            fold(n)
-            if ahead:
-                invert_and_pick(n + AHEAD)
-            if n > 0:
-                agree(n - 1)
-            if not ahead:
-                grp = n + AHEAD - len(units)
-                requantise(0, double, grp, hand_out(0, double, grp))
+        root_first(0)
+        root_first(2)
+        invert_and_pick(0)
+        root_first(1)
+        root_first(3)
+        invert_and_pick(1)
+        root_second(0)
+        invert_and_pick(2)
+        agree(0)
+        root_first(4)
+        root_second(1)
+        invert_and_pick(3)
+        agree(1)
+        invert_and_pick(4)
+        root_second(2)
+        root_second(3)
+        agree(2)
+        y_first = [hand_out(0, double, 0)]
+        agree(3)
+        root_second(4)
+        y_first.append(hand_out(0, double, 1))
+        agree(4)
+        for grp in range(SPANS):
+            requantise(0, double, grp, y_first[grp])
         store_codes(0, double, nc.sync)
-        agree(len(units) - 1)
         for grp in range(SPANS):
             requantise(third, CHUNK, grp, hand_out(third, CHUNK, grp))
         store_codes(third, CHUNK, nc.sync)

@@ -96,22 +96,28 @@ def tile_list_malware_pair_family_kernel(
         w1_codes = {}
         w1_planes = kept([P, SPANS, SPANS, PACK, P], U8, "w1_planes")
 
-        def quantise_w1(b, a, copies, together):
-            dealt = kept([P, PACK, P, PACK], BF16, "dealt%d%d" % (b, a))
-            for (piece, c0, width), copy in zip(raw[(b, a)], copies):
-                src = piece.rearrange("p j (m t) -> p m j t", t=PACK)
-                dst = dealt[:, :, c0 // PACK : (c0 + width) // PACK, :].rearrange("p t m j -> p m j t")
-                copy(dst, src)
-            for t0 in range(0, PACK, together):
-                codes = kept([P, together, P], U32, "w1_codes%d%d%d" % (b, a, t0))
-                rows = slice(t0, t0 + together)
-                nc.vector.quantize_mx(
-                    out=codes[:].rearrange("p t m -> p (t m)").bitcast(E4M3),
-                    scales=w1_planes[:, b, a, rows, :].rearrange("p t m -> p (t m)"),
-                    in_=dealt[:, rows, :, :].rearrange("p t m j -> p (t m j)"),
-                )
-                for u in range(together):
-                    w1_codes[(b, a, t0 + u)] = codes[:, u, :]
+        dealt = {}
+
+        def cast_w1(b, a, piece, slices, copy):
+            if (b, a) not in dealt:
+                dealt[(b, a)] = kept([P, PACK, P, PACK], BF16, "dealt%d%d" % (b, a))
+            rows, c0, width = piece
+            src = rows.rearrange("p j (m t) -> p m j t", t=PACK)[:, :, :, slices]
+            dst = dealt[(b, a)][:, slices, c0 // PACK : (c0 + width) // PACK, :].rearrange("p t m j -> p m j t")
+            copy(dst, src)
+
+        def quantise_w1(b, a, slices):
+            count = slices.stop - slices.start
+            codes = kept([P, count, P], U32, "w1_codes%d%d%d" % (b, a, slices.start))
+            nc.vector.quantize_mx(
+                out=codes[:].rearrange("p t m -> p (t m)").bitcast(E4M3),
+                scales=w1_planes[:, b, a, slices, :].rearrange("p t m -> p (t m)"),
+                in_=dealt[(b, a)][:, slices, :, :].rearrange("p t m j -> p (t m j)"),
+            )
+            for u in range(count):
+                w1_codes[(b, a, slices.start + u)] = codes[:, u, :]
+
+        whole, low, high = slice(0, PACK), slice(0, PACK // 2), slice(PACK // 2, PACK)
 
         halves = range(S // BANK)
 
@@ -133,13 +139,15 @@ def tile_list_malware_pair_family_kernel(
         accs = [
             {(t, half): bank(2 * t + half, [P, BANK], "acc%d" % b) for t in range(PACK) for half in halves} for b in range(SPANS)
         ]
-        quantise_w1(0, 0, [nc.scalar.copy], PACK)
+        cast_w1(0, 0, raw[(0, 0)][0], whole, nc.scalar.copy)
+        quantise_w1(0, 0, whole)
         first_pass(0, 0, by_pair)
         w4_raw = kept([P, SPANS, 2 * N], U8, "w4_raw", tag="w1_raw00_0")
         nc.sync.dma_start(w4_raw[:].bitcast(I32), w4_words.rearrange("a p c -> p a c").bitcast(I32))
         gain = kept([P, SPANS, PACK], F32, "gain", tag="dealt00")
         nc.sync.dma_start(gain[:], g.rearrange("(b p t) -> p b t", b=SPANS, t=PACK))
-        quantise_w1(0, 1, [nc.scalar.copy], PACK)
+        cast_w1(0, 1, raw[(0, 1)][0], whole, nc.scalar.copy)
+        quantise_w1(0, 1, whole)
         nc.sync.dma_start(w4_rows[0:P:4, :].bitcast(I32), w4_scales.rearrange("a q c -> q a c").bitcast(I32))
         for half in halves:
             nc.vector.tensor_copy(
@@ -164,9 +172,16 @@ def tile_list_malware_pair_family_kernel(
                 nc.vector.tensor_copy(first_sample[b][:, t, :], h[(b, t)][:].indirect(pos1_sb[:]))
 
         sigmoids(0, by_pair)
-        quantise_w1(1, 0, [nc.vector.tensor_copy], PACK)
+        for slices in (low, high):
+            cast_w1(1, 0, raw[(1, 0)][0], slices, nc.vector.tensor_copy)
+        for slices in (low, high):
+            quantise_w1(1, 0, slices)
         first_pass(1, 0, by_pair)
-        quantise_w1(1, 1, [nc.vector.tensor_copy, nc.vector.tensor_copy], 1)
+        cast_w1(1, 1, raw[(1, 1)][0], whole, nc.vector.tensor_copy)
+        for slices in (low, high):
+            cast_w1(1, 1, raw[(1, 1)][1], slices, nc.vector.tensor_copy)
+        for slices in (low, high):
+            quantise_w1(1, 1, slices)
         first_pass(1, 1, by_slice)
         pick_first(0)
         w4_dealt_rows = kept([P, N], U8, "w4_dealt_rows")
@@ -238,17 +253,22 @@ def tile_list_malware_pair_family_kernel(
         def agree(n):
             b, j0, width = units[n]
             nc.scalar.activation(backward[n][:], backward[n][:], ACT.Square)
+            parts = [slice(c0, c0 + width // 2) for c0 in (0, width // 2)]
             z = kept([P, width, PACK], BF16, "z%d" % n)
-            nc.vector.tensor_tensor(
-                z[:].rearrange("p (c i) t -> p c t i", i=LINE // 4),
-                forward[n][:].rearrange("p t (c i) -> p c t i", i=LINE // 4),
-                backward[n][:].rearrange("p t (c i) -> p c t i", i=LINE // 4),
-                ALU.min,
-            )
+            for part in parts:
+                nc.vector.tensor_tensor(
+                    z[:, part, :].rearrange("p (c i) t -> p c t i", i=LINE // 4),
+                    forward[n][:, :, part].rearrange("p t (c i) -> p c t i", i=LINE // 4),
+                    backward[n][:, :, part].rearrange("p t (c i) -> p c t i", i=LINE // 4),
+                    ALU.min,
+                )
             codes = kept([P, width], U32, "z_codes%d" % n)
-            nc.vector.quantize_mx(
-                out=codes[:].bitcast(E4M3), scales=z_planes[:, b, j0 : j0 + width], in_=z[:].rearrange("p j t -> p (j t)")
-            )
+            for part in parts:
+                nc.vector.quantize_mx(
+                    out=codes[:, part].bitcast(E4M3),
+                    scales=z_planes[:, b, j0 + part.start : j0 + part.stop],
+                    in_=z[:, part, :].rearrange("p j t -> p (j t)"),
+                )
             for c0 in range(0, width, CHUNK):
                 z_codes[(b, j0 + c0)] = codes[:, c0 : c0 + CHUNK]
                 second_pass(b, j0 + c0)
@@ -266,15 +286,18 @@ def tile_list_malware_pair_family_kernel(
 
         def requantise(j0, width, grp, src, copy=nc.vector.tensor_copy):
             rounded = kept([P, width, PACK], BF16, "rounded%d_%d" % (j0, grp))
-            copy(
-                rounded[:].rearrange("p (c i) t -> p c t i", i=LINE // 4),
-                src[:].rearrange("p t (c i) -> p c t i", i=LINE // 4),
-            )
-            nc.vector.quantize_mx(
-                out=y_codes[j0][:, grp, :].bitcast(E4M3),
-                scales=y_planes[:, grp, j0 : j0 + width],
-                in_=rounded[:].rearrange("p j t -> p (j t)"),
-            )
+            parts = [slice(c0, c0 + width // 2) for c0 in (0, width // 2)]
+            for part in parts:
+                copy(
+                    rounded[:, part, :].rearrange("p (c i) t -> p c t i", i=LINE // 4),
+                    src[:, :, part].rearrange("p t (c i) -> p c t i", i=LINE // 4),
+                )
+            for part in parts:
+                nc.vector.quantize_mx(
+                    out=y_codes[j0][:, grp, part].bitcast(E4M3),
+                    scales=y_planes[:, grp, j0 + part.start : j0 + part.stop],
+                    in_=rounded[:, part, :].rearrange("p j t -> p (j t)"),
+                )
 
         def store_codes(j0, width, queue):
             queue.dma_start(out_1[:, :, j0 : j0 + width, :].rearrange("g p m i -> p g (m i)").bitcast(I32), y_codes[j0][:])

@@ -68,10 +68,10 @@ def tile_list_malware_pair_family_kernel(
             nc.sync.dma_start(piece[:], w1[SPAN * a : SPAN * (a + 1), cols].rearrange("(p j) c -> p j c", j=PACK))
             return piece[:], c0, width
 
-        nc.sync.dma_start(offs_sb[:], offs)
         table = [staged(0)([P, T], I32, "table0")]
         table_hbm = [tab_words[a].rearrange("p t i -> p (t i)").bitcast(I32) for a in range(SPANS)]
         nc.sync.dma_start(table[0][:, : T // 2], table_hbm[0][:, : T // 2])
+        nc.sync.dma_start(offs_sb[:], offs)
         nc.sync.dma_start(pos1_sb[:], pos1)
         nc.sync.dma_start(pos2_sb[:], pos2)
         nc.sync.dma_start(tab_rows[0:P:4, :].bitcast(I32), tab_scales.rearrange("a q t -> q a t").bitcast(I32))
@@ -119,6 +119,7 @@ def tile_list_malware_pair_family_kernel(
 
         whole, low, high = slice(0, PACK), slice(0, PACK // 2), slice(PACK // 2, PACK)
 
+        RUN = 4
         halves = range(S // BANK)
 
         def first_pass(b, a, order):
@@ -221,9 +222,12 @@ def tile_list_malware_pair_family_kernel(
                     inverse[n][:, t, :], first_sample[b][:, t, j0 : j0 + width], ACT.Abs_reciprocal_sqrt, scale=inv_gain[:, b, t : t + 1]
                 )
 
-        def invert_and_pick(n):
+        def invert(n, groups=(whole,)):
+            for slices in groups:
+                nc.scalar.activation(inverse[n][:, slices, :], inverse[n][:, slices, :], ACT.Square)
+
+        def pick_second(n):
             b, j0, width = units[n]
-            nc.scalar.activation(inverse[n][:], inverse[n][:], ACT.Square)
             forward[n] = kept([P, PACK, width], F32, "forward%d" % n)
             cols = slice(j0 // PER_COLUMN, (j0 + width) // PER_COLUMN)
             for t in range(PACK):
@@ -250,16 +254,17 @@ def tile_list_malware_pair_family_kernel(
                     stop=(a == SPANS - 1 and t == PACK - 1),
                 )
 
-        def agree(n):
+        def agree(n, count, groups=(whole,)):
             b, j0, width = units[n]
-            nc.scalar.activation(backward[n][:], backward[n][:], ACT.Square)
-            parts = [slice(c0, c0 + width // 2) for c0 in (0, width // 2)]
+            for slices in groups:
+                nc.scalar.activation(backward[n][:, slices, :], backward[n][:, slices, :], ACT.Square)
+            parts = [slice(c0, c0 + width // count) for c0 in range(0, width, width // count)]
             z = kept([P, width, PACK], BF16, "z%d" % n)
             for part in parts:
                 nc.vector.tensor_tensor(
-                    z[:, part, :].rearrange("p (c i) t -> p c t i", i=LINE // 4),
-                    forward[n][:, :, part].rearrange("p t (c i) -> p c t i", i=LINE // 4),
-                    backward[n][:, :, part].rearrange("p t (c i) -> p c t i", i=LINE // 4),
+                    z[:, part, :].rearrange("p (c i) t -> p c t i", i=RUN),
+                    forward[n][:, :, part].rearrange("p t (c i) -> p c t i", i=RUN),
+                    backward[n][:, :, part].rearrange("p t (c i) -> p c t i", i=RUN),
                     ALU.min,
                 )
             codes = kept([P, width], U32, "z_codes%d" % n)
@@ -275,29 +280,31 @@ def tile_list_malware_pair_family_kernel(
 
         y_planes = kept([P, SPANS, PAIRS], U8, "y_planes")
 
-        def hand_out(j0, width, grp, copy=nc.scalar.copy):
-            y = kept([P, PACK, width], F32, "y%d_%d" % (j0, grp))
-            for c0 in range(0, width, CHUNK):
-                copy(y[:, :, c0 : c0 + CHUNK], sums[j0 + c0][grp][:])
-            nc.sync.dma_start(
-                out_0[SPAN * grp : SPAN * (grp + 1), j0 : j0 + width].rearrange("(p t) j -> p t j", t=PACK), y[:]
-            )
-            return y
+        y, rounded = {}, {}
 
-        def requantise(j0, width, grp, src, copy=nc.vector.tensor_copy):
-            rounded = kept([P, width, PACK], BF16, "rounded%d_%d" % (j0, grp))
-            parts = [slice(c0, c0 + width // 2) for c0 in (0, width // 2)]
-            for part in parts:
-                copy(
-                    rounded[:, part, :].rearrange("p (c i) t -> p c t i", i=LINE // 4),
-                    src[:, :, part].rearrange("p t (c i) -> p c t i", i=LINE // 4),
+        def hand_out(j0, width, c0, grp, copy=nc.scalar.copy):
+            if c0 == 0:
+                y[(j0, grp)] = kept([P, PACK, width], F32, "y%d_%d" % (j0, grp))
+            copy(y[(j0, grp)][:, :, c0 : c0 + CHUNK], sums[j0 + c0][grp][:])
+            if c0 + CHUNK == width:
+                nc.sync.dma_start(
+                    out_0[SPAN * grp : SPAN * (grp + 1), j0 : j0 + width].rearrange("(p t) j -> p t j", t=PACK), y[(j0, grp)][:]
                 )
-            for part in parts:
-                nc.vector.quantize_mx(
-                    out=y_codes[j0][:, grp, part].bitcast(E4M3),
-                    scales=y_planes[:, grp, j0 + part.start : j0 + part.stop],
-                    in_=rounded[:, part, :].rearrange("p j t -> p (j t)"),
-                )
+
+        def round_y(j0, width, grp, src, part, copy=nc.vector.tensor_copy):
+            if (j0, grp) not in rounded:
+                rounded[(j0, grp)] = kept([P, width, PACK], BF16, "rounded%d_%d" % (j0, grp))
+            copy(
+                rounded[(j0, grp)][:, part, :].rearrange("p (c i) t -> p c t i", i=RUN),
+                src.rearrange("p t (c i) -> p c t i", i=RUN),
+            )
+
+        def quantise_y(j0, grp, part):
+            nc.vector.quantize_mx(
+                out=y_codes[j0 // double * double][:, grp, j0 % double + part.start : j0 % double + part.stop].bitcast(E4M3),
+                scales=y_planes[:, grp, j0 + part.start : j0 + part.stop],
+                in_=rounded[(j0, grp)][:, part, :].rearrange("p j t -> p (j t)"),
+            )
 
         def store_codes(j0, width, queue):
             queue.dma_start(out_1[:, :, j0 : j0 + width, :].rearrange("g p m i -> p g (m i)").bitcast(I32), y_codes[j0][:])
@@ -306,40 +313,62 @@ def tile_list_malware_pair_family_kernel(
             j0: [bank(SPANS * (j0 // CHUNK) + grp, [P, PACK, CHUNK], "sums") for grp in range(SPANS)]
             for j0 in range(0, PAIRS, CHUNK)
         }
-        y_codes = {j0: kept([P, SPANS, width], I32, "y_codes%d" % j0) for b, j0, width in units if b}
+        y_codes = {j0: kept([P, SPANS, double], I32, "y_codes%d" % j0) for j0 in (0, double)}
         root_first(0)
         root_first(2)
-        invert_and_pick(0)
+        invert(0)
+        pick_second(0)
         root_first(1)
         root_first(3)
-        invert_and_pick(1)
+        invert(1)
+        pick_second(1)
         root_second(0)
-        invert_and_pick(2)
-        agree(0)
+        invert(2)
+        pick_second(2)
+        agree(0, 2)
         root_first(4)
         root_second(1)
-        invert_and_pick(3)
-        agree(1)
-        invert_and_pick(4)
+        invert(3)
+        pick_second(3)
+        agree(1, 2)
+        invert(4)
+        pick_second(4)
         root_second(2)
         root_second(3)
-        agree(2)
-        y_first = [hand_out(0, double, 0)]
-        agree(3)
+        agree(2, 2)
+        hand_out(0, double, 0, 0)
+        hand_out(0, double, CHUNK, 0)
+        agree(3, 2)
         root_second(4)
-        y_first.append(hand_out(0, double, 1))
-        agree(4)
-        for grp in range(SPANS):
-            requantise(0, double, grp, y_first[grp])
+        hand_out(0, double, 0, 1)
+        hand_out(0, double, CHUNK, 1)
+        agree(4, 2)
+        for part in (slice(0, double // 2), slice(double // 2, double)):
+            round_y(0, double, 0, y[(0, 0)][:, :, part], part)
+        for part in (slice(0, double // 2), slice(double // 2, double)):
+            quantise_y(0, 0, part)
+        round_y(0, double, 1, y[(0, 1)][:, :, :CHUNK], slice(0, CHUNK))
+        round_y(0, double, 1, sums[CHUNK][1][:], slice(CHUNK, double), nc.scalar.copy)
+        for part in (slice(0, CHUNK), slice(CHUNK, double)):
+            quantise_y(0, 1, part)
         store_codes(0, double, nc.sync)
         for grp in range(SPANS):
-            requantise(third, CHUNK, grp, hand_out(third, CHUNK, grp))
-        store_codes(third, CHUNK, nc.sync)
-        hand_out(last, CHUNK, 0)
-        y_second = hand_out(last, CHUNK, 1, nc.vector.tensor_copy)
-        requantise(last, CHUNK, 0, sums[last][0], nc.scalar.copy)
-        requantise(last, CHUNK, 1, y_second)
-        store_codes(last, CHUNK, nc.scalar)
+            hand_out(third, CHUNK, 0, grp)
+        round_y(third, CHUNK, 0, sums[third][0][:], slice(0, CHUNK), nc.scalar.copy)
+        quantise_y(third, 0, slice(0, CHUNK))
+        for part in (slice(0, CHUNK // 2), slice(CHUNK // 2, CHUNK)):
+            round_y(third, CHUNK, 1, y[(third, 1)][:, :, part], part)
+        for part in (slice(0, CHUNK // 2), slice(CHUNK // 2, CHUNK)):
+            quantise_y(third, 1, part)
+        hand_out(last, CHUNK, 0, 0)
+        hand_out(last, CHUNK, 0, 1, nc.vector.tensor_copy)
+        round_y(last, CHUNK, 0, sums[last][0][:], slice(0, CHUNK), nc.scalar.copy)
+        quantise_y(last, 0, slice(0, CHUNK))
+        for part in (slice(0, CHUNK // 2), slice(CHUNK // 2, CHUNK)):
+            round_y(last, CHUNK, 1, y[(last, 1)][:, :, part], part)
+        for part in (slice(0, CHUNK // 2), slice(CHUNK // 2, CHUNK)):
+            quantise_y(last, 1, part)
+        store_codes(double, double, nc.scalar)
         for q in range(QUADS):
             queue = nc.scalar if q % 2 else nc.sync
             queue.dma_start(

@@ -315,14 +315,14 @@ def tile_list_malware_pair_family_kernel(
         }
         y_codes = {j0: kept([P, SPANS, double], I32, "y_codes%d" % j0) for j0 in (0, double)}
         root_first(0)
-        root_first(2)
-        invert(0)
+        invert(0, (low, high))
         pick_second(0)
+        root_first(2)
         root_first(1)
-        root_first(3)
-        invert(1)
+        invert(1, (low, high))
         pick_second(1)
         root_second(0)
+        root_first(3)
         invert(2)
         pick_second(2)
         agree(0, 2)

@@ -51,7 +51,7 @@ def tile_list_malware_pair_family_kernel(
         pos2_sb = keep.tile([P, PAIRS // PER_COLUMN], U16, name="pos2_sb")
 
         def staged(offset):
-            return lambda shape, dtype, name: stage.tile(shape, dtype, name=name, tag=name, offset=offset)
+            return lambda shape, dtype, name: stage.tile(shape, dtype, name=name, tag=name, offset=offset, align_bytes=64)
 
         tab_rows = staged(TABLE_BYTES)([P, T], U8, "tab_rows")
         nc.vector.memset(tab_rows[:].bitcast(I32), 0)
@@ -106,9 +106,9 @@ def tile_list_malware_pair_family_kernel(
             dst = dealt[(b, a)][:, slices, c0 // PACK : (c0 + width) // PACK, :].rearrange("p t m j -> p m j t")
             copy(dst, src)
 
-        def quantise_w1(b, a, slices):
+        def quantise_w1(b, a, slices, make=kept):
             count = slices.stop - slices.start
-            codes = kept([P, count, P], U32, "w1_codes%d%d%d" % (b, a, slices.start))
+            codes = make([P, count, P], U32, "w1_codes%d%d%d" % (b, a, slices.start))
             nc.vector.quantize_mx(
                 out=codes[:].rearrange("p t m -> p (t m)").bitcast(E4M3),
                 scales=w1_planes[:, b, a, slices, :].rearrange("p t m -> p (t m)"),
@@ -175,15 +175,16 @@ def tile_list_malware_pair_family_kernel(
         sigmoids(0, by_pair)
         for slices in (low, high):
             cast_w1(1, 0, raw[(1, 0)][0], slices, nc.vector.tensor_copy)
-        for slices in (low, high):
-            quantise_w1(1, 0, slices)
-        first_pass(1, 0, by_pair)
+        quantise_w1(1, 0, low)
         cast_w1(1, 1, raw[(1, 1)][0], whole, nc.vector.tensor_copy)
         for slices in (low, high):
             cast_w1(1, 1, raw[(1, 1)][1], slices, nc.vector.tensor_copy)
-        for slices in (low, high):
-            quantise_w1(1, 1, slices)
-        first_pass(1, 1, by_slice)
+        quantise_w1(1, 1, low)
+        quantise_w1(1, 0, high, staged(3 * TABLE_BYTES // 4))
+        quantise_w1(1, 1, high)
+        for step in by_slice:
+            for a in range(SPANS):
+                first_pass(1, a, [step])
         pick_first(0)
         w4_dealt_rows = kept([P, N], U8, "w4_dealt_rows")
         nc.vector.tensor_copy(

@@ -210,18 +210,17 @@ def tile_list_malware_pair_family_kernel(
 
         double, third, last = 2 * CHUNK, 2 * CHUNK, 3 * CHUNK
         units = [(0, 0, double), (1, 0, double), (0, third, double), (1, third, CHUNK), (1, last, CHUNK)]
-        slots = ["picked1", None, "picked0", None, None]
         inverse, forward, backward = {}, {}, {}
         z_codes = {}
         z_planes = kept([P, SPANS, PAIRS], U8, "z_planes")
 
-        def root_first(n):
-            b, j0, width = units[n]
-            inverse[n] = kept([P, PACK, width], F32, "inverse%d" % n, tag=slots[n])
+        def root_first(b):
+            roots = kept([P, PACK, PAIRS], F32, "inverse%d" % b, tag="picked%d" % b)
             for t in range(PACK):
-                nc.scalar.activation(
-                    inverse[n][:, t, :], first_sample[b][:, t, j0 : j0 + width], ACT.Abs_reciprocal_sqrt, scale=inv_gain[:, b, t : t + 1]
-                )
+                nc.scalar.activation(roots[:, t, :], first_sample[b][:, t, :], ACT.Abs_reciprocal_sqrt, scale=inv_gain[:, b, t : t + 1])
+            for n, (span, j0, width) in enumerate(units):
+                if span == b:
+                    inverse[n] = roots[:, :, j0 : j0 + width]
 
         def invert(n, groups=(whole,)):
             for slices in groups:
@@ -318,16 +317,13 @@ def tile_list_malware_pair_family_kernel(
         root_first(0)
         invert(0, (low, high))
         pick_second(0)
-        root_first(2)
         root_first(1)
         invert(1, (low, high))
         pick_second(1)
         root_second(0)
-        root_first(3)
         invert(2)
         pick_second(2)
         agree(0, 2)
-        root_first(4)
         root_second(1)
         invert(3)
         pick_second(3)
@@ -337,9 +333,9 @@ def tile_list_malware_pair_family_kernel(
         root_second(2)
         root_second(3)
         agree(2, 2)
+        agree(3, 2)
         hand_out(0, double, 0, 0)
         hand_out(0, double, CHUNK, 0)
-        agree(3, 2)
         root_second(4)
         hand_out(0, double, 0, 1)
         hand_out(0, double, CHUNK, 1)

@@ -351,12 +351,9 @@ def tile_list_malware_pair_family_kernel(
         store_codes(0, double, nc.sync)
         for grp in range(SPANS):
             hand_out(third, CHUNK, 0, grp)
-        round_y(third, CHUNK, 0, sums[third][0][:], slice(0, CHUNK), nc.scalar.copy)
-        quantise_y(third, 0, slice(0, CHUNK))
-        for part in (slice(0, CHUNK // 2), slice(CHUNK // 2, CHUNK)):
-            round_y(third, CHUNK, 1, y[(third, 1)][:, :, part], part)
-        for part in (slice(0, CHUNK // 2), slice(CHUNK // 2, CHUNK)):
-            quantise_y(third, 1, part)
+        for grp in range(SPANS):
+            round_y(third, CHUNK, grp, sums[third][grp][:], slice(0, CHUNK), nc.scalar.copy)
+            quantise_y(third, grp, slice(0, CHUNK))
         hand_out(last, CHUNK, 0, 0)
         hand_out(last, CHUNK, 0, 1, nc.vector.tensor_copy)
         round_y(last, CHUNK, 0, sums[last][0][:], slice(0, CHUNK), nc.scalar.copy)

@@ -22,13 +22,15 @@ PACK = 4
 SPAN = P * PACK
 SPANS = 2
 QUADS = 4
+QUAD = P // QUADS
+ROWS = 4
+SPREAD = QUAD // (ROWS * SPANS)
 BANK = 512
 CHUNK = BANK // PACK
+DOUBLE = 2 * CHUNK
 LINE = 16
 PER_COLUMN = 16
-SPREAD = P // (4 * QUADS)
 TABLE_BYTES = 4 * T
-AHEAD = 2
 
 
 def tile_list_malware_pair_family_kernel(
@@ -46,12 +48,22 @@ def tile_list_malware_pair_family_kernel(
         def bank(index, shape, name):
             return psum.tile(shape, F32, name=name, tag="bank%d" % index)
 
+        def staged(offset):
+            return lambda shape, dtype, name: stage.tile(shape, dtype, name=name, tag=name, offset=offset, align_bytes=64)
+
+        def two_parts(width):
+            return slice(0, width // 2), slice(width // 2, width)
+
+        def carry(planes, rows, step):
+            for q in range(QUADS):
+                nc.sync.dma_start(
+                    planes[QUAD * q : QUAD * q + ROWS, :, :].bitcast(I32),
+                    rows[QUAD * q : QUAD * (q + 1) : step, :].bitcast(I32),
+                )
+
         offs_sb = keep.tile([P, S // PER_COLUMN], U16, name="offs_sb")
         pos1_sb = keep.tile([P, PAIRS // PER_COLUMN], U16, name="pos1_sb")
         pos2_sb = keep.tile([P, PAIRS // PER_COLUMN], U16, name="pos2_sb")
-
-        def staged(offset):
-            return lambda shape, dtype, name: stage.tile(shape, dtype, name=name, tag=name, offset=offset, align_bytes=64)
 
         tab_rows = staged(TABLE_BYTES)([P, T], U8, "tab_rows")
         nc.vector.memset(tab_rows[:].bitcast(I32), 0)
@@ -59,7 +71,7 @@ def tile_list_malware_pair_family_kernel(
         nc.vector.memset(picked_planes[:].rearrange("p a s -> p (a s)").bitcast(I32), 0)
         w4_planes = kept([P, SPANS * N], U8, "w4_planes")
         nc.vector.memset(w4_planes[:].bitcast(I32), 0)
-        w4_rows = kept([P, N], U8, "w4_rows")
+        w4_rows = kept([P, SPAN], U8, "w4_rows")
         nc.vector.memset(w4_rows[:].bitcast(I32), 0)
 
         def load_w1(make_tile, b, a, c0, width):
@@ -74,29 +86,27 @@ def tile_list_malware_pair_family_kernel(
         nc.sync.dma_start(offs_sb[:], offs)
         nc.sync.dma_start(pos1_sb[:], pos1)
         nc.sync.dma_start(pos2_sb[:], pos2)
-        nc.sync.dma_start(tab_rows[0:P:4, :].bitcast(I32), tab_scales.rearrange("a q t -> q a t").bitcast(I32))
+        nc.sync.dma_start(tab_rows[0:P:SPREAD, :].bitcast(I32), tab_scales.rearrange("a q t -> q a t").bitcast(I32))
         nc.sync.dma_start(table[0][:, T // 2 :], table_hbm[0][:, T // 2 :])
         raw = {(0, a): [load_w1(kept, 0, a, 0, SPAN)] for a in range(SPANS)}
 
         picked_rows = kept([P, S], U8, "picked_rows")
         nc.vector.tensor_copy(picked_rows[:], tab_rows[:].indirect(offs_sb[:]))
-        for q in range(QUADS):
-            nc.sync.dma_start(
-                picked_planes[32 * q : 32 * q + 4, :, :].bitcast(I32),
-                picked_rows[32 * q : 32 * q + 32 : 4, :].bitcast(I32),
-            )
+        carry(picked_planes, picked_rows, SPREAD)
         table.append(staged(TABLE_BYTES)([P, T], I32, "table1"))
         nc.sync.dma_start(table[1][:], table_hbm[1])
         picked = [kept([P, S], U32, "picked%d" % a) for a in range(SPANS)]
         nc.vector.tensor_copy(picked[0][:], table[0][:].bitcast(U32).indirect(offs_sb[:]))
 
+        last_half_at = TABLE_BYTES // 2 + 4 * PACK * SPAN // 2
         raw[(1, 0)] = [load_w1(staged(0), 1, 0, 0, SPAN)]
-        raw[(1, 1)] = [load_w1(staged(TABLE_BYTES // 2 + 4 * PACK * c0), 1, 1, c0, SPAN // 2) for c0 in (0, SPAN // 2)]
+        raw[(1, 1)] = [
+            load_w1(staged(offset), 1, 1, c0, SPAN // 2) for c0, offset in ((0, TABLE_BYTES // 2), (SPAN // 2, last_half_at))
+        ]
 
-        w1_codes = {}
         w1_planes = kept([P, SPANS, SPANS, PACK, P], U8, "w1_planes")
-
-        dealt = {}
+        w1_codes, dealt = {}, {}
+        whole, (low, high) = slice(0, PACK), two_parts(PACK)
 
         def cast_w1(b, a, piece, slices, copy):
             if (b, a) not in dealt:
@@ -106,9 +116,9 @@ def tile_list_malware_pair_family_kernel(
             dst = dealt[(b, a)][:, slices, c0 // PACK : (c0 + width) // PACK, :].rearrange("p t m j -> p m j t")
             copy(dst, src)
 
-        def quantise_w1(b, a, slices, make=kept):
+        def quantise_w1(b, a, slices, make_tile=kept):
             count = slices.stop - slices.start
-            codes = make([P, count, P], U32, "w1_codes%d%d%d" % (b, a, slices.start))
+            codes = make_tile([P, count, P], U32, "w1_codes%d%d%d" % (b, a, slices.start))
             nc.vector.quantize_mx(
                 out=codes[:].rearrange("p t m -> p (t m)").bitcast(E4M3),
                 scales=w1_planes[:, b, a, slices, :].rearrange("p t m -> p (t m)"),
@@ -117,23 +127,19 @@ def tile_list_malware_pair_family_kernel(
             for u in range(count):
                 w1_codes[(b, a, slices.start + u)] = codes[:, u, :]
 
-        whole, low, high = slice(0, PACK), slice(0, PACK // 2), slice(PACK // 2, PACK)
-
-        RUN = 4
         halves = range(S // BANK)
 
-        def first_pass(b, a, order):
-            for t, half in order:
-                cols = slice(half * BANK, (half + 1) * BANK)
-                nc.tensor.matmul_mx(
-                    out=accs[b][(t, half)][:],
-                    lhsT=w1_codes[(b, a, t)].bitcast(E4M3),
-                    lhsT_scale=w1_planes[:, b, a, t, :],
-                    rhs=picked[a][:, cols].bitcast(E4M3),
-                    rhs_scale=picked_planes[:, a, cols],
-                    start=(a == 0),
-                    stop=(a == SPANS - 1),
-                )
+        def first_pass(b, a, t, half):
+            cols = slice(half * BANK, (half + 1) * BANK)
+            nc.tensor.matmul_mx(
+                out=accs[b][(t, half)][:],
+                lhsT=w1_codes[(b, a, t)].bitcast(E4M3),
+                lhsT_scale=w1_planes[:, b, a, t, :],
+                rhs=picked[a][:, cols].bitcast(E4M3),
+                rhs_scale=picked_planes[:, a, cols],
+                start=(a == 0),
+                stop=(a == SPANS - 1),
+            )
 
         by_slice = list(product(range(PACK), halves))
         by_pair = [(t0 + t, half) for t0, half, t in product(range(0, PACK, 2), halves, range(2))]
@@ -142,20 +148,26 @@ def tile_list_malware_pair_family_kernel(
         ]
         cast_w1(0, 0, raw[(0, 0)][0], whole, nc.scalar.copy)
         quantise_w1(0, 0, whole)
-        first_pass(0, 0, by_pair)
+        for t, half in by_pair:
+            first_pass(0, 0, t, half)
         w4_raw = kept([P, SPANS, 2 * N], U8, "w4_raw", tag="w1_raw00_0")
         nc.sync.dma_start(w4_raw[:].bitcast(I32), w4_words.rearrange("a p c -> p a c").bitcast(I32))
         gain = kept([P, SPANS, PACK], F32, "gain", tag="dealt00")
         nc.sync.dma_start(gain[:], g.rearrange("(b p t) -> p b t", b=SPANS, t=PACK))
         cast_w1(0, 1, raw[(0, 1)][0], whole, nc.scalar.copy)
         quantise_w1(0, 1, whole)
-        nc.sync.dma_start(w4_rows[0:P:4, :].bitcast(I32), w4_scales.rearrange("a q c -> q a c").bitcast(I32))
+        for a in range(SPANS):
+            nc.sync.dma_start(
+                w4_rows[SPREAD // SPANS * a : P : SPREAD, :].bitcast(I32),
+                w4_scales[a].rearrange("q (x c) -> (q x) c", c=SPAN).bitcast(I32),
+            )
         for half in halves:
             nc.vector.tensor_copy(
                 picked[1][:, half * BANK : (half + 1) * BANK],
                 table[1][:].bitcast(U32).indirect(offs_sb[:, half * BANK // PER_COLUMN : (half + 1) * BANK // PER_COLUMN]),
             )
-        first_pass(0, 1, by_pair)
+        for t, half in by_pair:
+            first_pass(0, 1, t, half)
 
         h = {}
         first_sample = [
@@ -180,26 +192,23 @@ def tile_list_malware_pair_family_kernel(
         for slices in (low, high):
             cast_w1(1, 1, raw[(1, 1)][1], slices, nc.vector.tensor_copy)
         quantise_w1(1, 1, low)
-        quantise_w1(1, 0, high, staged(3 * TABLE_BYTES // 4))
+        quantise_w1(1, 0, high, staged(last_half_at))
         quantise_w1(1, 1, high)
-        for step in by_slice:
-            for a in range(SPANS):
-                first_pass(1, a, [step])
+        for (t, half), a in product(by_slice, range(SPANS)):
+            first_pass(1, a, t, half)
         pick_first(0)
-        w4_dealt_rows = kept([P, N], U8, "w4_dealt_rows")
+
+        w4_dealt_rows = kept([P, SPAN], U8, "w4_dealt_rows")
         nc.vector.tensor_copy(
-            w4_dealt_rows[:].rearrange("p (x t c i) -> p x c t i", x=SPANS, t=PACK, i=LINE),
-            w4_rows[:].rearrange("p (x c i t) -> p x c t i", x=SPANS, t=PACK, i=LINE),
+            w4_dealt_rows[:].rearrange("p (t c i) -> p c t i", t=PACK, i=LINE),
+            w4_rows[:].rearrange("p (c i t) -> p c t i", t=PACK, i=LINE),
         )
-        for q in range(QUADS):
-            nc.sync.dma_start(
-                w4_planes[32 * q : 32 * q + 4, :].rearrange("p (x c) -> p x c", c=N).bitcast(I32),
-                w4_dealt_rows[32 * q : 32 * q + 32 : 4, :].bitcast(I32),
-            )
+        carry(w4_planes[:].rearrange("p (x c) -> p x c", c=SPAN), w4_dealt_rows, SPREAD // SPANS)
         w4_codes = kept([P, SPANS, 2 * N], U8, "w4_codes")
+        words_in, words_out = (words[:].rearrange("p a c -> p (a c)").bitcast(U16) for words in (w4_raw, w4_codes))
         nc.vector.tensor_copy(
-            w4_codes[:].rearrange("p a c -> p (a c)").bitcast(U16).rearrange("p (x t c i) -> p x c t i", x=SPANS * SPANS, t=PACK, i=LINE // 2),
-            w4_raw[:].rearrange("p a c -> p (a c)").bitcast(U16).rearrange("p (x c i t) -> p x c t i", x=SPANS * SPANS, t=PACK, i=LINE // 2),
+            words_out.rearrange("p (x t c i) -> p x c t i", x=SPANS * SPANS, t=PACK, i=LINE // 2),
+            words_in.rearrange("p (x c i t) -> p x c t i", x=SPANS * SPANS, t=PACK, i=LINE // 2),
         )
         inv_gain = kept([P, SPANS, PACK], F32, "inv_gain")
         nc.vector.reciprocal(inv_gain[:], gain[:])
@@ -208,11 +217,16 @@ def tile_list_malware_pair_family_kernel(
         sigmoids(1, by_slice)
         pick_first(1)
 
-        double, third, last = 2 * CHUNK, 2 * CHUNK, 3 * CHUNK
-        units = [(0, 0, double), (1, 0, double), (0, third, double), (1, third, CHUNK), (1, last, CHUNK)]
-        inverse, forward, backward = {}, {}, {}
-        z_codes = {}
+        third, last = 2 * CHUNK, 3 * CHUNK
+        units = [(0, 0, DOUBLE), (1, 0, DOUBLE), (0, third, DOUBLE), (1, third, CHUNK), (1, last, CHUNK)]
+        inverse, forward, backward, z_codes = {}, {}, {}, {}
         z_planes = kept([P, SPANS, PAIRS], U8, "z_planes")
+
+        def interleaved(view):
+            return view.rearrange("p (c i) t -> p c t i", i=LINE // 4)
+
+        def by_lines(view):
+            return view.rearrange("p t (c i) -> p c t i", i=LINE // 4)
 
         def root_first(b):
             roots = kept([P, PACK, PAIRS], F32, "inverse%d" % b, tag="picked%d" % b)
@@ -222,12 +236,10 @@ def tile_list_malware_pair_family_kernel(
                 if span == b:
                     inverse[n] = roots[:, :, j0 : j0 + width]
 
-        def invert(n, groups=(whole,)):
+        def invert_and_pick(n, groups=(whole,)):
+            b, j0, width = units[n]
             for slices in groups:
                 nc.scalar.activation(inverse[n][:, slices, :], inverse[n][:, slices, :], ACT.Square)
-
-        def pick_second(n):
-            b, j0, width = units[n]
             forward[n] = kept([P, PACK, width], F32, "forward%d" % n)
             cols = slice(j0 // PER_COLUMN, (j0 + width) // PER_COLUMN)
             for t in range(PACK):
@@ -244,31 +256,27 @@ def tile_list_malware_pair_family_kernel(
         def second_pass(a, j0):
             for grp, t in product(range(SPANS), range(PACK)):
                 c0 = SPAN * grp + P * t
+                s0 = SPAN * (SPANS * grp + a) + P * t
                 nc.tensor.matmul_mx(
                     out=sums[j0][grp][:, t, :],
                     lhsT=w4_codes[:, a, 2 * c0 : 2 * (c0 + P)].bitcast(E2M1),
-                    lhsT_scale=w4_planes[:, a * N + c0 : a * N + c0 + P],
+                    lhsT_scale=w4_planes[:, s0 : s0 + P],
                     rhs=z_codes[(a, j0)].bitcast(E4M3),
                     rhs_scale=z_planes[:, a, j0 : j0 + CHUNK],
                     start=(a == 0 and t == 0),
                     stop=(a == SPANS - 1 and t == PACK - 1),
                 )
 
-        def agree(n, count, groups=(whole,)):
+        def agree(n):
             b, j0, width = units[n]
-            for slices in groups:
-                nc.scalar.activation(backward[n][:, slices, :], backward[n][:, slices, :], ACT.Square)
-            parts = [slice(c0, c0 + width // count) for c0 in range(0, width, width // count)]
+            nc.scalar.activation(backward[n][:], backward[n][:], ACT.Square)
             z = kept([P, width, PACK], BF16, "z%d" % n)
-            for part in parts:
+            for part in two_parts(width):
                 nc.vector.tensor_tensor(
-                    z[:, part, :].rearrange("p (c i) t -> p c t i", i=RUN),
-                    forward[n][:, :, part].rearrange("p t (c i) -> p c t i", i=RUN),
-                    backward[n][:, :, part].rearrange("p t (c i) -> p c t i", i=RUN),
-                    ALU.min,
+                    interleaved(z[:, part, :]), by_lines(forward[n][:, :, part]), by_lines(backward[n][:, :, part]), ALU.min
                 )
             codes = kept([P, width], U32, "z_codes%d" % n)
-            for part in parts:
+            for part in two_parts(width):
                 nc.vector.quantize_mx(
                     out=codes[:, part].bitcast(E4M3),
                     scales=z_planes[:, b, j0 + part.start : j0 + part.stop],
@@ -279,93 +287,75 @@ def tile_list_malware_pair_family_kernel(
                 second_pass(b, j0 + c0)
 
         y_planes = kept([P, SPANS, PAIRS], U8, "y_planes")
-
         y, rounded = {}, {}
 
-        def hand_out(j0, width, c0, grp, copy=nc.scalar.copy):
-            if c0 == 0:
-                y[(j0, grp)] = kept([P, PACK, width], F32, "y%d_%d" % (j0, grp))
-            copy(y[(j0, grp)][:, :, c0 : c0 + CHUNK], sums[j0 + c0][grp][:])
-            if c0 + CHUNK == width:
-                nc.sync.dma_start(
-                    out_0[SPAN * grp : SPAN * (grp + 1), j0 : j0 + width].rearrange("(p t) j -> p t j", t=PACK), y[(j0, grp)][:]
-                )
+        def hand_out(j0, width, grp, copy=nc.scalar.copy):
+            y[(j0, grp)] = kept([P, PACK, width], F32, "y%d_%d" % (j0, grp))
+            for c0 in range(0, width, CHUNK):
+                copy(y[(j0, grp)][:, :, c0 : c0 + CHUNK], sums[j0 + c0][grp][:])
+            nc.sync.dma_start(
+                out_0[SPAN * grp : SPAN * (grp + 1), j0 : j0 + width].rearrange("(p t) j -> p t j", t=PACK), y[(j0, grp)][:]
+            )
 
-        def round_y(j0, width, grp, src, part, copy=nc.vector.tensor_copy):
+        def round_y(j0, width, grp, part, from_bank):
             if (j0, grp) not in rounded:
                 rounded[(j0, grp)] = kept([P, width, PACK], BF16, "rounded%d_%d" % (j0, grp))
-            copy(
-                rounded[(j0, grp)][:, part, :].rearrange("p (c i) t -> p c t i", i=RUN),
-                src.rearrange("p t (c i) -> p c t i", i=RUN),
-            )
+            dst = interleaved(rounded[(j0, grp)][:, part, :])
+            if from_bank:
+                nc.scalar.copy(dst, by_lines(sums[j0 + part.start][grp][:]))
+            else:
+                nc.vector.tensor_copy(dst, by_lines(y[(j0, grp)][:, :, part]))
 
-        def quantise_y(j0, grp, part):
-            nc.vector.quantize_mx(
-                out=y_codes[j0 // double * double][:, grp, j0 % double + part.start : j0 % double + part.stop].bitcast(E4M3),
-                scales=y_planes[:, grp, j0 + part.start : j0 + part.stop],
-                in_=rounded[(j0, grp)][:, part, :].rearrange("p j t -> p (j t)"),
-            )
+        def requantise(j0, width, grp, parts):
+            for part, from_bank in parts:
+                round_y(j0, width, grp, part, from_bank)
+            base = j0 % DOUBLE
+            for part, from_bank in parts:
+                nc.vector.quantize_mx(
+                    out=y_codes[j0 - base][:, grp, base + part.start : base + part.stop].bitcast(E4M3),
+                    scales=y_planes[:, grp, j0 + part.start : j0 + part.stop],
+                    in_=rounded[(j0, grp)][:, part, :].rearrange("p j t -> p (j t)"),
+                )
 
-        def store_codes(j0, width, queue):
-            queue.dma_start(out_1[:, :, j0 : j0 + width, :].rearrange("g p m i -> p g (m i)").bitcast(I32), y_codes[j0][:])
+        def store_codes(j0, queue):
+            queue.dma_start(out_1[:, :, j0 : j0 + DOUBLE, :].rearrange("g p m i -> p g (m i)").bitcast(I32), y_codes[j0][:])
 
         sums = {
             j0: [bank(SPANS * (j0 // CHUNK) + grp, [P, PACK, CHUNK], "sums") for grp in range(SPANS)]
             for j0 in range(0, PAIRS, CHUNK)
         }
-        y_codes = {j0: kept([P, SPANS, double], I32, "y_codes%d" % j0) for j0 in (0, double)}
-        root_first(0)
-        invert(0, (low, high))
-        pick_second(0)
-        root_first(1)
-        invert(1, (low, high))
-        pick_second(1)
-        root_second(0)
-        invert(2)
-        pick_second(2)
-        agree(0, 2)
-        root_second(1)
-        invert(3)
-        pick_second(3)
-        agree(1, 2)
-        invert(4)
-        pick_second(4)
-        root_second(2)
-        root_second(3)
-        agree(2, 2)
-        agree(3, 2)
-        hand_out(0, double, 0, 0)
-        hand_out(0, double, CHUNK, 0)
+        y_codes = {j0: kept([P, SPANS, DOUBLE], I32, "y_codes%d" % j0) for j0 in range(0, PAIRS, DOUBLE)}
+
+        for n in range(SPANS):
+            root_first(n)
+            invert_and_pick(n, (low, high))
+        for n in range(SPANS):
+            root_second(n)
+            invert_and_pick(n + 2)
+            agree(n)
+        invert_and_pick(4)
+        for step in (root_second, agree):
+            for n in (2, 3):
+                step(n)
+        hand_out(0, DOUBLE, 0)
         root_second(4)
-        hand_out(0, double, 0, 1)
-        hand_out(0, double, CHUNK, 1)
-        agree(4, 2)
-        for part in (slice(0, double // 2), slice(double // 2, double)):
-            round_y(0, double, 0, y[(0, 0)][:, :, part], part)
-        for part in (slice(0, double // 2), slice(double // 2, double)):
-            quantise_y(0, 0, part)
-        round_y(0, double, 1, y[(0, 1)][:, :, :CHUNK], slice(0, CHUNK))
-        round_y(0, double, 1, sums[CHUNK][1][:], slice(CHUNK, double), nc.scalar.copy)
-        for part in (slice(0, CHUNK), slice(CHUNK, double)):
-            quantise_y(0, 1, part)
-        store_codes(0, double, nc.sync)
-        for grp in range(SPANS):
-            hand_out(third, CHUNK, 0, grp)
-        for grp in range(SPANS):
-            round_y(third, CHUNK, grp, sums[third][grp][:], slice(0, CHUNK), nc.scalar.copy)
-            quantise_y(third, grp, slice(0, CHUNK))
-        hand_out(last, CHUNK, 0, 0)
-        hand_out(last, CHUNK, 0, 1, nc.vector.tensor_copy)
-        round_y(last, CHUNK, 0, sums[last][0][:], slice(0, CHUNK), nc.scalar.copy)
-        quantise_y(last, 0, slice(0, CHUNK))
-        for part in (slice(0, CHUNK // 2), slice(CHUNK // 2, CHUNK)):
-            round_y(last, CHUNK, 1, y[(last, 1)][:, :, part], part)
-        for part in (slice(0, CHUNK // 2), slice(CHUNK // 2, CHUNK)):
-            quantise_y(last, 1, part)
-        store_codes(double, double, nc.scalar)
+        hand_out(0, DOUBLE, 1)
+        agree(4)
+        first_chunk, second_chunk = two_parts(DOUBLE)
+        on_scalar = [(slice(0, CHUNK), True)]
+        on_vector = [(part, False) for part in two_parts(CHUNK)]
+        requantise(0, DOUBLE, 0, [(first_chunk, False), (second_chunk, False)])
+        requantise(0, DOUBLE, 1, [(first_chunk, False), (second_chunk, True)])
+        store_codes(0, nc.sync)
+        for j0, second_copy, second_round in ((third, nc.scalar.copy, on_scalar), (last, nc.vector.tensor_copy, on_vector)):
+            hand_out(j0, CHUNK, 0)
+            hand_out(j0, CHUNK, 1, second_copy)
+            requantise(j0, CHUNK, 0, on_scalar)
+            requantise(j0, CHUNK, 1, second_round)
+        store_codes(DOUBLE, nc.scalar)
         for q in range(QUADS):
             queue = nc.scalar if q % 2 else nc.sync
             queue.dma_start(
-                out_2[:, 4 * q : 4 * q + 4, :].rearrange("g r m -> r g m").bitcast(I32),
-                y_planes[32 * q : 32 * q + 4, :, :].bitcast(I32),
+                out_2[:, ROWS * q : ROWS * (q + 1), :].rearrange("g r m -> r g m").bitcast(I32),
+                y_planes[QUAD * q : QUAD * q + ROWS, :, :].bitcast(I32),
             )

@@ -54,11 +54,11 @@ def tile_list_malware_pair_family_kernel(
         def two_parts(width):
             return slice(0, width // 2), slice(width // 2, width)
 
-        def carry(planes, rows, step):
-            for q in range(QUADS):
+        def carry(planes, rows, step, first=0):
+            for q in (0, 2, 1, 3):
                 nc.sync.dma_start(
                     planes[QUAD * q : QUAD * q + ROWS, :, :].bitcast(I32),
-                    rows[QUAD * q : QUAD * (q + 1) : step, :].bitcast(I32),
+                    rows[QUAD * q + first : QUAD * (q + 1) : step, :].bitcast(I32),
                 )
 
         offs_sb = keep.tile([P, S // PER_COLUMN], U16, name="offs_sb")
@@ -92,9 +92,10 @@ def tile_list_malware_pair_family_kernel(
 
         picked_rows = kept([P, S], U8, "picked_rows")
         nc.vector.tensor_copy(picked_rows[:], tab_rows[:].indirect(offs_sb[:]))
-        carry(picked_planes, picked_rows, SPREAD)
+        carry(picked_planes[:, 0:1, :], picked_rows[:], SPANS * SPREAD)
         table.append(staged(TABLE_BYTES)([P, T], I32, "table1"))
         nc.sync.dma_start(table[1][:], table_hbm[1])
+        carry(picked_planes[:, 1:2, :], picked_rows[:], SPANS * SPREAD, SPREAD)
         picked = [kept([P, S], U32, "picked%d" % a) for a in range(SPANS)]
         nc.vector.tensor_copy(picked[0][:], table[0][:].bitcast(U32).indirect(offs_sb[:]))
 

@@ -128,29 +128,32 @@ def tile_list_malware_pair_family_kernel(
             for u in range(count):
                 w1_codes[(b, a, slices.start + u)] = codes[:, u, :]
 
-        halves = range(S // BANK)
+        def first_pass(b, a, group):
+            acc, sums = group
+            for u, (t, cols) in enumerate(sums):
+                width = cols.stop - cols.start
+                nc.tensor.matmul_mx(
+                    out=acc[:, u * width : (u + 1) * width],
+                    lhsT=w1_codes[(b, a, t)].bitcast(E4M3),
+                    lhsT_scale=w1_planes[:, b, a, t, :],
+                    rhs=picked[a][:, cols].bitcast(E4M3),
+                    rhs_scale=picked_planes[:, a, cols],
+                    start=(a == 0 and u == 0),
+                    stop=(a == SPANS - 1 and u == len(sums) - 1),
+                )
 
-        def first_pass(b, a, t, half):
-            cols = slice(half * BANK, (half + 1) * BANK)
-            nc.tensor.matmul_mx(
-                out=accs[b][(t, half)][:],
-                lhsT=w1_codes[(b, a, t)].bitcast(E4M3),
-                lhsT_scale=w1_planes[:, b, a, t, :],
-                rhs=picked[a][:, cols].bitcast(E4M3),
-                rhs_scale=picked_planes[:, a, cols],
-                start=(a == 0),
-                stop=(a == SPANS - 1),
-            )
-
-        by_slice = list(product(range(PACK), halves))
-        by_pair = [(t0 + t, half) for t0, half, t in product(range(0, PACK, 2), halves, range(2))]
-        accs = [
-            {(t, half): bank(2 * t + half, [P, BANK], "acc%d" % b) for t in range(PACK) for half in halves} for b in range(SPANS)
+        first_half, second_half = two_parts(S)
+        quarters = two_parts(BANK)
+        contents = [
+            [[(t0, cols), (t0 + 1, cols)] for cols, t0 in product(quarters, range(0, PACK, 2))]
+            + [[(t, second_half)] for t in range(PACK)],
+            [[(t, cols)] for t, cols in product(range(PACK), (first_half, second_half))],
         ]
+        groups = [[(bank(u, [P, BANK], "acc%d" % b), sums) for u, sums in enumerate(contents[b])] for b in range(SPANS)]
         cast_w1(0, 0, raw[(0, 0)][0], whole, nc.scalar.copy)
         quantise_w1(0, 0, whole)
-        for t, half in by_pair:
-            first_pass(0, 0, t, half)
+        for group in groups[0]:
+            first_pass(0, 0, group)
         w4_raw = kept([P, SPANS, 2 * N], U8, "w4_raw", tag="w1_raw00_0")
         nc.sync.dma_start(w4_raw[:].bitcast(I32), w4_words.rearrange("a p c -> p a c").bitcast(I32))
         gain = kept([P, SPANS, PACK], F32, "gain", tag="dealt00")
@@ -162,41 +165,46 @@ def tile_list_malware_pair_family_kernel(
                 w4_rows[SPREAD // SPANS * a : P : SPREAD, :].bitcast(I32),
                 w4_scales[a].rearrange("q (x c) -> (q x) c", c=SPAN).bitcast(I32),
             )
-        for half in halves:
+        for cols in quarters + (second_half,):
             nc.vector.tensor_copy(
-                picked[1][:, half * BANK : (half + 1) * BANK],
-                table[1][:].bitcast(U32).indirect(offs_sb[:, half * BANK // PER_COLUMN : (half + 1) * BANK // PER_COLUMN]),
+                picked[1][:, cols],
+                table[1][:].bitcast(U32).indirect(offs_sb[:, cols.start // PER_COLUMN : cols.stop // PER_COLUMN]),
             )
-        for t, half in by_pair:
-            first_pass(0, 1, t, half)
+        for group in groups[0]:
+            first_pass(0, 1, group)
 
         h = {}
         first_sample = [
             kept([P, PACK, PAIRS], F32, "first_sample%d" % b, tag=tag) for b, tag in enumerate(("dealt11", "w1_raw01_0"))
         ]
 
-        def sigmoids(b, order):
+        def sigmoids(b):
             for t in range(PACK):
                 h[(b, t)] = kept([P, S], F32, "h%d%d" % (b, t))
-            for t, half in order:
-                nc.scalar.activation(h[(b, t)][:, half * BANK : (half + 1) * BANK], accs[b][(t, half)][:], ACT.Sigmoid)
+            for acc, sums in groups[b]:
+                for u, (t, cols) in enumerate(sums):
+                    width = cols.stop - cols.start
+                    nc.scalar.activation(h[(b, t)][:, cols], acc[:, u * width : (u + 1) * width], ACT.Sigmoid)
 
         def pick_first(b):
             for t in range(PACK):
                 nc.vector.tensor_copy(first_sample[b][:, t, :], h[(b, t)][:].indirect(pos1_sb[:]))
 
-        sigmoids(0, by_pair)
+        sigmoids(0)
         for slices in (low, high):
             cast_w1(1, 0, raw[(1, 0)][0], slices, nc.vector.tensor_copy)
-        quantise_w1(1, 0, low)
+        first_slice, second_slice = two_parts(PACK // 2)
+        quantise_w1(1, 0, first_slice)
         cast_w1(1, 1, raw[(1, 1)][0], whole, nc.vector.tensor_copy)
         for slices in (low, high):
             cast_w1(1, 1, raw[(1, 1)][1], slices, nc.vector.tensor_copy)
-        quantise_w1(1, 1, low)
-        quantise_w1(1, 0, high, staged(last_half_at))
+        quantise_w1(1, 1, first_slice)
+        quantise_w1(1, 0, second_slice, staged(last_half_at))
+        quantise_w1(1, 1, second_slice)
+        quantise_w1(1, 0, high, staged(last_half_at + 4 * P))
         quantise_w1(1, 1, high)
-        for (t, half), a in product(by_slice, range(SPANS)):
-            first_pass(1, a, t, half)
+        for group, a in product(groups[1], range(SPANS)):
+            first_pass(1, a, group)
         pick_first(0)
 
         w4_dealt_rows = kept([P, SPAN], U8, "w4_dealt_rows")
@@ -215,7 +223,7 @@ def tile_list_malware_pair_family_kernel(
         nc.vector.reciprocal(inv_gain[:], gain[:])
         inv_gain2 = kept([P, SPANS, PACK], F32, "inv_gain2")
         nc.vector.tensor_tensor(inv_gain2[:], inv_gain[:], inv_gain[:], ALU.mult)
-        sigmoids(1, by_slice)
+        sigmoids(1)
         pick_first(1)
 
         third, last = 2 * CHUNK, 3 * CHUNK

@@ -111,7 +111,7 @@ def tile_list_malware_pair_family_kernel(
 
         def cast_w1(b, a, piece, slices, copy):
             if (b, a) not in dealt:
-                dealt[(b, a)] = kept([P, PACK, P, PACK], BF16, "dealt%d%d" % (b, a))
+                dealt[(b, a)] = kept([P, PACK, P, PACK], BF16, "dealt%d%d" % (b, a), tag="dealt%d%d" % (b, a * b))
             rows, c0, width = piece
             src = rows.rearrange("p j (m t) -> p m j t", t=PACK)[:, :, :, slices]
             dst = dealt[(b, a)][:, slices, c0 // PACK : (c0 + width) // PACK, :].rearrange("p t m j -> p m j t")
@@ -156,10 +156,10 @@ def tile_list_malware_pair_family_kernel(
             first_pass(0, 0, group)
         w4_raw = kept([P, SPANS, 2 * N], U8, "w4_raw", tag="w1_raw00_0")
         nc.sync.dma_start(w4_raw[:].bitcast(I32), w4_words.rearrange("a p c -> p a c").bitcast(I32))
+        cast_w1(0, 1, raw[(0, 1)][0], whole, nc.vector.tensor_copy)
         gain = kept([P, SPANS, PACK], F32, "gain", tag="dealt00")
-        nc.sync.dma_start(gain[:], g.rearrange("(b p t) -> p b t", b=SPANS, t=PACK))
-        cast_w1(0, 1, raw[(0, 1)][0], whole, nc.scalar.copy)
         quantise_w1(0, 1, whole)
+        nc.sync.dma_start(gain[:], g.rearrange("(b p t) -> p b t", b=SPANS, t=PACK))
         for a in range(SPANS):
             nc.sync.dma_start(
                 w4_rows[SPREAD // SPANS * a : P : SPREAD, :].bitcast(I32),

@@ -175,7 +175,7 @@ def tile_list_malware_pair_family_kernel(
 
         h = {}
         first_sample = [
-            kept([P, PACK, PAIRS], F32, "first_sample%d" % b, tag=tag) for b, tag in enumerate(("dealt11", "w1_raw01_0"))
+            kept([P, PACK, PAIRS], F32, "first_sample%d" % b, tag=tag) for b, tag in enumerate(("dealt10", "w1_raw01_0"))
         ]
 
         def sigmoids(b):
@@ -315,11 +315,11 @@ def tile_list_malware_pair_family_kernel(
             else:
                 nc.vector.tensor_copy(dst, by_lines(y[(j0, grp)][:, :, part]))
 
-        def requantise(j0, width, grp, parts):
+        def requantise(j0, width, grp, parts, calls=None):
             for part, from_bank in parts:
                 round_y(j0, width, grp, part, from_bank)
             base = j0 % DOUBLE
-            for part, from_bank in parts:
+            for part in calls or [part for part, from_bank in parts]:
                 nc.vector.quantize_mx(
                     out=y_codes[j0 - base][:, grp, base + part.start : base + part.stop].bitcast(E4M3),
                     scales=y_planes[:, grp, j0 + part.start : j0 + part.stop],
@@ -354,7 +354,7 @@ def tile_list_malware_pair_family_kernel(
         on_scalar = [(slice(0, CHUNK), True)]
         on_vector = [(part, False) for part in two_parts(CHUNK)]
         requantise(0, DOUBLE, 0, [(first_chunk, False), (second_chunk, False)])
-        requantise(0, DOUBLE, 1, [(first_chunk, False), (second_chunk, True)])
+        requantise(0, DOUBLE, 1, [(first_chunk, False), (second_chunk, True)], [slice(0, DOUBLE)])
         store_codes(0, nc.sync)
         for j0, second_copy, second_round in ((third, nc.scalar.copy, on_scalar), (last, nc.vector.tensor_copy, on_vector)):
             hand_out(j0, CHUNK, 0)

@@ -111,7 +111,10 @@ def tile_list_malware_pair_family_kernel(
 
         def cast_w1(b, a, piece, slices, copy):
             if (b, a) not in dealt:
-                dealt[(b, a)] = kept([P, PACK, P, PACK], BF16, "dealt%d%d" % (b, a), tag="dealt%d%d" % (b, a * b))
+                if a * b:
+                    dealt[(b, a)] = staged(TABLE_BYTES)([P, PACK, P, PACK], BF16, "dealt11")
+                else:
+                    dealt[(b, a)] = kept([P, PACK, P, PACK], BF16, "dealt%d%d" % (b, a), tag="dealt%d0" % b)
             rows, c0, width = piece
             src = rows.rearrange("p j (m t) -> p m j t", t=PACK)[:, :, :, slices]
             dst = dealt[(b, a)][:, slices, c0 // PACK : (c0 + width) // PACK, :].rearrange("p t m j -> p m j t")
@@ -207,22 +210,22 @@ def tile_list_malware_pair_family_kernel(
             first_pass(1, a, group)
         pick_first(0)
 
-        w4_dealt_rows = kept([P, SPAN], U8, "w4_dealt_rows")
-        nc.vector.tensor_copy(
+        w4_dealt_rows = staged(TABLE_BYTES)([P, SPAN], U8, "w4_dealt_rows")
+        nc.gpsimd.tensor_copy(
             w4_dealt_rows[:].rearrange("p (t c i) -> p c t i", t=PACK, i=LINE),
             w4_rows[:].rearrange("p (c i t) -> p c t i", t=PACK, i=LINE),
         )
         carry(w4_planes[:].rearrange("p (x c) -> p x c", c=SPAN), w4_dealt_rows, SPREAD // SPANS)
-        w4_codes = kept([P, SPANS, 2 * N], U8, "w4_codes")
-        words_in, words_out = (words[:].rearrange("p a c -> p (a c)").bitcast(U16) for words in (w4_raw, w4_codes))
-        nc.vector.tensor_copy(
-            words_out.rearrange("p (x t c i) -> p x c t i", x=SPANS * SPANS, t=PACK, i=LINE // 2),
-            words_in.rearrange("p (x c i t) -> p x c t i", x=SPANS * SPANS, t=PACK, i=LINE // 2),
-        )
+        w4_codes = staged(TABLE_BYTES + SPAN)([P, SPANS, 2 * N], U8, "w4_codes")
+        for a in range(SPANS):
+            nc.gpsimd.tensor_copy(
+                w4_codes[:, a, :].rearrange("p (x t m e) -> p x t m e", x=SPANS, t=PACK, e=2),
+                w4_raw[:, a, :].rearrange("p (x m t e) -> p x t m e", x=SPANS, t=PACK, e=2),
+            )
         inv_gain = kept([P, SPANS, PACK], F32, "inv_gain")
         nc.vector.reciprocal(inv_gain[:], gain[:])
         inv_gain2 = kept([P, SPANS, PACK], F32, "inv_gain2")
-        nc.vector.tensor_tensor(inv_gain2[:], inv_gain[:], inv_gain[:], ALU.mult)
+        nc.gpsimd.tensor_tensor(inv_gain2[:], inv_gain[:], inv_gain[:], ALU.mult)
         sigmoids(1)
         pick_first(1)
 
@@ -239,17 +242,19 @@ def tile_list_malware_pair_family_kernel(
 
         def root_first(b):
             roots = kept([P, PACK, PAIRS], F32, "inverse%d" % b, tag="picked%d" % b)
-            for t in range(PACK):
-                nc.scalar.activation(roots[:, t, :], first_sample[b][:, t, :], ACT.Abs_reciprocal_sqrt, scale=inv_gain[:, b, t : t + 1])
             for n, (span, j0, width) in enumerate(units):
                 if span == b:
                     inverse[n] = roots[:, :, j0 : j0 + width]
+            for t in range(PACK):
+                if b == 1 and t == PACK - 1:
+                    nc.scalar.activation(inverse[1][:, low, :], inverse[1][:, low, :], ACT.Square)
+                nc.scalar.activation(roots[:, t, :], first_sample[b][:, t, :], ACT.Abs_reciprocal_sqrt, scale=inv_gain[:, b, t : t + 1])
 
         def invert_and_pick(n, groups=(whole,)):
             b, j0, width = units[n]
             for slices in groups:
                 nc.scalar.activation(inverse[n][:, slices, :], inverse[n][:, slices, :], ACT.Square)
-            forward[n] = kept([P, PACK, width], F32, "forward%d" % n)
+            forward[n] = kept([P, PACK, width], F32, "forward%d" % n, tag=("forward0", "forward1", "w1_raw01_0", "forward0", "forward1")[n])
             cols = slice(j0 // PER_COLUMN, (j0 + width) // PER_COLUMN)
             for t in range(PACK):
                 nc.vector.tensor_tensor(forward[n][:, t, :], h[(b, t)][:].indirect(pos2_sb[:, cols]), inverse[n][:, t, :], ALU.mult)
@@ -337,12 +342,16 @@ def tile_list_malware_pair_family_kernel(
 
         for n in range(SPANS):
             root_first(n)
-            invert_and_pick(n, (low, high))
+            if n == 0:
+                for slices in (low, high):
+                    nc.gpsimd.tensor_tensor(inverse[2][:, slices, :], inverse[2][:, slices, :], inverse[2][:, slices, :], ALU.mult)
+            invert_and_pick(n, (low, high)[n:])
         for n in range(SPANS):
             root_second(n)
-            invert_and_pick(n + 2)
+            if n == 0:
+                invert_and_pick(2, ())
             agree(n)
-        invert_and_pick(4)
+            invert_and_pick(n + 3)
         for step in (root_second, agree):
             for n in (2, 3):
                 step(n)

@@ -365,11 +365,16 @@ def tile_list_malware_pair_family_kernel(
         requantise(0, DOUBLE, 0, [(first_chunk, False), (second_chunk, False)])
         requantise(0, DOUBLE, 1, [(first_chunk, False), (second_chunk, True)], [slice(0, DOUBLE)])
         store_codes(0, nc.sync)
-        for j0, second_copy, second_round in ((third, nc.scalar.copy, on_scalar), (last, nc.vector.tensor_copy, on_vector)):
-            hand_out(j0, CHUNK, 0)
-            hand_out(j0, CHUNK, 1, second_copy)
-            requantise(j0, CHUNK, 0, on_scalar)
-            requantise(j0, CHUNK, 1, second_round)
+        for grp in range(SPANS):
+            hand_out(third, CHUNK, grp)
+        for grp in range(SPANS):
+            round_y(third, CHUNK, grp, slice(0, CHUNK), False)
+        for grp in range(SPANS):
+            requantise(third, CHUNK, grp, [], [slice(0, CHUNK)])
+        hand_out(last, CHUNK, 0)
+        hand_out(last, CHUNK, 1, nc.vector.tensor_copy)
+        requantise(last, CHUNK, 0, on_scalar)
+        requantise(last, CHUNK, 1, on_vector)
         store_codes(DOUBLE, nc.scalar)
         for q in range(QUADS):
             queue = nc.scalar if q % 2 else nc.sync

@@ -86,6 +86,8 @@ def tile_list_malware_pair_family_kernel(
         nc.sync.dma_start(offs_sb[:], offs)
         nc.sync.dma_start(pos1_sb[:], pos1)
         nc.sync.dma_start(pos2_sb[:], pos2)
+        gain = kept([P, SPANS, PACK], F32, "gain")
+        nc.sync.dma_start(gain[:], g.rearrange("(b p t) -> p b t", b=SPANS, t=PACK))
         nc.sync.dma_start(tab_rows[0:P:SPREAD, :].bitcast(I32), tab_scales.rearrange("a q t -> q a t").bitcast(I32))
         nc.sync.dma_start(table[0][:, T // 2 :], table_hbm[0][:, T // 2 :])
         raw = {(0, a): [load_w1(kept, 0, a, 0, SPAN)] for a in range(SPANS)}
@@ -160,9 +162,7 @@ def tile_list_malware_pair_family_kernel(
         w4_raw = kept([P, SPANS, 2 * N], U8, "w4_raw", tag="w1_raw00_0")
         nc.sync.dma_start(w4_raw[:].bitcast(I32), w4_words.rearrange("a p c -> p a c").bitcast(I32))
         cast_w1(0, 1, raw[(0, 1)][0], whole, nc.vector.tensor_copy)
-        gain = kept([P, SPANS, PACK], F32, "gain", tag="dealt00")
         quantise_w1(0, 1, whole)
-        nc.sync.dma_start(gain[:], g.rearrange("(b p t) -> p b t", b=SPANS, t=PACK))
         for a in range(SPANS):
             nc.sync.dma_start(
                 w4_rows[SPREAD // SPANS * a : P : SPREAD, :].bitcast(I32),
@@ -210,22 +210,22 @@ def tile_list_malware_pair_family_kernel(
             first_pass(1, a, group)
         pick_first(0)
 
-        w4_dealt_rows = staged(TABLE_BYTES)([P, SPAN], U8, "w4_dealt_rows")
-        nc.gpsimd.tensor_copy(
-            w4_dealt_rows[:].rearrange("p (t c i) -> p c t i", t=PACK, i=LINE),
-            w4_rows[:].rearrange("p (c i t) -> p c t i", t=PACK, i=LINE),
-        )
-        carry(w4_planes[:].rearrange("p (x c) -> p x c", c=SPAN), w4_dealt_rows, SPREAD // SPANS)
         w4_codes = staged(TABLE_BYTES + SPAN)([P, SPANS, 2 * N], U8, "w4_codes")
         for a in range(SPANS):
             nc.gpsimd.tensor_copy(
                 w4_codes[:, a, :].rearrange("p (x t m e) -> p x t m e", x=SPANS, t=PACK, e=2),
                 w4_raw[:, a, :].rearrange("p (x m t e) -> p x t m e", x=SPANS, t=PACK, e=2),
             )
+        w4_dealt_rows = staged(TABLE_BYTES)([P, SPAN], U8, "w4_dealt_rows")
+        nc.gpsimd.tensor_copy(
+            w4_dealt_rows[:].rearrange("p (t c i) -> p c t i", t=PACK, i=LINE),
+            w4_rows[:].rearrange("p (c i t) -> p c t i", t=PACK, i=LINE),
+        )
+        carry(w4_planes[:].rearrange("p (x c) -> p x c", c=SPAN), w4_dealt_rows, SPREAD // SPANS)
         inv_gain = kept([P, SPANS, PACK], F32, "inv_gain")
         nc.vector.reciprocal(inv_gain[:], gain[:])
         inv_gain2 = kept([P, SPANS, PACK], F32, "inv_gain2")
-        nc.gpsimd.tensor_tensor(inv_gain2[:], inv_gain[:], inv_gain[:], ALU.mult)
+        nc.vector.tensor_tensor(inv_gain2[:], inv_gain[:], inv_gain[:], ALU.mult)
         sigmoids(1)
         pick_first(1)
 

@@ -245,10 +245,13 @@ def tile_list_malware_pair_family_kernel(
             for n, (span, j0, width) in enumerate(units):
                 if span == b:
                     inverse[n] = roots[:, :, j0 : j0 + width]
-            for t in range(PACK):
-                if b == 1 and t == PACK - 1:
-                    nc.scalar.activation(inverse[1][:, low, :], inverse[1][:, low, :], ACT.Square)
-                nc.scalar.activation(roots[:, t, :], first_sample[b][:, t, :], ACT.Abs_reciprocal_sqrt, scale=inv_gain[:, b, t : t + 1])
+            parts = two_parts(PAIRS)[::-1] if b == 0 else (slice(0, PAIRS),)
+            for cols, t in product(parts, range(PACK)):
+                if cols.start == 0 and t == PACK - 1:
+                    nc.scalar.activation(inverse[b][:, low, :], inverse[b][:, low, :], ACT.Square)
+                nc.scalar.activation(
+                    roots[:, t, cols], first_sample[b][:, t, cols], ACT.Abs_reciprocal_sqrt, scale=inv_gain[:, b, t : t + 1]
+                )
 
         def invert_and_pick(n, groups=(whole,)):
             b, j0, width = units[n]
@@ -345,7 +348,7 @@ def tile_list_malware_pair_family_kernel(
             if n == 0:
                 for slices in (low, high):
                     nc.gpsimd.tensor_tensor(inverse[2][:, slices, :], inverse[2][:, slices, :], inverse[2][:, slices, :], ALU.mult)
-            invert_and_pick(n, (low, high)[n:])
+            invert_and_pick(n, (high,))
         for n in range(SPANS):
             root_second(n)
             if n == 0:

from contextlib import ExitStack
from itertools import product

import concourse.mybir as mybir

K, T, S, PAIRS, H, N = 1024, 4096, 1024, 512, 1024, 1024
FLOPS = 2 * K * H * S + 2 * H * N * PAIRS

F32 = mybir.dt.float32
BF16 = mybir.dt.bfloat16
I32 = mybir.dt.int32
U32 = mybir.dt.uint32
U16 = mybir.dt.uint16
U8 = mybir.dt.uint8
E4M3 = mybir.dt.float8_e4m3fn_x4
E2M1 = mybir.dt.float4_e2m1fn_x4
ACT = mybir.ActivationFunctionType
ALU = mybir.AluOpType

P = 128
PACK = 4
SPAN = P * PACK
SPANS = 2
QUADS = 4
QUAD = P // QUADS
ROWS = 4
SPREAD = QUAD // (ROWS * SPANS)
BANK = 512
CHUNK = BANK // PACK
DOUBLE = 2 * CHUNK
LINE = 16
PER_COLUMN = 16
TABLE_BYTES = 4 * T


def tile_list_malware_pair_family_kernel(
    tc, tab_words, tab_scales, offs, w1, pos1, pos2, g, w4_words, w4_scales, out_0, out_1, out_2
):
    nc = tc.nc
    with ExitStack() as ctx:
        keep = ctx.enter_context(tc.tile_pool(name="keep", bufs=1))
        stage = ctx.enter_context(tc.tile_pool(name="stage", bufs=1))
        psum = ctx.enter_context(tc.psum_pool(name="psum", bufs=1))

        def kept(shape, dtype, name, tag=None):
            return keep.tile(shape, dtype, name=name, tag=tag or name, align_bytes=64)

        def bank(index, shape, name):
            return psum.tile(shape, F32, name=name, tag="bank%d" % index)

        def staged(offset):
            return lambda shape, dtype, name: stage.tile(shape, dtype, name=name, tag=name, offset=offset, align_bytes=64)

        def two_parts(width):
            return slice(0, width // 2), slice(width // 2, width)

        def carry(planes, rows, step, first=0):
            for q in (0, 2, 1, 3):
                nc.sync.dma_start(
                    planes[QUAD * q : QUAD * q + ROWS, :, :].bitcast(I32),
                    rows[QUAD * q + first : QUAD * (q + 1) : step, :].bitcast(I32),
                )

        offs_sb = keep.tile([P, S // PER_COLUMN], U16, name="offs_sb")
        pos1_sb = keep.tile([P, PAIRS // PER_COLUMN], U16, name="pos1_sb")
        pos2_sb = keep.tile([P, PAIRS // PER_COLUMN], U16, name="pos2_sb")

        tab_rows = staged(TABLE_BYTES)([P, T], U8, "tab_rows")
        nc.vector.memset(tab_rows[:].bitcast(I32), 0)
        picked_planes = kept([P, SPANS, S], U8, "picked_planes")
        nc.vector.memset(picked_planes[:].rearrange("p a s -> p (a s)").bitcast(I32), 0)
        w4_planes = kept([P, SPANS * N], U8, "w4_planes")
        nc.vector.memset(w4_planes[:].bitcast(I32), 0)
        w4_rows = kept([P, SPAN], U8, "w4_rows")
        nc.vector.memset(w4_rows[:].bitcast(I32), 0)

        def load_w1(make_tile, b, a, c0, width):
            piece = make_tile([P, PACK, width], F32, "w1_raw%d%d_%d" % (b, a, c0))
            cols = slice(SPAN * b + c0, SPAN * b + c0 + width)
            nc.sync.dma_start(piece[:], w1[SPAN * a : SPAN * (a + 1), cols].rearrange("(p j) c -> p j c", j=PACK))
            return piece[:], c0, width

        table = [staged(0)([P, T], I32, "table0")]
        table_hbm = [tab_words[a].rearrange("p t i -> p (t i)").bitcast(I32) for a in range(SPANS)]
        nc.sync.dma_start(table[0][:, : T // 2], table_hbm[0][:, : T // 2])
        nc.sync.dma_start(offs_sb[:], offs)
        nc.sync.dma_start(pos1_sb[:], pos1)
        nc.sync.dma_start(pos2_sb[:], pos2)
        gain = kept([P, SPANS, PACK], F32, "gain")
        nc.sync.dma_start(gain[:], g.rearrange("(b p t) -> p b t", b=SPANS, t=PACK))
        nc.sync.dma_start(tab_rows[0:P:SPREAD, :].bitcast(I32), tab_scales.rearrange("a q t -> q a t").bitcast(I32))
        nc.sync.dma_start(table[0][:, T // 2 :], table_hbm[0][:, T // 2 :])
        raw = {(0, a): [load_w1(kept, 0, a, 0, SPAN)] for a in range(SPANS)}

        picked_rows = kept([P, S], U8, "picked_rows")
        nc.vector.tensor_copy(picked_rows[:], tab_rows[:].indirect(offs_sb[:]))
        carry(picked_planes[:, 0:1, :], picked_rows[:], SPANS * SPREAD)
        table.append(staged(TABLE_BYTES)([P, T], I32, "table1"))
        nc.sync.dma_start(table[1][:], table_hbm[1])
        carry(picked_planes[:, 1:2, :], picked_rows[:], SPANS * SPREAD, SPREAD)
        picked = [kept([P, S], U32, "picked%d" % a) for a in range(SPANS)]
        nc.vector.tensor_copy(picked[0][:], table[0][:].bitcast(U32).indirect(offs_sb[:]))

        last_half_at = TABLE_BYTES // 2 + 4 * PACK * SPAN // 2
        raw[(1, 0)] = [load_w1(staged(0), 1, 0, 0, SPAN)]
        raw[(1, 1)] = [
            load_w1(staged(offset), 1, 1, c0, SPAN // 2) for c0, offset in ((0, TABLE_BYTES // 2), (SPAN // 2, last_half_at))
        ]

        w1_planes = kept([P, SPANS, SPANS, PACK, P], U8, "w1_planes")
        w1_codes, dealt = {}, {}
        whole, (low, high) = slice(0, PACK), two_parts(PACK)

        def cast_w1(b, a, piece, slices, copy):
            if (b, a) not in dealt:
                if a * b:
                    dealt[(b, a)] = staged(TABLE_BYTES)([P, PACK, P, PACK], BF16, "dealt11")
                else:
                    dealt[(b, a)] = kept([P, PACK, P, PACK], BF16, "dealt%d%d" % (b, a), tag="dealt%d0" % b)
            rows, c0, width = piece
            src = rows.rearrange("p j (m t) -> p m j t", t=PACK)[:, :, :, slices]
            dst = dealt[(b, a)][:, slices, c0 // PACK : (c0 + width) // PACK, :].rearrange("p t m j -> p m j t")
            copy(dst, src)

        def quantise_w1(b, a, slices, make_tile=kept):
            count = slices.stop - slices.start
            codes = make_tile([P, count, P], U32, "w1_codes%d%d%d" % (b, a, slices.start))
            nc.vector.quantize_mx(
                out=codes[:].rearrange("p t m -> p (t m)").bitcast(E4M3),
                scales=w1_planes[:, b, a, slices, :].rearrange("p t m -> p (t m)"),
                in_=dealt[(b, a)][:, slices, :, :].rearrange("p t m j -> p (t m j)"),
            )
            for u in range(count):
                w1_codes[(b, a, slices.start + u)] = codes[:, u, :]

        def first_pass(b, a, group):
            acc, sums = group
            for u, (t, cols) in enumerate(sums):
                width = cols.stop - cols.start
                nc.tensor.matmul_mx(
                    out=acc[:, u * width : (u + 1) * width],
                    lhsT=w1_codes[(b, a, t)].bitcast(E4M3),
                    lhsT_scale=w1_planes[:, b, a, t, :],
                    rhs=picked[a][:, cols].bitcast(E4M3),
                    rhs_scale=picked_planes[:, a, cols],
                    start=(a == 0 and u == 0),
                    stop=(a == SPANS - 1 and u == len(sums) - 1),
                )

        first_half, second_half = two_parts(S)
        quarters = two_parts(BANK)
        contents = [
            [[(t0, cols), (t0 + 1, cols)] for cols, t0 in product(quarters, range(0, PACK, 2))]
            + [[(t, second_half)] for t in range(PACK)],
            [[(t, cols)] for t, cols in product(range(PACK), (first_half, second_half))],
        ]
        groups = [[(bank(u, [P, BANK], "acc%d" % b), sums) for u, sums in enumerate(contents[b])] for b in range(SPANS)]
        cast_w1(0, 0, raw[(0, 0)][0], whole, nc.scalar.copy)
        quantise_w1(0, 0, whole)
        for group in groups[0]:
            first_pass(0, 0, group)
        w4_raw = kept([P, SPANS, 2 * N], U8, "w4_raw", tag="w1_raw00_0")
        nc.sync.dma_start(w4_raw[:].bitcast(I32), w4_words.rearrange("a p c -> p a c").bitcast(I32))
        cast_w1(0, 1, raw[(0, 1)][0], whole, nc.vector.tensor_copy)
        quantise_w1(0, 1, whole)
        for a in range(SPANS):
            nc.sync.dma_start(
                w4_rows[SPREAD // SPANS * a : P : SPREAD, :].bitcast(I32),
                w4_scales[a].rearrange("q (x c) -> (q x) c", c=SPAN).bitcast(I32),
            )
        for cols in quarters + (second_half,):
            nc.vector.tensor_copy(
                picked[1][:, cols],
                table[1][:].bitcast(U32).indirect(offs_sb[:, cols.start // PER_COLUMN : cols.stop // PER_COLUMN]),
            )
        for group in groups[0]:
            first_pass(0, 1, group)

        h = {}
        first_sample = [
            kept([P, PACK, PAIRS], F32, "first_sample%d" % b, tag=tag) for b, tag in enumerate(("dealt10", "w1_raw01_0"))
        ]

        def sigmoids(b):
            for t in range(PACK):
                h[(b, t)] = kept([P, S], F32, "h%d%d" % (b, t))
            for acc, sums in groups[b]:
                for u, (t, cols) in enumerate(sums):
                    width = cols.stop - cols.start
                    nc.scalar.activation(h[(b, t)][:, cols], acc[:, u * width : (u + 1) * width], ACT.Sigmoid)

        def pick_first(b):
            for t in range(PACK):
                nc.vector.tensor_copy(first_sample[b][:, t, :], h[(b, t)][:].indirect(pos1_sb[:]))

        sigmoids(0)
        for slices in (low, high):
            cast_w1(1, 0, raw[(1, 0)][0], slices, nc.vector.tensor_copy)
        first_slice, second_slice = two_parts(PACK // 2)
        quantise_w1(1, 0, first_slice)
        cast_w1(1, 1, raw[(1, 1)][0], whole, nc.vector.tensor_copy)
        for slices in (low, high):
            cast_w1(1, 1, raw[(1, 1)][1], slices, nc.vector.tensor_copy)
        quantise_w1(1, 1, first_slice)
        quantise_w1(1, 0, second_slice, staged(last_half_at))
        quantise_w1(1, 1, second_slice)
        quantise_w1(1, 0, high, staged(last_half_at + 4 * P))
        quantise_w1(1, 1, high)
        for group, a in product(groups[1], range(SPANS)):
            first_pass(1, a, group)
        pick_first(0)

        w4_codes = staged(TABLE_BYTES + SPAN)([P, SPANS, 2 * N], U8, "w4_codes")
        for a in range(SPANS):
            nc.gpsimd.tensor_copy(
                w4_codes[:, a, :].rearrange("p (x t m e) -> p x t m e", x=SPANS, t=PACK, e=2),
                w4_raw[:, a, :].rearrange("p (x m t e) -> p x t m e", x=SPANS, t=PACK, e=2),
            )
        w4_dealt_rows = staged(TABLE_BYTES)([P, SPAN], U8, "w4_dealt_rows")
        nc.gpsimd.tensor_copy(
            w4_dealt_rows[:].rearrange("p (t c i) -> p c t i", t=PACK, i=LINE),
            w4_rows[:].rearrange("p (c i t) -> p c t i", t=PACK, i=LINE),
        )
        carry(w4_planes[:].rearrange("p (x c) -> p x c", c=SPAN), w4_dealt_rows, SPREAD // SPANS)
        inv_gain = kept([P, SPANS, PACK], F32, "inv_gain")
        nc.vector.reciprocal(inv_gain[:], gain[:])
        inv_gain2 = kept([P, SPANS, PACK], F32, "inv_gain2")
        nc.vector.tensor_tensor(inv_gain2[:], inv_gain[:], inv_gain[:], ALU.mult)
        sigmoids(1)
        pick_first(1)

        third, last = 2 * CHUNK, 3 * CHUNK
        units = [(0, 0, DOUBLE), (1, 0, DOUBLE), (0, third, DOUBLE), (1, third, CHUNK), (1, last, CHUNK)]
        inverse, forward, backward, z_codes = {}, {}, {}, {}
        z_planes = kept([P, SPANS, PAIRS], U8, "z_planes")

        def interleaved(view):
            return view.rearrange("p (c i) t -> p c t i", i=LINE // 4)

        def by_lines(view):
            return view.rearrange("p t (c i) -> p c t i", i=LINE // 4)

        def root_first(b):
            roots = kept([P, PACK, PAIRS], F32, "inverse%d" % b, tag="picked%d" % b)
            for n, (span, j0, width) in enumerate(units):
                if span == b:
                    inverse[n] = roots[:, :, j0 : j0 + width]
            parts = two_parts(PAIRS)[::-1] if b == 0 else (slice(0, PAIRS),)
            for cols, t in product(parts, range(PACK)):
                if cols.start == 0 and t == PACK - 1:
                    nc.scalar.activation(inverse[b][:, low, :], inverse[b][:, low, :], ACT.Square)
                nc.scalar.activation(
                    roots[:, t, cols], first_sample[b][:, t, cols], ACT.Abs_reciprocal_sqrt, scale=inv_gain[:, b, t : t + 1]
                )

        def invert_and_pick(n, groups=(whole,)):
            b, j0, width = units[n]
            for slices in groups:
                nc.scalar.activation(inverse[n][:, slices, :], inverse[n][:, slices, :], ACT.Square)
            forward[n] = kept([P, PACK, width], F32, "forward%d" % n, tag=("forward0", "forward1", "w1_raw01_0", "forward0", "forward1")[n])
            cols = slice(j0 // PER_COLUMN, (j0 + width) // PER_COLUMN)
            for t in range(PACK):
                nc.vector.tensor_tensor(forward[n][:, t, :], h[(b, t)][:].indirect(pos2_sb[:, cols]), inverse[n][:, t, :], ALU.mult)

        def root_second(n):
            b, j0, width = units[n]
            backward[n] = kept([P, PACK, width], F32, "backward%d" % n)
            for t in range(PACK):
                nc.scalar.activation(
                    backward[n][:, t, :], forward[n][:, t, :], ACT.Abs_reciprocal_sqrt, scale=inv_gain2[:, b, t : t + 1]
                )

        def second_pass(a, j0):
            for grp, t in product(range(SPANS), range(PACK)):
                c0 = SPAN * grp + P * t
                s0 = SPAN * (SPANS * grp + a) + P * t
                nc.tensor.matmul_mx(
                    out=sums[j0][grp][:, t, :],
                    lhsT=w4_codes[:, a, 2 * c0 : 2 * (c0 + P)].bitcast(E2M1),
                    lhsT_scale=w4_planes[:, s0 : s0 + P],
                    rhs=z_codes[(a, j0)].bitcast(E4M3),
                    rhs_scale=z_planes[:, a, j0 : j0 + CHUNK],
                    start=(a == 0 and t == 0),
                    stop=(a == SPANS - 1 and t == PACK - 1),
                )

        def agree(n):
            b, j0, width = units[n]
            nc.scalar.activation(backward[n][:], backward[n][:], ACT.Square)
            z = kept([P, width, PACK], BF16, "z%d" % n)
            for part in two_parts(width):
                nc.vector.tensor_tensor(
                    interleaved(z[:, part, :]), by_lines(forward[n][:, :, part]), by_lines(backward[n][:, :, part]), ALU.min
                )
            codes = kept([P, width], U32, "z_codes%d" % n)
            for part in two_parts(width):
                nc.vector.quantize_mx(
                    out=codes[:, part].bitcast(E4M3),
                    scales=z_planes[:, b, j0 + part.start : j0 + part.stop],
                    in_=z[:, part, :].rearrange("p j t -> p (j t)"),
                )
            for c0 in range(0, width, CHUNK):
                z_codes[(b, j0 + c0)] = codes[:, c0 : c0 + CHUNK]
                second_pass(b, j0 + c0)

        y_planes = kept([P, SPANS, PAIRS], U8, "y_planes")
        y, rounded = {}, {}

        def hand_out(j0, width, grp, copy=nc.scalar.copy):
            y[(j0, grp)] = kept([P, PACK, width], F32, "y%d_%d" % (j0, grp))
            for c0 in range(0, width, CHUNK):
                copy(y[(j0, grp)][:, :, c0 : c0 + CHUNK], sums[j0 + c0][grp][:])
            nc.sync.dma_start(
                out_0[SPAN * grp : SPAN * (grp + 1), j0 : j0 + width].rearrange("(p t) j -> p t j", t=PACK), y[(j0, grp)][:]
            )

        def round_y(j0, width, grp, part, from_bank):
            if (j0, grp) not in rounded:
                rounded[(j0, grp)] = kept([P, width, PACK], BF16, "rounded%d_%d" % (j0, grp))
            dst = interleaved(rounded[(j0, grp)][:, part, :])
            if from_bank:
                nc.scalar.copy(dst, by_lines(sums[j0 + part.start][grp][:]))
            else:
                nc.vector.tensor_copy(dst, by_lines(y[(j0, grp)][:, :, part]))

        def requantise(j0, width, grp, parts, calls=None):
            for part, from_bank in parts:
                round_y(j0, width, grp, part, from_bank)
            base = j0 % DOUBLE
            for part in calls or [part for part, from_bank in parts]:
                nc.vector.quantize_mx(
                    out=y_codes[j0 - base][:, grp, base + part.start : base + part.stop].bitcast(E4M3),
                    scales=y_planes[:, grp, j0 + part.start : j0 + part.stop],
                    in_=rounded[(j0, grp)][:, part, :].rearrange("p j t -> p (j t)"),
                )

        def store_codes(j0, queue):
            queue.dma_start(out_1[:, :, j0 : j0 + DOUBLE, :].rearrange("g p m i -> p g (m i)").bitcast(I32), y_codes[j0][:])

        sums = {
            j0: [bank(SPANS * (j0 // CHUNK) + grp, [P, PACK, CHUNK], "sums") for grp in range(SPANS)]
            for j0 in range(0, PAIRS, CHUNK)
        }
        y_codes = {j0: kept([P, SPANS, DOUBLE], I32, "y_codes%d" % j0) for j0 in range(0, PAIRS, DOUBLE)}

        for n in range(SPANS):
            root_first(n)
            if n == 0:
                for slices in (low, high):
                    nc.gpsimd.tensor_tensor(inverse[2][:, slices, :], inverse[2][:, slices, :], inverse[2][:, slices, :], ALU.mult)
            invert_and_pick(n, (high,))
        for n in range(SPANS):
            root_second(n)
            if n == 0:
                invert_and_pick(2, ())
            agree(n)
            invert_and_pick(n + 3)
        for step in (root_second, agree):
            for n in (2, 3):
                step(n)
        hand_out(0, DOUBLE, 0)
        root_second(4)
        hand_out(0, DOUBLE, 1)
        agree(4)
        first_chunk, second_chunk = two_parts(DOUBLE)
        on_scalar = [(slice(0, CHUNK), True)]
        on_vector = [(part, False) for part in two_parts(CHUNK)]
        requantise(0, DOUBLE, 0, [(first_chunk, False), (second_chunk, False)])
        requantise(0, DOUBLE, 1, [(first_chunk, False), (second_chunk, True)], [slice(0, DOUBLE)])
        store_codes(0, nc.sync)
        for grp in range(SPANS):
            hand_out(third, CHUNK, grp)
        for grp in range(SPANS):
            round_y(third, CHUNK, grp, slice(0, CHUNK), False)
        for grp in range(SPANS):
            requantise(third, CHUNK, grp, [], [slice(0, CHUNK)])
        hand_out(last, CHUNK, 0)
        hand_out(last, CHUNK, 1, nc.vector.tensor_copy)
        requantise(last, CHUNK, 0, on_scalar)
        requantise(last, CHUNK, 1, on_vector)
        store_codes(DOUBLE, nc.scalar)
        for q in range(QUADS):
            queue = nc.scalar if q % 2 else nc.sync
            queue.dma_start(
                out_2[:, ROWS * q : ROWS * (q + 1), :].rearrange("g r m -> r g m").bitcast(I32),
                y_planes[QUAD * q : QUAD * q + ROWS, :, :].bitcast(I32),
            )
